import numpy as np, ml_dtypes
CORES = [35,38,43,46]
N = 4
BF = ml_dtypes.bfloat16
W, R, Q, RO, HOP, E = 4096, 256, 12, 6, 1, 512
def parts(rng):
    v = rng.integers(0, 256, (N, 8, 16, W)); v[..., 1::8] = v[..., 0::8]
    s = 0.15 + 0.85 * rng.random((N, 8, 16, 1)); w = rng.choice(np.array([0.0, 0.1, 0.2]), (N, 8, 1, 1))
    k = np.minimum((W * s * ((1 - w) * rng.random((N, 8, 16, W)) + w * rng.random((N, 8, 1, W))) ** 2).astype(np.int64), W - 1)
    pop = np.argsort(rng.random((8, E)), axis=1)[:, :24] * 8; pop = np.concatenate([pop, pop + 1], axis=1)
    hit = np.take_along_axis(np.broadcast_to(pop, (N, 8, 48)), rng.integers(0, 48, (N, 8, 16 * R)), 2).reshape(N, 8, 16, R)
    p = np.where(rng.random((N, 8, 16, R)) < 0.3, hit, rng.integers(0, W, (N, 8, 16, R)))
    return v, k, p
def look(rng, v, p):
    o = np.take_along_axis(p, rng.integers(0, 16, (N, 8, 1, R)), 2); y = np.take_along_axis(v, o, 3)
    near = np.clip(y + rng.integers(-3, 4, y.shape) * (rng.random(y.shape) < 0.5), 0, 255)
    return np.where(rng.random((N, 8, 1, R)) < 0.75, near, rng.integers(0, 256, y.shape))
def pack(v, k, p, y):
    return {"val": np.ascontiguousarray(v.reshape(N, 128, W)).astype(np.float32).astype(BF), "clk": np.ascontiguousarray(k.reshape(N, 128, W)).astype(np.int32),
            "nam": np.ascontiguousarray(p.reshape(N, 128, R)).astype(np.int32), "seen": np.ascontiguousarray(y.reshape(N, 128, R)).astype(np.float32).astype(BF)}
def setup_inputs(rng):
    v, k, p = parts(rng)
    return pack(v, k, p, look(rng, v, p))
def setup_inputs_count(rng):
    v, k, p = parts(rng); A = W // 4; q = rng.permutation(N)
    v[q[:2]] = rng.integers(0, 256, (2, 8, 16, W)); z = rng.random((N, 8, W))
    for g in (1, 3, 5, 7):
        s = int(rng.integers(0, W - R + 1)); z[q[0], g, s:s + R] -= 1
    b = rng.integers(W // 4, W // 2, (N, 8, 16, 1)); m = np.argsort(z, axis=2); pos = np.argsort(m, axis=2)[:, :, None, :]
    n = np.where(pos < A, 16, np.where(pos < 3 * A, Q - 1, Q)); at = np.argsort(rng.random((N, 8, 16, W)), axis=2) < n
    up = (pos >= A) * rng.choice(np.array([0, 0, 1, 5]), (N, 8, 16, W))
    k = np.where(at, b + up, b - rng.integers(1, W // 8, (N, 8, 16, W)))
    def pick(lo, hi, c): return np.take_along_axis(m, rng.integers(lo, hi, (N, 8, c * R)), 2).reshape(N, 8, c, R)
    o = pick(0, A, 1); o[q[0]] = m[q[0], :, None, :R]; i = np.arange(16)[None, None, :, None]
    k0 = rng.integers(0, 16, (N, 8, 1, R)); k1 = (k0 + rng.integers(1, 16, (N, 8, 1, R))) & 15; k2 = (k0 + rng.integers(1, 16, (N, 8, 1, R))) & 15
    h = rng.integers(0, 3, (N, 8, 1, R)); h[q[0]] = 0; h[q[1]] = rng.integers(1, 3, (8, 1, R))
    p = np.where(i == k0, o, np.where(((i == k1) & (h > 0)) | ((i == k2) & (h > 1)), pick(3 * A, W, 16), pick(A, 3 * A, 16)))
    return pack(v, k, p, np.take_along_axis(v, o, 3))
def setup_inputs_crowd(rng):
    v, k, p = parts(rng); c = np.argsort(rng.random((N, 8, W)), axis=2)[..., :3]; top = np.max(k, axis=3)
    np.put_along_axis(k, np.ascontiguousarray(np.broadcast_to(c[:, :, None, :], (N, 8, 16, 3))), np.stack([top - (top >> 3), top - (top >> 4), top], axis=3), 3)
    r = np.arange(R)[None, None, None, :]; g = np.arange(8)[None, :, None, None]; i = np.arange(16)[None, None, :, None]
    star = np.where((g % 2 == 0) & (r % 2 == 1), c[:, :, None, 1:2], c[:, :, None, 0:1])
    k0 = rng.integers(0, 16, (N, 8, 1, R)); no = (r < 2) | (rng.random((N, 8, 1, R)) < 0.125)
    p = np.where(i == k0, star, np.where((i == ((k0 + 5) & 15)) & no, c[:, :, None, 2:3], p))
    return pack(v, k, p, np.take_along_axis(v, star, 3))
def setup_inputs_ends(rng):
    v, k, p = parts(rng); y = look(rng, v, p)
    p[:, 0] = p[:, 0, :1]
    p[:, 1] = rng.choice(np.array([0, 1, W - 2, W - 1]), (N, 16, R))
    k[:, 2] = (W - 1) * rng.integers(0, 2, (N, 16, W))
    v[:, 3] = 255 * (rng.random((N, 16, W)) < 0.1); y[:, 3] = 255 * (rng.random((N, 16, R)) < 0.9)
    v[:, 3, :, W // 2:] = 0; y[:, 3, :, ::2] = 255
    p[:, 4] = rng.integers(1, W - 1, (N, 16, R)); p[:, 4, 0] = 0; p[:, 4, 15] = W - 1; k[:, 4, :, 0] = 0; k[:, 4, :, W - 1] = 1; y[:, 4] = v[:, 4, :, W - 1:]
    p[:, 5, 0] = 0; k[:, 5, :, 0] = W - 1; y[:, 5] = v[:, 5, :, :1]
    v[:, 6] = 1 * (rng.random((N, 16, W)) < 0.1); y[:, 6] = 255
    h = W - R
    own = np.argsort(rng.random((N, R)), axis=1); rest = np.argsort(rng.random((N, max(h, 15 * R))), axis=1)[:, :15 * R] % h
    p7 = np.concatenate([h + own[:, None, :], rest.reshape(N, 15, R)], axis=1)
    p[:, 7] = np.take_along_axis(p7, np.argsort(rng.random((N, 16, R)), axis=1), 1)
    lead = np.argsort(rng.random((N, 16)), axis=1)[:, :, None] <= 16 - Q
    k[:, 7] = (np.where(lead, h // 2, h) * rng.random((N, 16, W)) ** 4).astype(np.int64)
    k[:, 7, :, h:] = np.where(lead, rng.integers(h // 2, h, (N, 16, R)), rng.integers(0, 9, (N, 16, R)))
    sv = rng.integers(0, 256, (16, R)); v[:, 7, :, h:] = sv; y[:, 7] = sv[:, own].transpose(1, 0, 2)
    return pack(v, k, p, y)
def setup_inputs_ties(rng):
    v, k, p = parts(rng); g = np.arange(8)[None, :, None, None]
    v = rng.integers(0, 2, (N, 8, 16, W)) + 2 * rng.integers(0, 2, (N, 8, 16, W)) * (g % 2); y = rng.integers(0, 4, (N, 8, 16, R))
    k[:, :4] = rng.integers(0, 12, (N, 4, 16, W)); p[:, 3:5] = rng.integers(0, 24, (N, 2, 16, R)) * (W // 32) + 5
    return pack(v, k, p, y)
def setup_inputs_spread(rng):
    lw = np.log2(float(W)); g = np.arange(8)[None, :, None, None]
    c = np.exp2(8 * rng.random((N, 8, 1, W))) * (rng.random((N, 8, 1, W)) > 0.0625)
    v = np.minimum((c * rng.random((N, 8, 16, W))).astype(np.int64), 255)
    z = np.where(g < 4, rng.random((N, 8, 1, W)), rng.random((N, 8, 16, 1)))
    k = np.minimum((np.exp2(lw * z) * rng.random((N, 8, 16, W))).astype(np.int64), W - 1)
    p = np.minimum(np.exp2(lw * rng.random((N, 8, 16, R))).astype(np.int64), W - 1)
    return pack(v, k, p, look(rng, v, p))
def check_inputs(d):
    bad = []
    for k in ("clk", "nam"):
        if np.min(d[k]) < 0 or np.max(d[k]) > W - 1: bad.append("range of " + k)
    for k in ("val", "seen"):
        a = d[k].astype(np.float32)
        if not np.all((a == np.floor(a)) & (a >= 0) & (a <= 255)): bad.append("whole numbers of " + k)
    return bad
def reference(val, clk, nam, seen):
    v = val.astype(np.float32).astype(np.int32).reshape(N, 8, 16, W); y = seen.astype(np.float32).astype(np.int32).reshape(N, 8, 16, R)
    kn = np.array(clk, dtype=np.int32).reshape(N, 8, 16, W); p = np.array(nam, dtype=np.int32).reshape(N, 8, 16, R)
    row = np.arange(16)[None, :, None]
    for t in range(RO):
        for a in range(N):
            b = (a + HOP * t) % N
            pa = p[a]; ix = pa.reshape(8, 1, 16 * R)
            vg = np.take_along_axis(v[b], ix, 2).reshape(8, 16, 16, R)
            kg = np.take_along_axis(kn[b], ix, 2).reshape(8, 16, 16, R)
            d = np.add.reduce(np.abs(vg - y[a][:, :, None, :]), axis=1)
            ks = np.argmin(d, axis=1)
            o = np.take_along_axis(pa, ks[:, None, :], 1)
            ko = np.take_along_axis(kg, ks[:, None, None, :], 2)
            over = (np.add.reduce((kg >= ko).astype(np.int32), axis=1) >= Q) & (pa != o)
            free = ~np.any(over, axis=1); k1 = np.argmax(over, axis=1)
            j = np.maximum.reduce(kg, axis=2)
            p1 = np.take_along_axis(pa, k1[:, None, :], 1); kf = np.take_along_axis(kg, k1[:, None, None, :], 2)[:, :, 0, :]
            back = np.where(row == ks[:, None, :], kf, np.where(row == ((ks + 1) & 15)[:, None, :], p1, pa))
            p[a] = np.where(free[:, None, :], np.maximum(pa, j), back)
            for g in range(8):
                rr = np.flatnonzero(free[g]); names, first = np.unique(o[g, 0, rr], return_index=True)
                kn[b, g][:, names] = j[g][:, rr[first]]
    return {"yp": p.reshape(N, 128, R).astype(np.float32), "yk": np.add.reduce(kn.reshape(N, 128, 8, E), axis=2).astype(np.float32)}

@@ -1,0 +1,502 @@
+from concourse.bass import DstId, RemoteDMATransfer
+from concourse.mybir import AluOpType as A, ActivationFunctionType as F
+
+N, W, R, RO, E = 4, 4096, 256, 6, 512
+C = 128
+BIG = 8192.0
+OFF = 32768.0
+SEN = 40959.0
+M = 12582912.0
+CFG = {'tgv': [(0, 0), (0, 2), (1, 3)], 'vgv': [(0, 1), (0, 4)], 'win': 60.0, 'pri': {
+    'vg0a': -5.9, 'pd0a': -2.0, 'ab0a': 0.2, 'tg0a': 2.3, 'js0a': 0.8, 'vg1a': -0.7, 'pd1a': 23.1, 'ab1a': -3.9, 'tg1a': -2.8,
+    'js1a': -0.6, 'vg2a': -3.1, 'pd2a': 15.1, 'ab2a': 1.5, 'tg2a': 4.4, 'js2a': 0.5, 'vg3a': -8.2, 'pd3a': -11.7, 'ab3a': 0.6,
+    'tg3a': -0.1, 'js3a': -8.4, 'dk0a': 7.2, 'dk1a': -11.7, 'ksa': 0.5, 'k1a': 3.4, 'k2a': 1.4, 'kua': -4.7, 'tma': -5.6,
+    'toa': 1.3, 'tha': -12.0, 'cba': 0.8, 'fra': -7.4, 'o6a': -8.3, 'ppa': -4.9, 'eqa': -49.2, 'eta': -7.4, 'z1a': 2.4,
+    'ooa': -8.2, 'nra': 0.5, 'oaa': 3.8, 'zpa': 23.4, 'u0a': 2.9, 'uua': 1.5, 'usa': -12.0, 'jua': -5.9, 'xfa': -0.7,
+    'yya': 3.2, 'kfa': -3.9, 'pna': -0.4, 'jaa': -3.0, 'jba': 2.5, 'jia': -13.2, 'paa': -10.2, 'aaa': -0.1, 'zza': 0.7,
+    'baa': -2.3, 'mma': -0.4, 'nfa': -1.8, 'nua': 0.3, 'senda': 9.0, 'oba': 0.5, 'eea': -19.4, 'loa': 2.2, 'sua': -3.9,
+    'vg0b': 4.1, 'pd0b': -5.3, 'ab0b': -1.7, 'tg0b': 2.4, 'js0b': -4.1, 'vg1b': -4.1, 'pd1b': -4.9, 'ab1b': 3.8, 'tg1b': 7.3,
+    'js1b': 4.8, 'vg2b': 4.0, 'pd2b': 20.1, 'ab2b': 2.7, 'tg2b': 14.1, 'js2b': 4.2, 'vg3b': 4.5, 'pd3b': 13.4, 'ab3b': 2.8,
+    'tg3b': 6.7, 'js3b': 5.7, 'dk0b': 8.1, 'dk1b': 0.5, 'ksb': 7.2, 'k1b': -0.8, 'k2b': 6.1, 'kub': -0.6, 'tmb': 2.9,
+    'tob': 5.0, 'thb': 0.1, 'cbb': 4.0, 'frb': 4.0, 'o6b': 2.1, 'ppb': 0.7, 'eqb': -2.8, 'etb': 0.3, 'z1b': -5.1, 'oob': 7.6,
+    'nrb': 2.6, 'oab': -0.8, 'zpb': 2.0, 'u0b': -4.1, 'uub': 7.4, 'usb': 6.0, 'jub': -19.1, 'xfb': 4.1, 'yyb': 4.6,
+    'kfb': -3.3, 'pnb': 1.9, 'jab': -8.9, 'jbb': -1.6, 'jib': -0.4, 'pab': 5.3, 'aab': 7.8, 'zzb': -1.8, 'bab': 5.4,
+    'mmb': -9.7, 'nfb': 4.8, 'nub': 8.9, 'sendb': 21.5, 'obb': 3.4, 'eeb': 1.6, 'lob': -2.9, 'sub': 3.7, 'sca': 3.8, 'scb': 4.5}}
+
+S, P = "sbuf", "psum"
+SCRATCH = {
+    "vt": (S, [128, W], "bfloat16"), "ck": (S, [128, W], "int32"), "tt": (S, [128, W + 16], "float32"),
+    "nm": (S, [128, R], "int32"), "ys": (S, [128, 4 * R], "bfloat16"), "yx": (S, [128, 4 * W], "bfloat16"),
+    "lf": (S, [128, 7 * R], "float16"), "lu": (S, [128, 6 * R], "uint16"),
+    "nf": (S, [128, 6 * R], "float16"), "nu": (S, [128, 6 * R], "uint16"),
+    "iq": (S, [128, 512], "float32"), "pi": (S, [128, 8], "int32"), "col": (S, [128, 16], "float32"),
+    "eye": (S, [128, 128], "bfloat16"), "neye": (S, [128, 128], "bfloat16"), "beye": (S, [128, 128], "bfloat16"),
+    "eye4": (S, [128, 128], "float32"),
+    "bsh": (S, [128, 128], "bfloat16"), "bis": (S, [128, 128], "bfloat16"), "low": (S, [128, 128], "bfloat16"),
+    "t1": (S, [128, 128], "bfloat16"), "t2": (S, [128, 128], "bfloat16"), "ones": (S, [128, 128], "bfloat16"),
+    "cz": (S, [128, 384], "bfloat16"), "wb": (S, [128, 144], "bfloat16"), "wc": (S, [128, 144], "bfloat16"),
+    "wt": (S, [128, 2048], "bfloat16"),
+    "h0": (S, [128, 160], "bfloat16"), "h1": (S, [128, 160], "bfloat16"), "tri": (S, [128, 16], "float32"),
+    "j0": (S, [128, 136], "float32"), "jj": (S, [128, 136], "float32"), "j1": (S, [128, 128], "float32"),
+    "jc": (S, [128, 128], "float16"), "sd": (S, [128, 128], "float32"), "sj": (S, [128, 512], "float32"),
+    "bi": (S, [128, 8], "int32"), "bl": (S, [128, 8], "uint16"), "f0": (S, [128, 512], "float32"),
+    "rk": (S, [128, W], "float16"), "ok": (S, [128, E], "float32"), "op": (S, [128, R], "float32"),
+}
+for _c in "ab":
+    SCRATCH.update({
+        "vg" + _c: (S, [128, 2048], "bfloat16"), "ab" + _c: (S, [128, 8, 16, 16], "bfloat16"),
+        "tg" + _c: (S, [128, 2056], "float32"), "cb" + _c: (S, [128, 8, 16, 17], "bfloat16"),
+        "js" + _c: (S, [128, 2048], "float32"), "ks" + _c: (S, [128, 128], "float32"),
+        "k1" + _c: (S, [128, 8], "int32"), "k2" + _c: (S, [128, 8], "int32"), "ku" + _c: (S, [128, 8], "uint16"),
+        "to" + _c: (S, [128, C], "float32"), "tm" + _c: (S, [128, C], "float32"), "fr" + _c: (S, [128, C], "float32"),
+        "o6" + _c: (S, [128, C], "float16"),
+        "eq" + _c: (S, [128, C], "bfloat16"), "et" + _c: (S, [128, C], "bfloat16"), "nr" + _c: (S, [128, C], "bfloat16"),
+        "us" + _c: (S, [128, 136], "float32"), "ju" + _c: (S, [128, 8], "uint16"),
+        "oa" + _c: (S, [128, 8], "float32"), "ob" + _c: (S, [128, 8], "float32"), "ee" + _c: (S, [128, C], "bfloat16"),
+        "su" + _c: (S, [128, 16], "uint16"), "xf" + _c: (S, [128, C], "int32"), "kp" + _c: (S, [128, 2 * C], "int32"),
+        "ja" + _c: (S, [128, C], "float32"), "jb" + _c: (S, [128, C], "float32"), "ji" + _c: (S, [128, C], "float32"),
+        "yy" + _c: (S, [128, C], "float32"), "aa" + _c: (S, [128, C], "float32"), "ba" + _c: (S, [128, C], "float32"),
+        "mm" + _c: (S, [128, C], "float32"),
+    })
+for _b in range(8):
+    SCRATCH["ps%d" % _b] = (P, [128, 512], "float32")
+
+SEMAPHORES = (["cv", "cs", "ct", "cg", "sent", "l_nm", "l_ys", "l_v0", "l_v1", "st0", "st1", "st2", "y1", "y2", "y3"]
+              + ["l_k%d" % b for b in range(4)] + ["ar%d%s" % (t, c) for t in range(1, 7) for c in "ab"])
+
+EST = {"cy": 0.83, "g": 1.55, "sc": 3.8, "lat": 90.0, "fix": 25.0, "pe": 0.42, "hop": 2800.0}
+
+
+def vt_(n):
+    return EST["fix"] + max(64.0, n) * EST["cy"]
+
+
+def ga_(n):
+    return 55.0 + n * EST["g"] * EST["cy"]
+
+
+def pe_(*ns):
+    return sum(10.0 + max(64, n) * EST["pe"] for n in ns)
+
+
+def bits(engines):
+    m = 0
+    for e in engines:
+        m |= 1 << e
+    return m
+
+
+def build(g, core, T, topo):
+    rank = T.rank_of(core)
+    cores = T.cores
+    ops = []
+    ph = [-1.0]
+    V, Sc, Pe = g.vector, g.scalar, g.tensor
+
+    def op(q, dur, rd, wr, fn, banks=(), sig=None, fin=0.0, name=None):
+        ops.append({"q": q, "dur": dur, "rd": list(rd), "wr": list(wr), "fn": fn, "banks": tuple(banks), "sig": sig, "fin": fin,
+                    "name": name or wr[0], "pre": ph[0] < 0, "ph": ph[0]})
+
+    def v(dur, rd, wr, fn, banks=(), name=None):
+        op("v", dur, rd, wr, fn, banks, name=name)
+
+    def dma(q, out, in_, rd, wr, sem, fin):
+        e = g.sync if q == "y" else g.scalar
+        op(q, 60.0, rd, wr, lambda: e.dma_start(out, in_).then_inc(T.sem[sem], 16), sig=(sem, 16), fin=fin)
+
+    sent = [0]
+
+    dma("y", T.ys[:, 0:R], T.seen[:], [], ["ys0"], "l_ys", 2000.0)
+    dma("y", T.nm[:], T.nam[:], [], ["nm"], "l_nm", 2200.0)
+    dma("s", T.vt[:, 0:W // 2], T.val[:, 0:W // 2], [], ["vt0"], "l_v0", 3500.0)
+    dma("s", T.vt[:, W // 2:], T.val[:, W // 2:], [], ["vt1"], "l_v1", 5000.0)
+    for b in range(4):
+        dma("y", T.ck[:, b * 1024:(b + 1) * 1024], T.clk[:, b * 1024:(b + 1) * 1024], [], ["ck%d" % b], "l_k%d" % b, 6500.0 + 1500.0 * b)
+        ops[-1]["late"] = True
+
+    def common(src):
+        en = None
+        for d in cores:
+            if d != src:
+                e = topo.engines(src, d)
+                en = e if en is None else [x for x in en if x in e]
+        return en
+
+    def send_y():
+        en = common(core)
+        k = len(en) // 4
+        tr = []
+        for j in range(1, N):
+            d = cores[(rank + j) % N]
+            assert topo.may_write(core, d)
+            rid, pid, _ = topo.addr(d)
+            tr.append(RemoteDMATransfer(dst_ids=[DstId(rid=rid, pnc=pid)], dma_engine_mask=bits(en[(j - 1) * k:j * k]),
+                                        remote_sem=T.sem["y%d" % j], src=T.ys[:, 0:R], dst=T.ys[:, j * R:(j + 1) * R]))
+        g.remote_dma_fused(tr, local_sem=T.sem.sent)
+        sent[0] += k * (N - 1)
+    op("g", 1500.0, ["ys0"], ["ys1", "ys2", "ys3"], send_y,
+       sig={"ys%d" % j: ("y%d" % j, len(common(cores[(rank - j) % N])) // 4) for j in range(1, N)}, fin=5000.0)
+
+    flag = {"allow_small_or_imprecise_dtypes": True}
+    op("g", 1000.0, [], ["iq"], lambda: g.iota(T.iq[:], [[1, 512]], 0, 0, **flag))
+    op("g", 150.0, [], ["pi0"], lambda: g.iota(T.pi[:, 0:2], [[1, 2]], 0, 1))
+    op("g", 150.0, [], ["bi"], lambda: g.iota(T.bi[:], [[1, 8]], 0, 0))
+    op("g", 360.0, [], ["j0"], lambda: g.iota(T.j0[:], [[256, 8], [1, 17]], int(OFF), 0, **flag))
+    op("g", 350.0, [], ["j1"], lambda: g.iota(T.j1[:], [[256, 8], [1, 16]], 0, 0, **flag))
+    t0 = vt_(1)
+    col = lambda i: T.col[:, i:i + 1]
+    v(t0, ["pi0"], ["pi2"], lambda: V.tensor_scalar(T.pi[:, 2:4], T.pi[:, 0:2], 15, None, A.bitwise_and))
+    v(t0, ["pi0"], ["pi4"], lambda: V.tensor_scalar(T.pi[:, 4:5], T.pi[:, 0:1], 112, None, A.bitwise_and))
+    v(t0, ["pi0"], ["pi5"], lambda: V.tensor_scalar(T.pi[:, 5:6], T.pi[:, 0:1], 16, None, A.bitwise_and))
+    v(t0, ["pi0"], ["c0"], lambda: V.tensor_copy(col(0), T.pi[:, 0:1]))
+    v(t0, ["pi2"], ["c1"], lambda: V.tensor_copy(col(1), T.pi[:, 2:3]))
+    v(t0, ["pi2", "pi4"], ["c2"], lambda: V.tensor_tensor(col(2), T.pi[:, 3:4], T.pi[:, 4:5], A.add))
+    v(t0, ["pi4"], ["c3"], lambda: V.tensor_scalar(col(3), T.pi[:, 4:5], 15.0, None, A.add))
+    v(t0, ["pi0"], ["c4"], lambda: V.tensor_scalar(col(4), T.pi[:, 0:1], 16.0, None, A.add))
+    v(t0, ["pi5"], ["c5"], lambda: V.tensor_scalar(col(5), T.pi[:, 5:6], 4096.0, None, A.mult))
+    v(t0, ["pi5"], ["c6"], lambda: V.tensor_scalar(col(6), T.pi[:, 5:6], -4096.0, 65536.0, A.mult, A.add))
+    v(t0, ["pi2"], ["c7"], lambda: V.tensor_scalar(col(7), T.pi[:, 2:3], 16.0, None, A.mult))
+    v(t0, ["pi2"], ["c8"], lambda: V.tensor_scalar(col(8), T.pi[:, 2:3], float(W), None, A.add))
+    q128 = T.iq[:, 0:128]
+    t1 = vt_(128)
+    ts = t1 + 30
+    v(t1, ["iq", "c0"], ["eye"], lambda: V.tensor_scalar(T.eye[:], q128, col(0), None, A.is_equal))
+    v(t1, ["iq", "c0"], ["eye4"], lambda: V.tensor_scalar(T.eye4[:], q128, col(0), None, A.is_equal))
+    v(t1, ["iq", "c0"], ["neye"], lambda: V.tensor_scalar(T.neye[:], q128, col(0), -1.0, A.is_equal, A.mult))
+    v(t1, ["iq", "c0"], ["beye"], lambda: V.tensor_scalar(T.beye[:], q128, col(0), BIG / 2, A.is_equal, A.mult))
+    v(t1, ["iq", "c2"], ["bsh"], lambda: V.tensor_scalar(T.bsh[:], q128, col(2), BIG / 2, A.is_equal, A.mult))
+    v(vt_(256), ["beye", "bsh"], ["bis"], lambda: V.tensor_tensor(T.bis[:], T.beye[:], T.bsh[:], A.add))
+    v(t1, ["iq", "c0"], ["t1"], lambda: V.tensor_scalar(T.t1[:], q128, col(0), -1.0, A.is_gt, A.mult))
+    v(t1, ["iq", "c3"], ["t2"], lambda: V.tensor_scalar(T.t2[:], q128, col(3), None, A.is_le))
+    v(vt_(256), ["t1", "t2"], ["t1"], lambda: V.tensor_tensor(T.t1[:], T.t1[:], T.t2[:], A.mult))
+    v(vt_(256), ["t1", "eye"], ["low"], lambda: V.tensor_tensor(T.low[:], T.t1[:], T.eye[:], A.add))
+    v(t0, [], ["ones"], lambda: V.memset(T.ones[:], 1.0))
+    v(t0, [], ["cz0"], lambda: V.memset(T.cz[:, 0:128], BIG / 256))
+    v(t0, [], ["cz1"], lambda: V.memset(T.cz[:, 128:256], BIG / 256 + 16.0))
+    v(t0, [], ["cz2"], lambda: V.memset(T.cz[:, 256:384], -BIG / 128))
+    v(vt_(144), ["iq", "c3"], ["wb"], lambda: V.tensor_scalar(T.wb[:], T.iq[:, 0:144], col(3), 4096.0, A.is_equal, A.mult))
+    v(vt_(144), ["iq", "c3"], ["wc"], lambda: V.tensor_scalar(T.wc[:], T.iq[:, 0:144], col(3), 8192.0, A.is_equal, A.mult))
+    wn = lambda nl: T.wb[:, 15 - nl:143 - nl]
+    wm = lambda nl: T.wc[:, 15 - nl:143 - nl]
+    v(vt_(160), ["iq", "c4", "c6"], ["h0"], lambda: V.tensor_scalar(T.h0[:], T.iq[:, 0:160], col(4), col(6), A.is_equal, A.mult))
+    v(vt_(160), ["iq", "c4", "c5"], ["h1"], lambda: V.tensor_scalar(T.h1[:], T.iq[:, 0:160], col(4), col(5), A.is_equal, A.mult))
+    v(t0, ["iq", "c1"], ["tri"], lambda: V.tensor_scalar(T.tri[:], T.iq[:, 0:16], col(1), None, A.is_gt))
+    for nl in range(1, 16):
+        v(t0, ["wc", "tri"], ["wt%d" % nl], lambda nl=nl: V.tensor_scalar(T.wt[:, nl * 128:(nl + 1) * 128], wm(nl), T.tri[:, nl:nl + 1], None, A.mult))
+    v(vt_(136), ["j0", "c7"], ["jj"], lambda: V.tensor_scalar(T.jj[:], T.j0[:], col(7), None, A.add))
+    v(t0, [], ["jj"], lambda: V.memset(T.jj[:, 16::17], SEN))
+    v(t1, ["j1", "c7"], ["jc"], lambda: V.tensor_scalar(T.jc[:], T.j1[:], col(7), None, A.add))
+    v(t1, [], ["sd"], lambda: V.memset(T.sd[:], 0.0))
+    v(t0, [], ["sd"], lambda: V.memset(T.sd[:, 0::16], 1e9))
+    v(vt_(512), [], ["sj"], lambda: V.memset(T.sj[:], 0.0))
+    v(t0, [], ["sj"], lambda: V.memset(T.sj[:, 0::16], -1e9))
+    v(t0, ["bi"], ["bl"], lambda: V.tensor_copy(T.bl[:], T.bi[:]))
+    v(t0, [], ["ttx"], lambda: V.memset(T.tt[:, W:W + 16], 0.0))
+    for c in "ab":
+        v(t0, [], ["tgx" + c], lambda c=c: V.memset(T["tg" + c][:, 2048:2056], -4096.0))
+        v(t0, [], ["cbx" + c], lambda c=c: V.memset(T["cb" + c][:, :, :, 16], 0.0))
+        v(t0, [], ["su" + c], lambda c=c: V.memset(T["su" + c][:], 0))
+    v(vt_(256), ["nm"], ["lu0a", "lu0b"], lambda: V.tensor_copy(T.lu[:, 0:R], T.nm[:]))
+    v(vt_(256), ["nm"], ["lf0a", "lf0b"], lambda: V.tensor_scalar(T.lf[:, 0:R], T.nm[:], -2048.0, None, A.add))
+    for k in range(16):
+        v(vt_(128), ["ys0"], ["yx0_%d" % k], lambda k=k: V.tensor_copy(T.yx[:, k:W:16], T.ys[:, 0:R]))
+    for j in range(1, N):
+        for k in range(16):
+            op("g", 600.0, ["ys%d" % j], ["yx%d_%d" % (j, k)],
+               lambda j=j, k=k: g.affine_select(T.yx[:, j * W + k:(j + 1) * W:16], T.ys[:, j * R:(j + 1) * R], [[0, R]], A.is_gt, 0.0, 1, 0))
+    v(vt_(512), ["iq"], ["f0"], lambda: V.tensor_scalar(T.f0[:], T.iq[:], 1.0 / 4096, 0.5 / 4096, A.mult, A.add))
+    for b in range(8):
+        bk = 2 + b % 5
+        ps = T["ps%d" % bk]
+        op("s", vt_(512) + 30, ["f0"], ["ps%d" % bk], lambda b=b, ps=ps: Sc.activation(ps[:], T.f0[:], F.Identity, bias=b / 8.0 - 2048.0), [bk])
+        v(vt_(512), ["ps%d" % bk, "ck%d" % (b // 2)], ["tt"] if b == 0 else ["tt%d" % b],
+          lambda b=b, ps=ps: V.tensor_tensor(T.tt[:, b * 512:(b + 1) * 512], T.ck[:, b * 512:(b + 1) * 512], ps[:], A.add), [bk])
+    TT = ["tt", "ttx"] + ["tt%d" % b for b in range(1, 8)]
+    dbank = [0]
+
+    def half(t, h):
+        c = "ab"[h]
+        B = lambda n: T[n + c]
+        n0 = t * R + (1 - h) * C
+        pu, pf = "lu%d%s" % (t, c), "lf%d%s" % (t, c)
+        PF = T.lf[:, n0:n0 + C]
+        b1, b2 = 2 + h, 4 + h
+        p1, p2, p6 = T["ps%d" % b1], T["ps%d" % b2], T.ps6
+        f1, f2, f6 = ([["ps%d" % b] for b in (b1, b2, 6)] if t == 0 else ([], [], []))
+        dk, uu, oo, lo, z1 = p1[:, 0:128], p1[:, 128:264], p1[:, 264:272], p1[:, 272:280], p1[:, 384:512]
+        th, pp = p6[:, h * 128:h * 128 + 128], p2[:, 384:512]
+        k_ = lambda n: n + c
+        j = t % N
+        yxs = ["yx%d_%d" % (j, k) for k in range(16)]
+        for s in range(4):
+            cs = slice(s * 512, (s + 1) * 512)
+            off = T.lu[:, n0 + s * 32:n0 + (s + 1) * 32]
+            y0 = j * W + (1 - h) * 2048 + s * 512
+            if (h, s) in CFG["vgv"]:
+                v(ga_(512), [pu, "vt0", "vt1"] + yxs, [k_("vg%d" % s)],
+                  lambda cs=cs, off=off, y0=y0: V.tensor_tensor(B("vg")[:, cs], T.vt[:, 0:W].indirect(off), T.yx[:, y0:y0 + 512], A.subtract))
+                op("s", vt_(512) + 30, [k_("vg%d" % s)], [k_("ab%d" % s)],
+                   lambda s=s, cs=cs: Sc.activation(B("ab")[:, 2 * s:2 * s + 2], B("vg")[:, cs], F.Abs))
+            else:
+                op("s", ga_(512) + 10, [pu, "vt0", "vt1"], [k_("vg%d" % s)],
+                   lambda cs=cs, off=off: Sc.activation(B("vg")[:, cs], T.vt[:, 0:W].indirect(off), F.Copy))
+                bk = (0, 1, 7)[dbank[0] % 3]
+                dbank[0] += 1
+                pd = T["ps%d" % bk]
+                op("t", pe_(512, 512), [k_("vg%d" % s), "eye", "neye"] + yxs, ["pd%d" % bk],
+                   lambda cs=cs, pd=pd, y0=y0: [Pe.matmul(pd[:], T.eye[:], B("vg")[:, cs], True, False),
+                                                Pe.matmul(pd[:], T.neye[:], T.yx[:, y0:y0 + 512], False, True)], [bk], name=k_("pd%d" % s))
+                op("s", vt_(512) + 30, ["pd%d" % bk], [k_("ab%d" % s)],
+                   lambda s=s, pd=pd: Sc.activation(B("ab")[:, 2 * s:2 * s + 2], pd[:], F.Abs), [bk])
+            if (h, s) in CFG["tgv"]:
+                v(ga_(512), [pu] + TT, [k_("tg%d" % s)], lambda cs=cs, off=off: V.tensor_copy(B("tg")[:, cs], T.tt[:, 0:W].indirect(off)))
+            else:
+                op("s", ga_(512) + 10, [pu] + TT, [k_("tg%d" % s)],
+                   lambda cs=cs, off=off: Sc.activation(B("tg")[:, cs], T.tt[:, 0:W].indirect(off), F.Copy))
+            v(vt_(512), [k_("tg%d" % s), "sj"], [k_("js%d" % s)],
+              lambda cs=cs: V.tensor_tensor_scan(B("js")[:, cs], T.sj[:], B("tg")[:, cs], 0.0, A.add, A.max))
+        tgs = [k_("tg%d" % s) for s in range(4)]
+        for x in range(2):
+            op("t", pe_(*[64] * 17), [k_("ab%d" % s) for s in (2 * x, 2 * x + 1)] + ["wb", "eye", "jc"], [k_("dk%d" % x)] + f1,
+               lambda x=x: [Pe.matmul(p1[:, 64 * x:64 * x + 64], T.eye[:], T.jc[:, 64 * x:64 * x + 64], True, False)] +
+                           [Pe.matmul(p1[:, 64 * x:64 * x + 64], wn(nl), B("ab")[:, 4 * x:4 * x + 4, nl, :], False, nl == 15) for nl in range(16)], [b1])
+        v(vt_(128), [k_("dk0"), k_("dk1"), "sd"], [k_("ks")], lambda: V.tensor_tensor_scan(B("ks")[:], T.sd[:], dk, 0.0, A.add, A.min), [b1])
+        v(t0, [k_("ks")], [k_("k1")], lambda: V.tensor_copy(B("k1")[:], B("ks")[:, 15::16]))
+        v(t0, [k_("k1")], [k_("k2")], lambda: V.tensor_scalar(B("k2")[:], B("k1")[:], 4095, None, A.bitwise_and))
+        v(t0, [k_("k2")], [k_("ku")], lambda: V.tensor_copy(B("ku")[:], B("k2")[:]))
+        tw = lambda: B("tg")[:, 0:2048].indirect(B("ku")[:])
+        if (h, 4) in CFG["tgv"]:
+            v(ga_(C), [k_("ku")] + tgs, [k_("tm")], lambda: V.tensor_scalar(B("tm")[:], tw(), -0.5, None, A.add))
+        else:
+            op("s", ga_(C) + 10, [k_("ku")] + tgs, [k_("tm")], lambda: Sc.activation(B("tm")[:], tw(), F.Identity, bias=-0.5))
+        if (h, 4) in CFG["vgv"]:
+            v(ga_(C), [k_("ku")] + tgs, [k_("to")], lambda: V.tensor_copy(B("to")[:], tw()))
+        else:
+            op("s", ga_(C) + 10, [k_("ku")] + tgs, [k_("to")], lambda: Sc.activation(B("to")[:], tw(), F.Copy))
+        v(t1, [k_("tm")], [k_("th")] + f6, lambda: V.tensor_scalar(th, B("tm")[:], M, -M, A.add, A.add), [6])
+        for k in range(16):
+            v(t1, tgs + [k_("th")], [k_("cb%d" % k)],
+              lambda k=k: V.tensor_tensor(B("cb")[:, :, :, k], B("tg")[:, k:2048:16], th, A.is_lt), [6], name=k_("cb"))
+        v(t1, [k_("to"), k_("th")], [k_("fr")], lambda: V.tensor_tensor(B("fr")[:], B("to")[:], th, A.subtract), [6])
+        v(t1, [k_("fr")], [k_("o6")], lambda: V.tensor_scalar(B("o6")[:], B("fr")[:], 4096.0, -2048.5, A.mult, A.add))
+        op("t", pe_(128), [pf, "eye"], [k_("pp")] + f2, lambda: Pe.matmul(pp, T.eye[:], PF, True, True), [b2])
+        v(t1, [k_("pp"), k_("o6")], [k_("eq")], lambda: V.tensor_tensor(B("eq")[:], B("o6")[:], pp, A.is_equal), [b2])
+        v(t0, [k_("eq")], [k_("et")], lambda: V.transpose(B("et")[:], B("eq")[:]))
+        op("t", pe_(128), [k_("eq"), "low"], [k_("z1")], lambda: Pe.matmul(z1, T.low[:], B("eq")[:], True, True), [b1])
+        op("t", pe_(*[8] * 16), [k_("o6"), "wb"], [k_("oo")],
+           lambda: [Pe.matmul(oo, wn(nl), B("o6")[:, nl::16], nl == 0, nl == 15) for nl in range(16)], [b1])
+        op("s", ts, [k_("z1")], [k_("nr")], lambda: Sc.activation(B("nr")[:], z1, F.Sign, bias=0.5, scale=-1.0), [b1])
+        op("s", t0 + 30, [k_("oo")], [k_("oa")], lambda: Sc.activation(B("oa")[:], oo, F.Identity, bias=SEN, scale=1.0 / 65536), [b1])
+        op("t", pe_(384, 128, 128, 128, 128), [k_("nr"), pf, "ones", "cz0", "cz1", "cz2", "beye", "bsh", "bis", "eye"], [k_("zz"), k_("p0")],
+           lambda: [Pe.matmul(p2[:, 0:384], T.ones[:], T.cz[:], True, False),
+                    Pe.matmul(p2[:, 0:128], T.beye[:], B("nr")[:], False, False),
+                    Pe.matmul(p2[:, 128:256], T.bsh[:], B("nr")[:], False, False),
+                    Pe.matmul(p2[:, 256:384], T.bis[:], B("nr")[:], False, False),
+                    Pe.matmul(p2[:, 256:384], T.eye[:], PF, False, True)], [b2], name=k_("zp"))
+
+        def same():
+            r = [Pe.matmul(uu, T.wt[:, 0:128], T.wc[:, 0:136], True, False)]
+            for m in range(4):
+                for b in range(2):
+                    for a in range(2):
+                        hb = T.h0 if b == 0 else T.h1
+                        x = 16 + 16 * (b - a)
+                        u0 = 128 + (2 * m + b) * 17
+                        r.append(Pe.matmul(p1[:, u0:u0 + 16], hb[:, x:x + 128], B("et")[:, m * 32 + a * 16:m * 32 + a * 16 + 16], False, False))
+            return r
+        op("t", pe_(*([136] + [16] * 16)), [k_("et"), k_("z1"), k_("oo"), "h0", "h1", "wc", "wt0"], [k_("uu")], same, [b1], name=k_("u0"))
+        op("t", pe_(*[136] * 16), [k_("cb%d" % k) for k in range(16)] + [k_("cbx"), "wc"], [k_("uu")],
+           lambda: [Pe.matmul(uu, wm(nl), B("cb")[:, :, nl, :], False, nl == 15) for nl in range(16)], [b1])
+        v(vt_(136), [k_("uu"), "jj"], [k_("us")],
+          lambda: V.tensor_tensor_scan(B("us")[:, ::-1], p1[:, 263:127:-1], T.jj[:, ::-1], 0.0, A.min, A.max), [b1])
+        v(t0, [k_("us")], [k_("ju")], lambda: V.tensor_scalar(B("ju")[:], B("us")[:, 0::17], -OFF, 2048.0, A.add, A.min))
+        fw = lambda: B("tg")[:, 0:2056].indirect(B("ju")[:])
+        v(ga_(C), [k_("ju"), k_("tgx")] + tgs, [k_("xf")], lambda: V.tensor_scalar(B("xf")[:], fw(), 4096.0, -0.5, A.mult, A.add))
+        op("s", ga_(C) + 10, [k_("ju"), k_("tgx")] + tgs, [k_("yy")], lambda: Sc.activation(B("yy")[:], fw(), F.Identity, bias=-12288.0, scale=-4.0))
+        v(t1, [k_("xf")], [k_("kf")], lambda: V.tensor_scalar(B("kp")[:, 0:C], B("xf")[:], 12, None, A.arith_shift_right))
+        v(t1, [k_("xf")], [k_("pn")], lambda: V.tensor_scalar(B("kp")[:, C:2 * C], B("xf")[:], 4095, None, A.bitwise_and))
+        op("s", ts, [k_("js%d" % s) for s in range(4)], [k_("ja")], lambda: Sc.activation(B("ja")[:], B("js")[:, 15::16], F.Identity, bias=-0.5))
+        op("s", ts, [k_("ja")], [k_("jb")], lambda: Sc.activation(B("jb")[:], B("ja")[:], F.Identity, bias=M))
+        op("s", ts, [k_("jb")], [k_("ji")], lambda: Sc.activation(B("ji")[:], B("jb")[:], F.Identity, bias=-M))
+        v(t1, [k_("ji"), k_("pp")], [k_("pp")], lambda: V.tensor_tensor(pp, B("ji")[:], pp, A.max), [b2], name=k_("pa"))
+        v(t1, [k_("yy"), k_("pp")], [k_("aa")], lambda: V.tensor_tensor(B("aa")[:], B("yy")[:], pp, A.min), [b2])
+        v(vt_(256), [k_("kf"), k_("pn"), k_("zz")], [k_("zz")], lambda: V.tensor_tensor(p2[:, 0:256], B("kp")[:], p2[:, 0:256], A.subtract), [b2])
+        v(t1, [k_("aa"), k_("p0")], [k_("ba")], lambda: V.tensor_tensor(B("ba")[:], B("aa")[:], p2[:, 256:384], A.max), [b2])
+        v(t1, [k_("ba"), k_("zz")], [k_("mm")], lambda: V.tensor_tensor(B("mm")[:], B("ba")[:], p2[:, 0:128], A.max), [b2])
+        NF, NU = T.nf[:, n0:n0 + C], T.nu[:, n0:n0 + C]
+        v(t1, [k_("mm"), k_("zz")], [k_("nf%d" % t)], lambda: V.tensor_tensor(NF, B("mm")[:], p2[:, 128:256], A.max), [b2], name=k_("nf"))
+        last = t == RO - 1
+        if not last:
+            v(t0, [k_("nf%d" % t)], [k_("nu%d" % t)], lambda: V.tensor_scalar(NU, NF, 2048.0, None, A.add), name=k_("nu"))
+        hop = 1 if not last else -t
+        dst, src = cores[(rank + hop) % N], cores[(rank - hop) % N]
+        sem = "ar%d%s" % (t + 1, c)
+        k = len(common(core))
+
+        def send():
+            assert topo.may_write(core, dst)
+            rid, pid, _ = topo.addr(dst)
+            en = common(core)
+            ea, eb = en[:k // 2], en[k // 2:]
+            d = [DstId(rid=rid, pnc=pid)]
+            x = n0 + R
+            if last:
+                tr = [RemoteDMATransfer(dst_ids=d, dma_engine_mask=bits(en), remote_sem=T.sem[sem], src=NF, dst=T.lf[:, x:x + C])]
+            else:
+                tr = [RemoteDMATransfer(dst_ids=d, dma_engine_mask=bits(ea), remote_sem=T.sem[sem], src=NU, dst=T.lu[:, x:x + C]),
+                      RemoteDMATransfer(dst_ids=d, dma_engine_mask=bits(eb), remote_sem=T.sem[sem], src=NF, dst=T.lf[:, x:x + C])]
+            g.remote_dma_fused(tr, local_sem=T.sem.sent)
+            sent[0] += k
+        op("g", 300.0, [k_("nf%d" % t)] + ([] if last else [k_("nu%d" % t)]), ["lf%d%s" % (t + 1, c), "lu%d%s" % (t + 1, c)], send,
+           sig=(sem, len(common(src))), fin=EST["hop"], name=k_("send"))
+
+        v(t0, [k_("us"), k_("oa")], [k_("ob")], lambda: V.tensor_tensor(B("ob")[:], B("oa")[:], B("us")[:, 0::17], A.subtract))
+        v(ga_(C), [k_("ob"), k_("o6"), "bl"], [k_("ee")],
+          lambda: V.tensor_tensor(B("ee")[:], B("ob")[:, 0:8].indirect(T.bl[:]), B("o6")[:], A.is_equal))
+        op("t", pe_(*([256] + [8] * 15)), [k_("ee"), k_("ob"), "eye4"] + ["wt%d" % nl for nl in range(1, 16)], [k_("lo")],
+           lambda: [Pe.matmul(lo, T.eye4[:], B("ob")[:], True, False)] +
+                   [Pe.matmul(lo, T.wt[:, nl * 128:(nl + 1) * 128], B("ee")[:, nl::16], False, nl == 15) for nl in range(1, 16)], [b1])
+        v(t0, [k_("lo"), "c8"], [k_("su")], lambda: V.tensor_scalar(B("su")[:, 0::2], lo, 2048.0, col(8), A.add, A.min), [b1])
+
+    v(t0, [], ["wt0"], lambda: V.memset(T.wt[:, 0:128], 0.0))
+    for t in range(RO):
+        ph[0] = 20.0 * t
+        half(t, 0)
+        half(t, 1)
+        for c in "ab":
+            for nh in range(7, -1, -1):
+                x = slice(nh * 16, nh * 16 + 16)
+                v(55.0 + 16 * EST["sc"] * EST["cy"], ["su" + c, "ji" + c, "fr" + c], TT,
+                  lambda c=c, nh=nh, x=x: V.tensor_tensor(T.tt[:, 0:W + 16].indirect(T["su" + c][:, 2 * nh:2 * nh + 1]),
+                                                          T["ji" + c][:, x], T["fr" + c][:, x], A.add), name="sc" + c)
+
+    ph[0] = 20.0 * RO
+    for b in range(6):
+        v(vt_(512), TT, ["rk%d" % b], lambda b=b: V.tensor_scalar(T.rk[:, b * 512:(b + 1) * 512], T.tt[:, b * 512:(b + 1) * 512], M, -M, A.add, A.add))
+    for b in range(2):
+        x, y = slice(b * 512, (b + 1) * 512), slice((b + 2) * 512, (b + 3) * 512)
+        op("s", vt_(512) + 30, TT, ["js%da" % b], lambda b=b, x=x: Sc.activation(T.jsa[:, x], T.tt[:, (b + 6) * 512:(b + 7) * 512], F.Identity, bias=M), name="ra")
+        op("s", vt_(512) + 30, ["js%da" % b], ["js%da" % (b + 2)], lambda x=x, y=y: Sc.activation(T.jsa[:, y], T.jsa[:, x], F.Identity, bias=-M), name="rb")
+    steps = [(0, T.eye, T.rk[:, 0:512]), (1, T.eye, T.rk[:, 512:1024]), (6, T.eye4, T.jsa[:, 1024:1536]), (2, T.eye, T.rk[:, 1024:1536]),
+             (3, T.eye, T.rk[:, 1536:2048]), (7, T.eye4, T.jsa[:, 1536:2048]), (4, T.eye, T.rk[:, 2048:2560]), (5, T.eye, T.rk[:, 2560:3072])]
+    for i, (b, e, x) in enumerate(steps):
+        op("t", pe_(512 if b < 6 else 2048), ["rk%d" % b if b < 6 else "js%da" % (b - 4), "eye", "eye4"], ["pd0"],
+           lambda i=i, e=e, x=x: Pe.matmul(T.ps0[:], e[:], x, i == 0, i == 7), [0], name="fold")
+        ops[-1]["acc"] = i > 0
+    op("s", vt_(512), ["pd0"], ["ok"], lambda: Sc.activation(T.ok[:], T.ps0[:], F.Identity, bias=8 * 2048.0 - 4.0), [0])
+    dma("s", T.yk[:], T.ok[:], ["ok"], ["yk"], "st0", 2500.0)
+    for h in range(2):
+        c = "ba"[h]
+        x = RO * R + h * C
+        v(t1, ["lf6" + c], ["op" + c], lambda h=h, x=x: V.tensor_scalar(T.op[:, h * C:(h + 1) * C], T.lf[:, x:x + C], 2048.0, None, A.add))
+        dma("y", T.yp[:, h * C:(h + 1) * C], T.op[:, h * C:(h + 1) * C], ["op" + c], ["yp" + c], "st%d" % (1 + h), 2500.0)
+    return ops, sent
+
+
+def order(ops):
+    n = len(ops)
+    LAT = EST["lat"]
+    lw, rs = {}, {}
+    for i, o in enumerate(ops):
+        d = {}
+        for k in o["rd"]:
+            if k in lw:
+                d.setdefault(lw[k], set()).add(k)
+        for k in o["wr"]:
+            if k in lw:
+                d.setdefault(lw[k], set()).add(k)
+            for r in rs.get(k, ()):
+                if r != i:
+                    d.setdefault(r, set()).add(k)
+        for k in o["rd"]:
+            rs.setdefault(k, []).append(i)
+        for k in o["wr"]:
+            lw[k] = i
+            rs[k] = []
+        o["dep"] = d
+    succ = [[] for _ in range(n)]
+    for i, o in enumerate(ops):
+        for j in o["dep"]:
+            succ[j].append(i)
+    pr = [0.0] * n
+    key = [o["ph"] for o in ops]
+    for i in range(n - 1, -1, -1):
+        o = ops[i]
+        pr[i] = max(o["dur"], o["fin"]) + max([pr[s] + LAT for s in succ[i]] + [0.0])
+        if succ[i]:
+            key[i] = CFG["pri"].get(o["name"], 0.0) - pr[i] / 1000
+        if o.get("late"):
+            key[i] = 500.0 + i
+    left = [len(o["dep"]) for o in ops]
+    ready = [i for i in range(n) if left[i] == 0]
+    qf, end, bank, out = {}, [0.0] * n, {}, []
+    while ready:
+        est = {}
+        for i in ready:
+            o = ops[i]
+            s = qf.get(o["q"], 0.0)
+            for j in o["dep"]:
+                s = max(s, end[j] + LAT)
+            for b in o["banks"]:
+                for q, j in bank.get(b, {}).items():
+                    if q != o["q"]:
+                        s = max(s, end[j] + LAT)
+            est[i] = s
+        i0 = min(ready, key=lambda i: est[i])
+        cand = [i for i in ready if ops[i]["q"] == ops[i0]["q"] and est[i] <= est[i0] + CFG["win"]]
+        i = max(cand, key=lambda i: (-key[i], pr[i], -i))
+        o = ops[i]
+        for b in o["banks"]:
+            for q, j in bank.setdefault(b, {}).items():
+                if q != o["q"]:
+                    o["dep"].setdefault(j, set())
+            bank[b][o["q"]] = i
+        o["start"] = est[i]
+        qf[o["q"]] = est[i] + o["dur"]
+        end[i] = est[i] + max(o["dur"], o["fin"])
+        out.append(i)
+        ready.remove(i)
+        for s in succ[i]:
+            left[s] -= 1
+            if left[s] == 0:
+                ready.append(s)
+    return out, max(end)
+
+
+def rank_program(g, core, T, topo):
+    if T.rank_of(core) is None:
+        return
+    ops, sent = build(g, core, T, topo)
+    seq, _ = order(ops)
+    Q = {"v": g.vector, "s": g.scalar, "t": g.tensor, "g": g, "y": g.sync}
+    cnt = {"v": 0, "s": 0, "t": 0, "g": 0}
+    seen = {q: {} for q in Q}
+    done = {}
+    final = {}
+    for i in seq:
+        o = ops[i]
+        q = o["q"]
+        need = {}
+        for j, toks in o["dep"].items():
+            if q == "t" and ops[j]["q"] == "t" and (o.get("acc") or o["name"][:2] == "uu") and toks <= {"pd0", "uua", "uub"}:
+                continue
+            sg = done[j]
+            for s, val in ([sg[k] for k in toks if k in sg] if isinstance(sg, dict) else [sg]):
+                need[s] = max(need.get(s, 0), val)
+        for s, val in need.items():
+            if seen[q].get(s, 0) < val:
+                Q[q].wait_ge(T.sem[s], val)
+                seen[q][s] = val
+        r = o["fn"]()
+        if o["sig"] is None:
+            for ins in (r if isinstance(r, list) else [r]):
+                ins.then_inc(T.sem["c" + q], 1)
+                cnt[q] += 1
+            done[i] = ("c" + q, cnt[q])
+        else:
+            done[i] = o["sig"]
+        for s, val in (done[i].values() if isinstance(done[i], dict) else [done[i]]):
+            final[s] = val
+    final["sent"] = sent[0]
+    for s, val in final.items():
+        g.wait_ge(T.sem[s], val)

@@ -3,76 +3,69 @@ from concourse.mybir import AluOpType as A, ActivationFunctionType as F
 
 N, W, R, RO, E = 4, 4096, 256, 6, 512
 C = 128
-BIG = 8192.0
-OFF = 32768.0
-SEN = 40959.0
-M = 12582912.0
-CFG = {'tgv': [(0, 0), (0, 2), (1, 3)], 'vgv': [(0, 1), (0, 4)], 'win': 60.0, 'pri': {
-    'vg0a': -5.9, 'pd0a': -2.0, 'ab0a': 0.2, 'tg0a': 2.3, 'js0a': 0.8, 'vg1a': -0.7, 'pd1a': 23.1, 'ab1a': -3.9, 'tg1a': -2.8,
-    'js1a': -0.6, 'vg2a': -3.1, 'pd2a': 15.1, 'ab2a': 1.5, 'tg2a': 4.4, 'js2a': 0.5, 'vg3a': -8.2, 'pd3a': -11.7, 'ab3a': 0.6,
-    'tg3a': -0.1, 'js3a': -8.4, 'dk0a': 7.2, 'dk1a': -11.7, 'ksa': 0.5, 'k1a': 3.4, 'k2a': 1.4, 'kua': -4.7, 'tma': -5.6,
-    'toa': 1.3, 'tha': -12.0, 'cba': 0.8, 'fra': -7.4, 'o6a': -8.3, 'ppa': -4.9, 'eqa': -49.2, 'eta': -7.4, 'z1a': 2.4,
-    'ooa': -8.2, 'nra': 0.5, 'oaa': 3.8, 'zpa': 23.4, 'u0a': 2.9, 'uua': 1.5, 'usa': -12.0, 'jua': -5.9, 'xfa': -0.7,
-    'yya': 3.2, 'kfa': -3.9, 'pna': -0.4, 'jaa': -3.0, 'jba': 2.5, 'jia': -13.2, 'paa': -10.2, 'aaa': -0.1, 'zza': 0.7,
-    'baa': -2.3, 'mma': -0.4, 'nfa': -1.8, 'nua': 0.3, 'senda': 9.0, 'oba': 0.5, 'eea': -19.4, 'loa': 2.2, 'sua': -3.9,
-    'vg0b': 4.1, 'pd0b': -5.3, 'ab0b': -1.7, 'tg0b': 2.4, 'js0b': -4.1, 'vg1b': -4.1, 'pd1b': -4.9, 'ab1b': 3.8, 'tg1b': 7.3,
-    'js1b': 4.8, 'vg2b': 4.0, 'pd2b': 20.1, 'ab2b': 2.7, 'tg2b': 14.1, 'js2b': 4.2, 'vg3b': 4.5, 'pd3b': 13.4, 'ab3b': 2.8,
-    'tg3b': 6.7, 'js3b': 5.7, 'dk0b': 8.1, 'dk1b': 0.5, 'ksb': 7.2, 'k1b': -0.8, 'k2b': 6.1, 'kub': -0.6, 'tmb': 2.9,
-    'tob': 5.0, 'thb': 0.1, 'cbb': 4.0, 'frb': 4.0, 'o6b': 2.1, 'ppb': 0.7, 'eqb': -2.8, 'etb': 0.3, 'z1b': -5.1, 'oob': 7.6,
-    'nrb': 2.6, 'oab': -0.8, 'zpb': 2.0, 'u0b': -4.1, 'uub': 7.4, 'usb': 6.0, 'jub': -19.1, 'xfb': 4.1, 'yyb': 4.6,
-    'kfb': -3.3, 'pnb': 1.9, 'jab': -8.9, 'jbb': -1.6, 'jib': -0.4, 'pab': 5.3, 'aab': 7.8, 'zzb': -1.8, 'bab': 5.4,
-    'mmb': -9.7, 'nfb': 4.8, 'nub': 8.9, 'sendb': 21.5, 'obb': 3.4, 'eeb': 1.6, 'lob': -2.9, 'sub': 3.7, 'sca': 3.8, 'scb': 4.5}}
+K0 = 2 * R
+B = 8192.0
+M16 = 201326592.0
+WO = 2064.0
+CFG = {
+    "vp": {"a": "3333", "b": "1111"},
+    "vp0": {"a": "1133", "b": "1133"},
+    "kg": {"a": "ss", "b": "ss"},
+    "kg0": {"a": "sv", "b": "sv"},
+    "cp": {"a": "2222", "b": "2112"},
+    "eng": {"ou": "s", "off": "s", "pf": "s", "ko": "s"},
+    "whole": False,
+    "tt16": True, "waw": True, "win": 60.0, "pri": {},
+}
 
+CFG.update({'vp': {'a': '3322', 'b': '2323'}, 'vp0': {'a': '2233', 'b': '2223'}, 'kg': {'a': 'sv', 'b': 'ss'}, 'kg0': {'a': 'sv', 'b': 'ss'}, 'cp': {'a': '1111', 'b': '1121'}, 'eng': {'ou': 's', 'off': 's', 'pf': 'v', 'ko': 's'}, 'whole': False, 'tt16': True, 'waw': True, 'win': 60.0, 'pri': {'vga': 2.0, 'oba': 8.0, 'penb': -1.5, 'offa': 21.0, 'scb': 4.0, 'cbb': 9.5, 'eea': 16.5, 'vab': -19.5, 'ktb': -8.0, 'obb': 14.5, 'eqa': 10.5, 'vaa': -9.5, 'nua': -20.0, 'kob': 1.0, 'aca': -4.5, 'exa': 15.0, 'ova': -19.5, 'sendb': -10.5, 'ybb': -5.5, 'xfa': 28.5, 'ola': -1.0, 'eeb': 6.5, 'x2a': 14.5, 'ofra': -3.0, 'kpb': 19.5, 'jsa': -13.0, 'cba': -1.0, 'eqb': 6.0, 'sub': 17.5, 'acb': 40.0, 'ofrb': 6.0, 'orb': 10.0, 'zza': -2.0, 'ppb': -9.0, 'pdb': -11.5, 'poa': -4.0, 'exb': -11.5, 'ksb': 23.5, 'koa': 21.0, 'pfa': -2.0, 'oub': 9.5, 'jub': -2.5, 'm1b': 6.0, 'sua': 5.0, 'm1a': -1.0, 'ovb': -31.5, 'kta': 6.0, 'pxa': 1.5, 'xfb': 27.0, 'kub': 13.0, 'uua': 3.5, 'jsb': -19.5, 'ppa': -11.5, 'senda': 16.5, 'lob': -29.0, 'kpa': 12.0, 'pfb': -6.0, 'kgb': -1.0, 'kua': -0.5, 'ksa': 4.0, 'x2b': -5.0, 'jua': -7.0, 'pob': -2.5, 'ofb': -22.5, 'pxb': 5.5, 'offb': -1.5, 'dka': 11.5, 'pena': -2.0, 'olb': 11.5, 'nub': 4.5, 'dfb': 7.5, 'zzb': 13.0, 'aba': 2.5, 'ora': 6.0, 'uub': -2.5, 'abb': 3.0, 'yba': 3.0, 'b0b': 10.0, 'dkb': 2.5, 'vgb': 2.0, 'b0a': -1.0, 'loa': -1.5, 'obpb': 1.0, 'kga': 2.0, 'oua': 1.0, 'obpa': -2.5}})
 S, P = "sbuf", "psum"
 SCRATCH = {
-    "vt": (S, [128, W], "bfloat16"), "ck": (S, [128, W], "int32"), "tt": (S, [128, W + 16], "float32"),
+    "vt": (S, [128, W], "bfloat16"), "ck": (S, [128, K0 + W + 16], "int32"),
     "nm": (S, [128, R], "int32"), "ys": (S, [128, 4 * R], "bfloat16"), "yx": (S, [128, 4 * W], "bfloat16"),
-    "lf": (S, [128, 7 * R], "float16"), "lu": (S, [128, 6 * R], "uint16"),
-    "nf": (S, [128, 6 * R], "float16"), "nu": (S, [128, 6 * R], "uint16"),
-    "iq": (S, [128, 512], "float32"), "pi": (S, [128, 8], "int32"), "col": (S, [128, 16], "float32"),
-    "eye": (S, [128, 128], "bfloat16"), "neye": (S, [128, 128], "bfloat16"), "beye": (S, [128, 128], "bfloat16"),
-    "eye4": (S, [128, 128], "float32"),
-    "bsh": (S, [128, 128], "bfloat16"), "bis": (S, [128, 128], "bfloat16"), "low": (S, [128, 128], "bfloat16"),
-    "t1": (S, [128, 128], "bfloat16"), "t2": (S, [128, 128], "bfloat16"), "ones": (S, [128, 128], "bfloat16"),
-    "cz": (S, [128, 384], "bfloat16"), "wb": (S, [128, 144], "bfloat16"), "wc": (S, [128, 144], "bfloat16"),
-    "wt": (S, [128, 2048], "bfloat16"),
-    "h0": (S, [128, 160], "bfloat16"), "h1": (S, [128, 160], "bfloat16"), "tri": (S, [128, 16], "float32"),
-    "j0": (S, [128, 136], "float32"), "jj": (S, [128, 136], "float32"), "j1": (S, [128, 128], "float32"),
-    "jc": (S, [128, 128], "float16"), "sd": (S, [128, 128], "float32"), "sj": (S, [128, 512], "float32"),
-    "bi": (S, [128, 8], "int32"), "bl": (S, [128, 8], "uint16"), "f0": (S, [128, 512], "float32"),
-    "rk": (S, [128, W], "float16"), "ok": (S, [128, E], "float32"), "op": (S, [128, R], "float32"),
+    "lu": (S, [128, RO * R], "uint16"), "nu": (S, [128, RO * R], "uint16"), "nf": (S, [128, R], "float32"), "op": (S, [128, R], "float32"),
+    "iq": (S, [128, R], "float32"), "qm": (S, [128, R], "float32"), "qg": (S, [128, 128], "float32"),
+    "pi": (S, [128, 8], "int32"), "col": (S, [128, 16], "float32"),
+    "kc": (S, [128, 64], "bfloat16"), "sd": (S, [128, 128], "float32"), "sj": (S, [128, 1024], "bfloat16"),
+    "e1": (S, [128, 32], "bfloat16"), "pe": (S, [128, 32], "bfloat16"), "ncn": (S, [128, R], "float16"), "ncr": (S, [128, 16], "float16"),
+    "tri": (S, [128, R], "bfloat16"),
+    "pf": (S, [128, R], "float16"), "ks": (S, [128, R], "float32"), "kt": (S, [128, 16], "float32"), "kw": (S, [128, 16], "float32"),
+    "ku": (S, [128, 16], "uint16"), "ou": (S, [128, 16], "uint16"), "of": (S, [128, 16], "float16"), "ob": (S, [128, 16], "float16"),
+    "off": (S, [128, 16], "uint16"), "su": (S, [128, 32], "uint16"),
+    "po": (S, [128, R], "float16"), "pen": (S, [128, R], "bfloat16"), "ko": (S, [128, R], "float16"), "eq": (S, [128, R], "bfloat16"),
+    "ov": (S, [128, R], "bfloat16"), "va": (S, [128, R], "float16"), "xf": (S, [128, R], "float32"), "m1": (S, [128, R], "float32"),
+    "ac": (S, [128, R], "float16"), "ju": (S, [128, R], "float32"), "ee": (S, [128, R], "bfloat16"),
+    "rk": (S, [128, W], "float16"), "ok": (S, [128, E], "float32"),
 }
+for _n in ("eye", "neye", "n15", "blk", "nblk", "ish", "nsh", "t1", "t2", "tm", "czr", "k1", "k2"):
+    SCRATCH[_n] = (S, [128, 128], "bfloat16")
+for _n in ("w1", "w2", "w16", "wo"):
+    SCRATCH[_n] = (S, [128, 144], "bfloat16")
 for _c in "ab":
     SCRATCH.update({
-        "vg" + _c: (S, [128, 2048], "bfloat16"), "ab" + _c: (S, [128, 8, 16, 16], "bfloat16"),
-        "tg" + _c: (S, [128, 2056], "float32"), "cb" + _c: (S, [128, 8, 16, 17], "bfloat16"),
-        "js" + _c: (S, [128, 2048], "float32"), "ks" + _c: (S, [128, 128], "float32"),
-        "k1" + _c: (S, [128, 8], "int32"), "k2" + _c: (S, [128, 8], "int32"), "ku" + _c: (S, [128, 8], "uint16"),
-        "to" + _c: (S, [128, C], "float32"), "tm" + _c: (S, [128, C], "float32"), "fr" + _c: (S, [128, C], "float32"),
-        "o6" + _c: (S, [128, C], "float16"),
-        "eq" + _c: (S, [128, C], "bfloat16"), "et" + _c: (S, [128, C], "bfloat16"), "nr" + _c: (S, [128, C], "bfloat16"),
-        "us" + _c: (S, [128, 136], "float32"), "ju" + _c: (S, [128, 8], "uint16"),
-        "oa" + _c: (S, [128, 8], "float32"), "ob" + _c: (S, [128, 8], "float32"), "ee" + _c: (S, [128, C], "bfloat16"),
-        "su" + _c: (S, [128, 16], "uint16"), "xf" + _c: (S, [128, C], "int32"), "kp" + _c: (S, [128, 2 * C], "int32"),
-        "ja" + _c: (S, [128, C], "float32"), "jb" + _c: (S, [128, C], "float32"), "ji" + _c: (S, [128, C], "float32"),
-        "yy" + _c: (S, [128, C], "float32"), "aa" + _c: (S, [128, C], "float32"), "ba" + _c: (S, [128, C], "float32"),
-        "mm" + _c: (S, [128, C], "float32"),
+        "vx" + _c: (S, [128, 8, 16, 16], "bfloat16"), "vq" + _c: (S, [128, 2048], "bfloat16"), "ab" + _c: (S, [128, 8, 16, 16], "bfloat16"),
+        "kg" + _c: (S, [128, 2048], "float16"), "js" + _c: (S, [128, 2048], "float16"), "cb" + _c: (S, [128, 2048], "bfloat16"),
+        "bc" + _c: (S, [128, 1], "float32"),
     })
 for _b in range(8):
     SCRATCH["ps%d" % _b] = (P, [128, 512], "float32")
 
-SEMAPHORES = (["cv", "cs", "ct", "cg", "sent", "l_nm", "l_ys", "l_v0", "l_v1", "st0", "st1", "st2", "y1", "y2", "y3"]
-              + ["l_k%d" % b for b in range(4)] + ["ar%d%s" % (t, c) for t in range(1, 7) for c in "ab"])
+SEMAPHORES = (["cv", "cs", "ct", "cg", "sent", "l_nm", "l_ys", "l_v", "l_k", "st0", "st1", "st2", "y1", "y2", "y3"]
+              + ["ar%d%s" % (t, c) for t in range(1, 7) for c in "ab"])
 
-EST = {"cy": 0.83, "g": 1.55, "sc": 3.8, "lat": 90.0, "fix": 25.0, "pe": 0.42, "hop": 2800.0}
+EST = {"cy": 0.83, "g": 1.56, "sc": 3.8, "lat": 100.0, "v": 30.0, "s": 60.0, "pe": 0.42, "hop": 2800.0, "lv": 5500.0, "lk": 11500.0}
 
 
 def vt_(n):
-    return EST["fix"] + max(64.0, n) * EST["cy"]
+    return EST["v"] + max(64.0, n) * EST["cy"]
 
 
-def ga_(n):
-    return 55.0 + n * EST["g"] * EST["cy"]
+def st_(n):
+    return EST["s"] + max(64.0, n) * EST["cy"]
+
+
+def ga_(n, q):
+    return (55.0 if q == "v" else 70.0) + n * EST["g"] * EST["cy"]
 
 
 def pe_(*ns):
@@ -90,29 +83,48 @@ def build(g, core, T, topo):
     rank = T.rank_of(core)
     cores = T.cores
     ops = []
-    ph = [-1.0]
+    ph = [-1]
     V, Sc, Pe = g.vector, g.scalar, g.tensor
 
-    def op(q, dur, rd, wr, fn, banks=(), sig=None, fin=0.0, name=None):
+    def op(q, dur, rd, wr, fn, banks=(), sig=None, fin=0.0, name=None, free=()):
         ops.append({"q": q, "dur": dur, "rd": list(rd), "wr": list(wr), "fn": fn, "banks": tuple(banks), "sig": sig, "fin": fin,
-                    "name": name or wr[0], "pre": ph[0] < 0, "ph": ph[0]})
+                    "name": name or wr[0], "ph": ph[0], "free": set(free)})
 
-    def v(dur, rd, wr, fn, banks=(), name=None):
-        op("v", dur, rd, wr, fn, banks, name=name)
+    def v(n, rd, wr, fn, banks=(), name=None):
+        op("v", vt_(n), rd, wr, fn, banks, name=name)
 
-    def dma(q, out, in_, rd, wr, sem, fin):
-        e = g.sync if q == "y" else g.scalar
-        op(q, 60.0, rd, wr, lambda: e.dma_start(out, in_).then_inc(T.sem[sem], 16), sig=(sem, 16), fin=fin)
+    def s(n, rd, wr, fn, banks=(), name=None):
+        op("s", st_(n), rd, wr, fn, banks, name=name)
+
+    def mm(rd, wr, bank, groups, name=None, free=(), opens=True, closes=True):
+        def fn():
+            return [Pe.matmul(o, l, r, opens and i == 0, closes and i == len(grp) - 1) for grp in groups for i, (o, l, r, _) in enumerate(grp)]
+        op("t", pe_(*[x[3] for grp in groups for x in grp]), rd, wr, fn, [bank], name=name, free=free)
+
+    def lin(q, n, rd, wr, out, in_, add, banks=(), name=None, half=False):
+        if q == "v":
+            v(n / 2 if half else n, rd, wr, lambda: V.tensor_scalar(out, in_, add, None, A.add), banks, name)
+        else:
+            s(n, rd, wr, lambda: Sc.activation(out, in_, F.Identity, bias=add), banks, name)
+
+    def gat(q, n, rd, wr, out, win, add, name=None):
+        if q == "v":
+            op(q, ga_(n, q), rd, wr, lambda: V.tensor_scalar(out, win(), add, None, A.add), name=name)
+        else:
+            op(q, ga_(n, q), rd, wr, lambda: Sc.activation(out, win(), F.Identity, bias=add), name=name)
+
+    def dma(out, in_, rd, wr, sem, fin):
+        op("y", 60.0, rd, wr, lambda: g.sync.dma_start(out, in_).then_inc(T.sem[sem], 16), sig=(sem, 16), fin=fin)
 
     sent = [0]
 
-    dma("y", T.ys[:, 0:R], T.seen[:], [], ["ys0"], "l_ys", 2000.0)
-    dma("y", T.nm[:], T.nam[:], [], ["nm"], "l_nm", 2200.0)
-    dma("s", T.vt[:, 0:W // 2], T.val[:, 0:W // 2], [], ["vt0"], "l_v0", 3500.0)
-    dma("s", T.vt[:, W // 2:], T.val[:, W // 2:], [], ["vt1"], "l_v1", 5000.0)
-    for b in range(4):
-        dma("y", T.ck[:, b * 1024:(b + 1) * 1024], T.clk[:, b * 1024:(b + 1) * 1024], [], ["ck%d" % b], "l_k%d" % b, 6500.0 + 1500.0 * b)
-        ops[-1]["late"] = True
+    dma(T.ys[:, 0:R], T.seen[:], [], ["ys0", "q"], "l_ys", 2000.0)
+    dma(T.nm[:], T.nam[:], [], ["nm", "q"], "l_nm", 2200.0)
+    dma(T.vt[:], T.val[:], [], ["vt", "q"], "l_v", EST["lv"])
+    dma(T.ck[:, K0:K0 + W], T.clk[:], [], ["K", "q"], "l_k", EST["lk"])
+    for o in ops:
+        o["wr"].remove("q")
+        o["first"] = True
 
     def common(src):
         en = None
@@ -138,258 +150,233 @@ def build(g, core, T, topo):
        sig={"ys%d" % j: ("y%d" % j, len(common(cores[(rank - j) % N])) // 4) for j in range(1, N)}, fin=5000.0)
 
     flag = {"allow_small_or_imprecise_dtypes": True}
-    op("g", 1000.0, [], ["iq"], lambda: g.iota(T.iq[:], [[1, 512]], 0, 0, **flag))
-    op("g", 150.0, [], ["pi0"], lambda: g.iota(T.pi[:, 0:2], [[1, 2]], 0, 1))
-    op("g", 150.0, [], ["bi"], lambda: g.iota(T.bi[:], [[1, 8]], 0, 0))
-    op("g", 360.0, [], ["j0"], lambda: g.iota(T.j0[:], [[256, 8], [1, 17]], int(OFF), 0, **flag))
-    op("g", 350.0, [], ["j1"], lambda: g.iota(T.j1[:], [[256, 8], [1, 16]], 0, 0, **flag))
-    t0 = vt_(1)
+    op("g", 140.0, [], ["pi0"], lambda: g.iota(T.pi[:, 0:2], [[1, 2]], 0, 1))
+    op("g", 560.0, [], ["iq"], lambda: g.iota(T.iq[:], [[1, R]], 0, 0, **flag))
+    op("g", 560.0, [], ["qm"], lambda: g.iota(T.qm[:], [[0, 16], [1, 16]], 0, 0, **flag))
+    op("g", 350.0, [], ["qg"], lambda: g.iota(T.qg[:], [[16, 8], [0, 16]], 0, 0, **flag))
     col = lambda i: T.col[:, i:i + 1]
-    v(t0, ["pi0"], ["pi2"], lambda: V.tensor_scalar(T.pi[:, 2:4], T.pi[:, 0:2], 15, None, A.bitwise_and))
-    v(t0, ["pi0"], ["pi4"], lambda: V.tensor_scalar(T.pi[:, 4:5], T.pi[:, 0:1], 112, None, A.bitwise_and))
-    v(t0, ["pi0"], ["pi5"], lambda: V.tensor_scalar(T.pi[:, 5:6], T.pi[:, 0:1], 16, None, A.bitwise_and))
-    v(t0, ["pi0"], ["c0"], lambda: V.tensor_copy(col(0), T.pi[:, 0:1]))
-    v(t0, ["pi2"], ["c1"], lambda: V.tensor_copy(col(1), T.pi[:, 2:3]))
-    v(t0, ["pi2", "pi4"], ["c2"], lambda: V.tensor_tensor(col(2), T.pi[:, 3:4], T.pi[:, 4:5], A.add))
-    v(t0, ["pi4"], ["c3"], lambda: V.tensor_scalar(col(3), T.pi[:, 4:5], 15.0, None, A.add))
-    v(t0, ["pi0"], ["c4"], lambda: V.tensor_scalar(col(4), T.pi[:, 0:1], 16.0, None, A.add))
-    v(t0, ["pi5"], ["c5"], lambda: V.tensor_scalar(col(5), T.pi[:, 5:6], 4096.0, None, A.mult))
-    v(t0, ["pi5"], ["c6"], lambda: V.tensor_scalar(col(6), T.pi[:, 5:6], -4096.0, 65536.0, A.mult, A.add))
-    v(t0, ["pi2"], ["c7"], lambda: V.tensor_scalar(col(7), T.pi[:, 2:3], 16.0, None, A.mult))
-    v(t0, ["pi2"], ["c8"], lambda: V.tensor_scalar(col(8), T.pi[:, 2:3], float(W), None, A.add))
+    v(1, ["pi0"], ["pi2"], lambda: V.tensor_scalar(T.pi[:, 2:4], T.pi[:, 0:2], 15, None, A.bitwise_and))
+    v(1, ["pi0"], ["pi4"], lambda: V.tensor_scalar(T.pi[:, 4:5], T.pi[:, 0:1], 112, None, A.bitwise_and))
+    v(1, ["pi0"], ["c0"], lambda: V.tensor_copy(col(0), T.pi[:, 0:1]))
+    v(1, ["pi2"], ["c1"], lambda: V.tensor_copy(col(1), T.pi[:, 2:3]))
+    v(1, ["pi2", "pi4"], ["c2"], lambda: V.tensor_tensor(col(2), T.pi[:, 3:4], T.pi[:, 4:5], A.add))
+    v(1, ["pi4"], ["c3"], lambda: V.tensor_copy(col(3), T.pi[:, 4:5]))
+    for i, (a, b, src) in enumerate([(1.0, 15.0, 3), (1.0, 8.0, 1), (2.0, -2048.0 - K0, 1), (-B / 2, -B / 2, 1), (1.0, float(W), 1)]):
+        s(1, ["c%d" % src], ["c%d" % (4 + i)], lambda i=i, a=a, b=b, src=src: Sc.activation(col(4 + i), col(src), F.Identity, bias=b, scale=a))
     q128 = T.iq[:, 0:128]
-    t1 = vt_(128)
-    ts = t1 + 30
-    v(t1, ["iq", "c0"], ["eye"], lambda: V.tensor_scalar(T.eye[:], q128, col(0), None, A.is_equal))
-    v(t1, ["iq", "c0"], ["eye4"], lambda: V.tensor_scalar(T.eye4[:], q128, col(0), None, A.is_equal))
-    v(t1, ["iq", "c0"], ["neye"], lambda: V.tensor_scalar(T.neye[:], q128, col(0), -1.0, A.is_equal, A.mult))
-    v(t1, ["iq", "c0"], ["beye"], lambda: V.tensor_scalar(T.beye[:], q128, col(0), BIG / 2, A.is_equal, A.mult))
-    v(t1, ["iq", "c2"], ["bsh"], lambda: V.tensor_scalar(T.bsh[:], q128, col(2), BIG / 2, A.is_equal, A.mult))
-    v(vt_(256), ["beye", "bsh"], ["bis"], lambda: V.tensor_tensor(T.bis[:], T.beye[:], T.bsh[:], A.add))
-    v(t1, ["iq", "c0"], ["t1"], lambda: V.tensor_scalar(T.t1[:], q128, col(0), -1.0, A.is_gt, A.mult))
-    v(t1, ["iq", "c3"], ["t2"], lambda: V.tensor_scalar(T.t2[:], q128, col(3), None, A.is_le))
-    v(vt_(256), ["t1", "t2"], ["t1"], lambda: V.tensor_tensor(T.t1[:], T.t1[:], T.t2[:], A.mult))
-    v(vt_(256), ["t1", "eye"], ["low"], lambda: V.tensor_tensor(T.low[:], T.t1[:], T.eye[:], A.add))
-    v(t0, [], ["ones"], lambda: V.memset(T.ones[:], 1.0))
-    v(t0, [], ["cz0"], lambda: V.memset(T.cz[:, 0:128], BIG / 256))
-    v(t0, [], ["cz1"], lambda: V.memset(T.cz[:, 128:256], BIG / 256 + 16.0))
-    v(t0, [], ["cz2"], lambda: V.memset(T.cz[:, 256:384], -BIG / 128))
-    v(vt_(144), ["iq", "c3"], ["wb"], lambda: V.tensor_scalar(T.wb[:], T.iq[:, 0:144], col(3), 4096.0, A.is_equal, A.mult))
-    v(vt_(144), ["iq", "c3"], ["wc"], lambda: V.tensor_scalar(T.wc[:], T.iq[:, 0:144], col(3), 8192.0, A.is_equal, A.mult))
-    wn = lambda nl: T.wb[:, 15 - nl:143 - nl]
-    wm = lambda nl: T.wc[:, 15 - nl:143 - nl]
-    v(vt_(160), ["iq", "c4", "c6"], ["h0"], lambda: V.tensor_scalar(T.h0[:], T.iq[:, 0:160], col(4), col(6), A.is_equal, A.mult))
-    v(vt_(160), ["iq", "c4", "c5"], ["h1"], lambda: V.tensor_scalar(T.h1[:], T.iq[:, 0:160], col(4), col(5), A.is_equal, A.mult))
-    v(t0, ["iq", "c1"], ["tri"], lambda: V.tensor_scalar(T.tri[:], T.iq[:, 0:16], col(1), None, A.is_gt))
-    for nl in range(1, 16):
-        v(t0, ["wc", "tri"], ["wt%d" % nl], lambda nl=nl: V.tensor_scalar(T.wt[:, nl * 128:(nl + 1) * 128], wm(nl), T.tri[:, nl:nl + 1], None, A.mult))
-    v(vt_(136), ["j0", "c7"], ["jj"], lambda: V.tensor_scalar(T.jj[:], T.j0[:], col(7), None, A.add))
-    v(t0, [], ["jj"], lambda: V.memset(T.jj[:, 16::17], SEN))
-    v(t1, ["j1", "c7"], ["jc"], lambda: V.tensor_scalar(T.jc[:], T.j1[:], col(7), None, A.add))
-    v(t1, [], ["sd"], lambda: V.memset(T.sd[:], 0.0))
-    v(t0, [], ["sd"], lambda: V.memset(T.sd[:, 0::16], 1e9))
-    v(vt_(512), [], ["sj"], lambda: V.memset(T.sj[:], 0.0))
-    v(t0, [], ["sj"], lambda: V.memset(T.sj[:, 0::16], -1e9))
-    v(t0, ["bi"], ["bl"], lambda: V.tensor_copy(T.bl[:], T.bi[:]))
-    v(t0, [], ["ttx"], lambda: V.memset(T.tt[:, W:W + 16], 0.0))
+    ts = lambda out, in_, a, b, o0, o1: (lambda: V.tensor_scalar(out, in_, a, b, o0, o1))
+    sc = lambda out, in_, a, b=0.0: (lambda: Sc.activation(out, in_, F.Identity, bias=b, scale=a))
+    v(128, ["iq", "c0"], ["eye"], ts(T.eye[:], q128, col(0), 1.0, A.is_equal, A.mult))
+    s(128, ["eye"], ["neye"], sc(T.neye[:], T.eye[:], -1.0))
+    s(128, ["eye"], ["n15"], sc(T.n15[:], T.eye[:], -15.0))
+    v(128, ["qg", "c3"], ["blk"], ts(T.blk[:], T.qg[:], col(3), 1.0, A.is_equal, A.mult))
+    s(128, ["blk"], ["nblk"], sc(T.nblk[:], T.blk[:], -1.0))
+    v(128, ["iq", "c2"], ["nsh"], ts(T.nsh[:], q128, col(2), -1.0, A.is_equal, A.mult))
+    v(256, ["eye", "nsh"], ["ish"], lambda: V.tensor_tensor(T.ish[:], T.eye[:], T.nsh[:], A.subtract))
+    s(128, ["blk"], ["t1"], sc(T.t1[:], T.blk[:], -B / 2))
+    op("g", 390.0, ["t1"], ["t2"], lambda: g.affine_select(T.t2[:], T.t1[:], [[1, 128]], A.is_gt, 0.0, 0, -1))
+    op("g", 390.0, ["t2"], ["tm"], lambda: g.affine_select(T.tm[:], T.t2[:], [[1, 128]], A.not_equal, B / 2, 0, -1))
+    s(128, ["iq", "c7"], ["czr"], lambda: Sc.activation(T.czr[:], q128, F.Identity, bias=col(7), scale=0.0))
+    v(64, [], ["k1"], lambda: V.memset(T.k1[:], 2048.0 - 2 * B))
+    v(64, [], ["k2"], lambda: V.memset(T.k2[:], 2048.0))
+    v(144, ["iq", "c4"], ["w1"], ts(T.w1[:], T.iq[:, 0:144], col(4), 1.0, A.is_equal, A.mult))
+    for nme, x in (("w16", 16.0), ("w2", 2.0), ("wo", WO)):
+        s(144, ["w1"], [nme], sc(T[nme][:], T.w1[:], x))
+    sel = lambda w, nl: T[w][:, 15 - nl:143 - nl]
+    s(64, ["qm"], ["kc"], sc(T.kc[:], T.qm[:, 0:64], 1.0, -7.75))
+    v(128, ["qm"], ["sd"], ts(T.sd[:], T.qm[:, 0:128], 0.0, 1e9, A.is_equal, A.mult))
+    v(512, [], ["sj"], lambda: V.memset(T.sj[:], 0.0))
+    v(64, [], ["sj"], lambda: V.memset(T.sj[:, 0::16], -16384.0))
+    v(32, ["iq", "c5"], ["e1"], ts(T.e1[:], T.iq[:, 0:32], col(5), 1.0, A.is_equal, A.mult))
+    s(32, ["e1"], ["pe"], sc(T.pe[:], T.e1[:], -B, B))
+    s(R, ["iq"], ["ncn"], sc(T.ncn[:], T.iq[:], 2.0, -2048.0 - K0))
+    s(16, ["iq", "c6"], ["ncr"], lambda: Sc.activation(T.ncr[:], T.iq[:, 0:16], F.Identity, bias=col(6), scale=32.0))
+    v(R, ["qm", "c1"], ["tri"], ts(T.tri[:], T.qm[:], col(1), 0.5, A.is_le, A.mult))
+    v(K0, [], ["exa", "exb"], lambda: V.memset(T.ck[:, 0:K0], 0), name="ex0")
+    v(16, [], ["Kx"], lambda: V.memset(T.ck[:, K0 + W:], 0))
+    v(32, [], ["sua", "sub"], lambda: V.memset(T.su[:], 0), name="su0")
     for c in "ab":
-        v(t0, [], ["tgx" + c], lambda c=c: V.memset(T["tg" + c][:, 2048:2056], -4096.0))
-        v(t0, [], ["cbx" + c], lambda c=c: V.memset(T["cb" + c][:, :, :, 16], 0.0))
-        v(t0, [], ["su" + c], lambda c=c: V.memset(T["su" + c][:], 0))
-    v(vt_(256), ["nm"], ["lu0a", "lu0b"], lambda: V.tensor_copy(T.lu[:, 0:R], T.nm[:]))
-    v(vt_(256), ["nm"], ["lf0a", "lf0b"], lambda: V.tensor_scalar(T.lf[:, 0:R], T.nm[:], -2048.0, None, A.add))
+        v(1, [], ["bc" + c], lambda c=c: V.memset(T["bc" + c][:], -7.0))
+        for q in range(4):
+            if CFG["cp"][c][q] == "1":
+                v(1, ["c1"], ["c9"], ts(col(9), col(1), 4.0 * q - 0.5, -16.0, A.is_gt, A.mult))
+                v(1, ["c1"], ["c10"], ts(col(10), col(1), 4.0 * q + 3.5, 16.0, A.is_gt, A.mult))
+                v(1, ["c9", "c10"], ["bc" + c], lambda c=c: V.tensor_scalar(T["bc" + c][:], T["bc" + c][:], col(9), col(10), A.add, A.add))
+                ops[-1]["rd"].append("bc" + c)
+    v(R, ["nm"], ["lu0a", "lu0b"], lambda: V.tensor_copy(T.lu[:, 0:R], T.nm[:]))
     for k in range(16):
-        v(vt_(128), ["ys0"], ["yx0_%d" % k], lambda k=k: V.tensor_copy(T.yx[:, k:W:16], T.ys[:, 0:R]))
+        v(R / 2, ["ys0"], ["yx0_%d" % k], lambda k=k: V.tensor_copy(T.yx[:, k:W:16], T.ys[:, 0:R]))
     for j in range(1, N):
         for k in range(16):
             op("g", 600.0, ["ys%d" % j], ["yx%d_%d" % (j, k)],
                lambda j=j, k=k: g.affine_select(T.yx[:, j * W + k:(j + 1) * W:16], T.ys[:, j * R:(j + 1) * R], [[0, R]], A.is_gt, 0.0, 1, 0))
-    v(vt_(512), ["iq"], ["f0"], lambda: V.tensor_scalar(T.f0[:], T.iq[:], 1.0 / 4096, 0.5 / 4096, A.mult, A.add))
-    for b in range(8):
-        bk = 2 + b % 5
-        ps = T["ps%d" % bk]
-        op("s", vt_(512) + 30, ["f0"], ["ps%d" % bk], lambda b=b, ps=ps: Sc.activation(ps[:], T.f0[:], F.Identity, bias=b / 8.0 - 2048.0), [bk])
-        v(vt_(512), ["ps%d" % bk, "ck%d" % (b // 2)], ["tt"] if b == 0 else ["tt%d" % b],
-          lambda b=b, ps=ps: V.tensor_tensor(T.tt[:, b * 512:(b + 1) * 512], T.ck[:, b * 512:(b + 1) * 512], ps[:], A.add), [bk])
-    TT = ["tt", "ttx"] + ["tt%d" % b for b in range(1, 8)]
-    dbank = [0]
+    cbank = [0]
+    KW = T.ck[:, K0:K0 + W]
 
-    def half(t, h):
-        c = "ab"[h]
-        B = lambda n: T[n + c]
-        n0 = t * R + (1 - h) * C
-        pu, pf = "lu%d%s" % (t, c), "lf%d%s" % (t, c)
-        PF = T.lf[:, n0:n0 + C]
-        b1, b2 = 2 + h, 4 + h
-        p1, p2, p6 = T["ps%d" % b1], T["ps%d" % b2], T.ps6
-        f1, f2, f6 = ([["ps%d" % b] for b in (b1, b2, 6)] if t == 0 else ([], [], []))
-        dk, uu, oo, lo, z1 = p1[:, 0:128], p1[:, 128:264], p1[:, 264:272], p1[:, 272:280], p1[:, 384:512]
-        th, pp = p6[:, h * 128:h * 128 + 128], p2[:, 384:512]
+    def half(t, c):
+        r0 = C if c == "a" else 0
+        rs, ns = slice(r0, r0 + C), slice(r0 // 16, r0 // 16 + 8)
+        H = lambda n: T[n + c]
         k_ = lambda n: n + c
+        eng = CFG["eng"]
+        n0 = t * R + r0
+        pu = "lu%d%s" % (t, c)
+        PF = T.pf[:, rs]
+        b1, b2 = (3, 5) if c == "a" else (4, 6)
+        p1, p2 = T["ps%d" % b1], T["ps%d" % b2]
+        uu, zz, orr, ofr = p1[:, 128:256], p1[:, 256:384], p1[:, 384:392], p1[:, 392:400]
+        ol, pp, b0, kp = p2[:, 0:128], p2[:, 128:256], p2[:, 256:384], p2[:, 384:512]
         j = t % N
         yxs = ["yx%d_%d" % (j, k) for k in range(16)]
-        for s in range(4):
-            cs = slice(s * 512, (s + 1) * 512)
-            off = T.lu[:, n0 + s * 32:n0 + (s + 1) * 32]
-            y0 = j * W + (1 - h) * 2048 + s * 512
-            if (h, s) in CFG["vgv"]:
-                v(ga_(512), [pu, "vt0", "vt1"] + yxs, [k_("vg%d" % s)],
-                  lambda cs=cs, off=off, y0=y0: V.tensor_tensor(B("vg")[:, cs], T.vt[:, 0:W].indirect(off), T.yx[:, y0:y0 + 512], A.subtract))
-                op("s", vt_(512) + 30, [k_("vg%d" % s)], [k_("ab%d" % s)],
-                   lambda s=s, cs=cs: Sc.activation(B("ab")[:, 2 * s:2 * s + 2], B("vg")[:, cs], F.Abs))
+        vp, kq, cp = CFG["vp0" if t == 0 else "vp"][c], CFG["kg0" if t == 0 else "kg"][c], CFG["cp"][c]
+        lin(eng["pf"], C, [pu], [k_("pf")], PF, T.lu[:, n0:n0 + C], -2048.0, half=True)
+        for x in range(4):
+            cs = slice(x * 512, (x + 1) * 512)
+            win = lambda x=x: T.vt[:, 0:W].indirect(T.lu[:, n0 + x * 32:n0 + (x + 1) * 32])
+            y0 = j * W + r0 * 16 + x * 512
+            yy, ab, vx, vq = T.yx[:, y0:y0 + 512], H("ab")[:, 2 * x:2 * x + 2], H("vx")[:, 2 * x:2 * x + 2], H("vq")[:, cs]
+            if vp[x] == "1":
+                op("v", ga_(512, "v"), [pu, "vt"] + yxs, [k_("vx%d" % x)], lambda vx=vx, win=win, yy=yy: V.tensor_tensor(vx, win(), yy, A.subtract), name=k_("vg"))
+                v(256, [k_("vx%d" % x)], [k_("ab%d" % x)], ts(ab, vx, 0.0, -2.0, A.min, A.mult), name=k_("ab"))
+            elif vp[x] == "2":
+                op("v", ga_(512, "v"), [pu, "vt"] + yxs, [k_("vq%d" % x)], lambda vq=vq, win=win, yy=yy: V.tensor_tensor(vq, win(), yy, A.subtract), name=k_("vg"))
+                s(512, [k_("vq%d" % x)], [k_("ab%d" % x)], lambda ab=ab, vq=vq: Sc.activation(ab, vq, F.Abs), name=k_("ab"))
             else:
-                op("s", ga_(512) + 10, [pu, "vt0", "vt1"], [k_("vg%d" % s)],
-                   lambda cs=cs, off=off: Sc.activation(B("vg")[:, cs], T.vt[:, 0:W].indirect(off), F.Copy))
-                bk = (0, 1, 7)[dbank[0] % 3]
-                dbank[0] += 1
-                pd = T["ps%d" % bk]
-                op("t", pe_(512, 512), [k_("vg%d" % s), "eye", "neye"] + yxs, ["pd%d" % bk],
-                   lambda cs=cs, pd=pd, y0=y0: [Pe.matmul(pd[:], T.eye[:], B("vg")[:, cs], True, False),
-                                                Pe.matmul(pd[:], T.neye[:], T.yx[:, y0:y0 + 512], False, True)], [bk], name=k_("pd%d" % s))
-                op("s", vt_(512) + 30, ["pd%d" % bk], [k_("ab%d" % s)],
-                   lambda s=s, pd=pd: Sc.activation(B("ab")[:, 2 * s:2 * s + 2], pd[:], F.Abs), [bk])
-            if (h, s) in CFG["tgv"]:
-                v(ga_(512), [pu] + TT, [k_("tg%d" % s)], lambda cs=cs, off=off: V.tensor_copy(B("tg")[:, cs], T.tt[:, 0:W].indirect(off)))
-            else:
-                op("s", ga_(512) + 10, [pu] + TT, [k_("tg%d" % s)],
-                   lambda cs=cs, off=off: Sc.activation(B("tg")[:, cs], T.tt[:, 0:W].indirect(off), F.Copy))
-            v(vt_(512), [k_("tg%d" % s), "sj"], [k_("js%d" % s)],
-              lambda cs=cs: V.tensor_tensor_scan(B("js")[:, cs], T.sj[:], B("tg")[:, cs], 0.0, A.add, A.max))
-        tgs = [k_("tg%d" % s) for s in range(4)]
+                gat("s", 512, [pu, "vt"], [k_("vq%d" % x)], vq, win, 0.0, name=k_("vg"))
+                mm([k_("vq%d" % x), "eye", "neye"] + yxs, ["pd0"], 0, [[(T.ps0[:], T.eye[:], vq, 512), (T.ps0[:], T.neye[:], yy, 512)]], name=k_("pd"))
+                s(512, ["pd0"], [k_("ab%d" % x)], lambda ab=ab: Sc.activation(ab, T.ps0[:], F.Abs), [0], name=k_("ab"))
+        kn = 2048 // len(kq)
+        for x in range(len(kq)):
+            cs = slice(x * kn, (x + 1) * kn)
+            gat(kq[x], kn, [pu, "K"], [k_("kg%d" % x)], H("kg")[:, cs],
+                lambda x=x: KW.indirect(T.lu[:, n0 + x * kn // 16:n0 + (x + 1) * kn // 16]), -2048.0, name=k_("kg"))
+            v(kn / 2, [k_("kg%d" % x), "sj"], [k_("js%d" % x)],
+              lambda cs=cs: V.tensor_tensor_scan(H("js")[:, cs], T.sj[:, 0:kn], H("kg")[:, cs], 0.0, A.add, A.max), name=k_("js"))
+        kgs, jss = [k_("kg%d" % x) for x in range(len(kq))], [k_("js%d" % x) for x in range(len(kq))]
         for x in range(2):
-            op("t", pe_(*[64] * 17), [k_("ab%d" % s) for s in (2 * x, 2 * x + 1)] + ["wb", "eye", "jc"], [k_("dk%d" % x)] + f1,
-               lambda x=x: [Pe.matmul(p1[:, 64 * x:64 * x + 64], T.eye[:], T.jc[:, 64 * x:64 * x + 64], True, False)] +
-                           [Pe.matmul(p1[:, 64 * x:64 * x + 64], wn(nl), B("ab")[:, 4 * x:4 * x + 4, nl, :], False, nl == 15) for nl in range(16)], [b1])
-        v(vt_(128), [k_("dk0"), k_("dk1"), "sd"], [k_("ks")], lambda: V.tensor_tensor_scan(B("ks")[:], T.sd[:], dk, 0.0, A.add, A.min), [b1])
-        v(t0, [k_("ks")], [k_("k1")], lambda: V.tensor_copy(B("k1")[:], B("ks")[:, 15::16]))
-        v(t0, [k_("k1")], [k_("k2")], lambda: V.tensor_scalar(B("k2")[:], B("k1")[:], 4095, None, A.bitwise_and))
-        v(t0, [k_("k2")], [k_("ku")], lambda: V.tensor_copy(B("ku")[:], B("k2")[:]))
-        tw = lambda: B("tg")[:, 0:2048].indirect(B("ku")[:])
-        if (h, 4) in CFG["tgv"]:
-            v(ga_(C), [k_("ku")] + tgs, [k_("tm")], lambda: V.tensor_scalar(B("tm")[:], tw(), -0.5, None, A.add))
+            d = p1[:, 64 * x:64 * x + 64]
+            grp = [(d, T.eye[:], T.kc[:], 64)] + [(d, sel("w16", nl), H("ab")[:, 4 * x:4 * x + 4, nl, :], 64) for nl in range(16)]
+            ones = [y for y in (2 * x, 2 * x + 1) if vp[y] == "1"]
+            if ones:
+                a, b = ones[0], ones[-1] + 1
+                grp += [(p1[:, 32 * a:32 * b], sel("w16", nl), H("vx")[:, 2 * a:2 * b, nl, :], 64) for nl in range(16)]
+            mm([k_("ab%d" % y) for y in (2 * x, 2 * x + 1)] + [k_("vx%d" % y) for y in ones] + ["w16", "eye", "kc"], [k_("dk%d" % x)], b1, [grp], name=k_("dk"))
+        v(C, [k_("dk0"), k_("dk1"), "sd"], [k_("ks")], lambda: V.tensor_tensor_scan(T.ks[:, rs], T.sd[:], p1[:, 0:128], 0.0, A.add, A.min), [b1])
+        kl = T.ks[:, r0 + 15:r0 + C:16]
+        v(8, [k_("ks")], [k_("kt")], ts(T.kt[:, ns], kl, M16, -M16 - 16.0, A.add, A.add))
+        if CFG["tt16"]:
+            v(16, [k_("ks"), k_("kt")], [k_("ku")], lambda: V.tensor_tensor(T.ku[:, ns], kl, T.kt[:, ns], A.subtract))
         else:
-            op("s", ga_(C) + 10, [k_("ku")] + tgs, [k_("tm")], lambda: Sc.activation(B("tm")[:], tw(), F.Identity, bias=-0.5))
-        if (h, 4) in CFG["vgv"]:
-            v(ga_(C), [k_("ku")] + tgs, [k_("to")], lambda: V.tensor_copy(B("to")[:], tw()))
-        else:
-            op("s", ga_(C) + 10, [k_("ku")] + tgs, [k_("to")], lambda: Sc.activation(B("to")[:], tw(), F.Copy))
-        v(t1, [k_("tm")], [k_("th")] + f6, lambda: V.tensor_scalar(th, B("tm")[:], M, -M, A.add, A.add), [6])
-        for k in range(16):
-            v(t1, tgs + [k_("th")], [k_("cb%d" % k)],
-              lambda k=k: V.tensor_tensor(B("cb")[:, :, :, k], B("tg")[:, k:2048:16], th, A.is_lt), [6], name=k_("cb"))
-        v(t1, [k_("to"), k_("th")], [k_("fr")], lambda: V.tensor_tensor(B("fr")[:], B("to")[:], th, A.subtract), [6])
-        v(t1, [k_("fr")], [k_("o6")], lambda: V.tensor_scalar(B("o6")[:], B("fr")[:], 4096.0, -2048.5, A.mult, A.add))
-        op("t", pe_(128), [pf, "eye"], [k_("pp")] + f2, lambda: Pe.matmul(pp, T.eye[:], PF, True, True), [b2])
-        v(t1, [k_("pp"), k_("o6")], [k_("eq")], lambda: V.tensor_tensor(B("eq")[:], B("o6")[:], pp, A.is_equal), [b2])
-        v(t0, [k_("eq")], [k_("et")], lambda: V.transpose(B("et")[:], B("eq")[:]))
-        op("t", pe_(128), [k_("eq"), "low"], [k_("z1")], lambda: Pe.matmul(z1, T.low[:], B("eq")[:], True, True), [b1])
-        op("t", pe_(*[8] * 16), [k_("o6"), "wb"], [k_("oo")],
-           lambda: [Pe.matmul(oo, wn(nl), B("o6")[:, nl::16], nl == 0, nl == 15) for nl in range(16)], [b1])
-        op("s", ts, [k_("z1")], [k_("nr")], lambda: Sc.activation(B("nr")[:], z1, F.Sign, bias=0.5, scale=-1.0), [b1])
-        op("s", t0 + 30, [k_("oo")], [k_("oa")], lambda: Sc.activation(B("oa")[:], oo, F.Identity, bias=SEN, scale=1.0 / 65536), [b1])
-        op("t", pe_(384, 128, 128, 128, 128), [k_("nr"), pf, "ones", "cz0", "cz1", "cz2", "beye", "bsh", "bis", "eye"], [k_("zz"), k_("p0")],
-           lambda: [Pe.matmul(p2[:, 0:384], T.ones[:], T.cz[:], True, False),
-                    Pe.matmul(p2[:, 0:128], T.beye[:], B("nr")[:], False, False),
-                    Pe.matmul(p2[:, 128:256], T.bsh[:], B("nr")[:], False, False),
-                    Pe.matmul(p2[:, 256:384], T.bis[:], B("nr")[:], False, False),
-                    Pe.matmul(p2[:, 256:384], T.eye[:], PF, False, True)], [b2], name=k_("zp"))
-
-        def same():
-            r = [Pe.matmul(uu, T.wt[:, 0:128], T.wc[:, 0:136], True, False)]
-            for m in range(4):
-                for b in range(2):
-                    for a in range(2):
-                        hb = T.h0 if b == 0 else T.h1
-                        x = 16 + 16 * (b - a)
-                        u0 = 128 + (2 * m + b) * 17
-                        r.append(Pe.matmul(p1[:, u0:u0 + 16], hb[:, x:x + 128], B("et")[:, m * 32 + a * 16:m * 32 + a * 16 + 16], False, False))
-            return r
-        op("t", pe_(*([136] + [16] * 16)), [k_("et"), k_("z1"), k_("oo"), "h0", "h1", "wc", "wt0"], [k_("uu")], same, [b1], name=k_("u0"))
-        op("t", pe_(*[136] * 16), [k_("cb%d" % k) for k in range(16)] + [k_("cbx"), "wc"], [k_("uu")],
-           lambda: [Pe.matmul(uu, wm(nl), B("cb")[:, :, nl, :], False, nl == 15) for nl in range(16)], [b1])
-        v(vt_(136), [k_("uu"), "jj"], [k_("us")],
-          lambda: V.tensor_tensor_scan(B("us")[:, ::-1], p1[:, 263:127:-1], T.jj[:, ::-1], 0.0, A.min, A.max), [b1])
-        v(t0, [k_("us")], [k_("ju")], lambda: V.tensor_scalar(B("ju")[:], B("us")[:, 0::17], -OFF, 2048.0, A.add, A.min))
-        fw = lambda: B("tg")[:, 0:2056].indirect(B("ju")[:])
-        v(ga_(C), [k_("ju"), k_("tgx")] + tgs, [k_("xf")], lambda: V.tensor_scalar(B("xf")[:], fw(), 4096.0, -0.5, A.mult, A.add))
-        op("s", ga_(C) + 10, [k_("ju"), k_("tgx")] + tgs, [k_("yy")], lambda: Sc.activation(B("yy")[:], fw(), F.Identity, bias=-12288.0, scale=-4.0))
-        v(t1, [k_("xf")], [k_("kf")], lambda: V.tensor_scalar(B("kp")[:, 0:C], B("xf")[:], 12, None, A.arith_shift_right))
-        v(t1, [k_("xf")], [k_("pn")], lambda: V.tensor_scalar(B("kp")[:, C:2 * C], B("xf")[:], 4095, None, A.bitwise_and))
-        op("s", ts, [k_("js%d" % s) for s in range(4)], [k_("ja")], lambda: Sc.activation(B("ja")[:], B("js")[:, 15::16], F.Identity, bias=-0.5))
-        op("s", ts, [k_("ja")], [k_("jb")], lambda: Sc.activation(B("jb")[:], B("ja")[:], F.Identity, bias=M))
-        op("s", ts, [k_("jb")], [k_("ji")], lambda: Sc.activation(B("ji")[:], B("jb")[:], F.Identity, bias=-M))
-        v(t1, [k_("ji"), k_("pp")], [k_("pp")], lambda: V.tensor_tensor(pp, B("ji")[:], pp, A.max), [b2], name=k_("pa"))
-        v(t1, [k_("yy"), k_("pp")], [k_("aa")], lambda: V.tensor_tensor(B("aa")[:], B("yy")[:], pp, A.min), [b2])
-        v(vt_(256), [k_("kf"), k_("pn"), k_("zz")], [k_("zz")], lambda: V.tensor_tensor(p2[:, 0:256], B("kp")[:], p2[:, 0:256], A.subtract), [b2])
-        v(t1, [k_("aa"), k_("p0")], [k_("ba")], lambda: V.tensor_tensor(B("ba")[:], B("aa")[:], p2[:, 256:384], A.max), [b2])
-        v(t1, [k_("ba"), k_("zz")], [k_("mm")], lambda: V.tensor_tensor(B("mm")[:], B("ba")[:], p2[:, 0:128], A.max), [b2])
-        NF, NU = T.nf[:, n0:n0 + C], T.nu[:, n0:n0 + C]
-        v(t1, [k_("mm"), k_("zz")], [k_("nf%d" % t)], lambda: V.tensor_tensor(NF, B("mm")[:], p2[:, 128:256], A.max), [b2], name=k_("nf"))
+            v(16, [k_("ks"), k_("kt")], [k_("kw")], lambda: V.tensor_tensor(T.kw[:, ns], kl, T.kt[:, ns], A.subtract))
+            v(8, [k_("kw")], [k_("ku")], lambda: V.tensor_copy(T.ku[:, ns], T.kw[:, ns]))
+        po, pen = T.po[:, rs], T.pen[:, rs]
+        op("v", ga_(C, "v"), [k_("ku"), k_("pf"), "e1"], [k_("po")], lambda: V.tensor_tensor(po, T.e1[:, 0:32].indirect(T.ku[:, ns]), PF, A.mult))
+        gat("s", C, [k_("ku"), "pe"], [k_("pen")], pen, lambda: T.pe[:, 0:32].indirect(T.ku[:, ns]), 0.0)
+        mm([k_("po"), "w1"], [k_("or")], b1, [[(orr, sel("w1", nl), T.po[:, r0 + nl:r0 + C:16], 8) for nl in range(16)]])
+        lin(eng["ou"], 8, [k_("or")], [k_("ou")], T.ou[:, ns], orr, 2048.0, [b1])
+        lin("s", 8, [k_("or")], [k_("of")], T.of[:, ns], orr, 0.0, [b1])
+        gat(eng["ko"], C, [k_("ou"), "K"], [k_("ko")], T.ko[:, rs], lambda: KW.indirect(T.ou[:, ns]), -2048.0)
+        mm([k_("po"), "blk"], [k_("ol")], b2, [[(ol, T.blk[:], po, C)]])
+        v(C, [k_("ol"), k_("pf")], [k_("eq")], lambda: V.tensor_tensor(T.eq[:, rs], PF, ol, A.is_equal), [b2])
+        if "1" in cp:
+            mm([k_("ko"), "eye"], [k_("kp")], b2, [[(kp, T.eye[:], T.ko[:, rs], C)]])
+        for q in range(4):
+            ks_ = range(4 * q, 4 * q + 4)
+            if cp[q] == "1":
+                for k in ks_:
+                    v(C, kgs + [k_("kp")], [k_("cb%d" % k)],
+                      lambda k=k: V.tensor_tensor(H("cb")[:, k * C:(k + 1) * C], H("kg")[:, k::16], kp, A.is_ge), [b2], name=k_("cb"))
+            else:
+                bk = 1 + cbank[0] % 2
+                cbank[0] += 1
+                pd = T["ps%d" % bk]
+                mm(kgs + [k_("ko"), "eye", "neye"], ["pd%d" % bk], bk,
+                   [[(pd[:, i * C:(i + 1) * C], T.eye[:], H("kg")[:, k::16], C), (pd[:, i * C:(i + 1) * C], T.neye[:], T.ko[:, rs], C)] for i, k in enumerate(ks_)], name=k_("df"))
+                s(512, ["pd%d" % bk], [k_("cb%d" % k) for k in ks_],
+                  lambda q=q, pd=pd: Sc.activation(H("cb")[:, q * 512:(q + 1) * 512], pd[:], F.Sign, bias=0.5), [bk], name=k_("cb"))
+            grp = [(uu, sel("w2" if cp[q] == "1" else "w1", k), H("cb")[:, k * C:(k + 1) * C], C) for k in ks_]
+            if q == 3:
+                grp.append((uu, T.n15[:], T.eq[:, rs], C))
+            mm([k_("cb%d" % k) for k in ks_] + ["w1", "w2", "n15"] + ([k_("eq")] if q == 3 else [k_("ou"), k_("of")] if q == 0 else []), [k_("uu")], b1, [grp],
+               free=[k_("uu")] if q else [], opens=q == 0, closes=q == 3)
+        s(C, [k_("uu"), k_("bc")], [k_("ov")], lambda: Sc.activation(T.ov[:, rs], uu, F.Sign, bias=H("bc")[:]), [b1])
+        mm([k_("ov"), k_("pf"), "tm", "czr", "eye"], [k_("zz")], b1, [[(zz, T.eye[:], PF, C), (zz, T.eye[:], T.czr[:], C), (zz, T.tm[:], T.ov[:, rs], C)]])
+        v(C, [k_("zz"), "ncn"], [k_("va")], lambda: V.tensor_tensor(T.va[:, rs], T.ncn[:, rs], zz, A.max), [b1])
+        mm([k_("va"), "w1", "n15", "ncr"], [k_("ofr")], b1,
+           [[(ofr, T.n15[:], T.ncr[:, ns], 8)] + [(ofr, sel("w1", nl), T.va[:, r0 + nl:r0 + C:16], 8) for nl in range(16)]])
+        lin(eng["off"], 8, [k_("ofr")], [k_("off")], T.off[:, ns], ofr, 2048.0 + K0 - 2 * r0, [b1])
+        mm([k_("pf"), "eye"], [k_("pp")], b2, [[(pp, T.eye[:], PF, C)]])
+        v(C, jss + [k_("pp")], [k_("ac")], lambda: V.tensor_tensor(T.ac[:, rs], H("js")[:, 15::16], pp, A.max), [b2])
+        mm([k_("ac"), k_("pen"), "eye"], [k_("pp")], b2, [[(pp, T.eye[:], T.ac[:, rs], C), (pp, T.eye[:], pen, C)]], name=k_("px"))
+        lin("s", C, [k_("pp")], [k_("ex")], T.ck[:, 2 * r0:2 * r0 + 2 * C:2], pp, 2048.0, [b2])
+        lin("s", C, jss, [k_("ju")], T.ju[:, rs], H("js")[:, 15::16], 2048.0)
+        mm([k_("pf"), k_("pen"), "eye", "ish", "k1"], [k_("b0")], b2, [[(b0, T.eye[:], PF, C), (b0, T.eye[:], T.k1[:], C), (b0, T.ish[:], pen, C)]])
+        mm([k_("va"), k_("pen"), "eye", "nsh", "k2", "n15", "ncn", "blk"], [k_("ol")], b2,
+           [[(ol, T.eye[:], T.k2[:], C), (ol, T.n15[:], T.ncn[:, rs], C), (ol, T.nsh[:], pen, C), (ol, T.blk[:], T.va[:, rs], C)]], name=k_("yb"))
+        op("v", ga_(C, "v"), [k_("off"), k_("pen"), "K", "exa"] + (["exb"] if c == "b" else []), [k_("xf")],
+           lambda: V.tensor_tensor(T.xf[:, rs], T.ck[:, 2 * r0:K0 + W].indirect(T.off[:, ns]), pen, A.subtract))
+        v(C, [k_("xf"), k_("b0")], [k_("m1")], lambda: V.tensor_tensor(T.m1[:, rs], T.xf[:, rs], b0, A.max), [b2])
         last = t == RO - 1
-        if not last:
-            v(t0, [k_("nf%d" % t)], [k_("nu%d" % t)], lambda: V.tensor_scalar(NU, NF, 2048.0, None, A.add), name=k_("nu"))
+        if last:
+            src, dst = T.nf[:, rs], T.op[:, rs]
+        else:
+            src, dst = T.nu[:, n0:n0 + C], T.lu[:, n0 + R:n0 + R + C]
+        if last or CFG["tt16"]:
+            v(C, [k_("m1"), k_("ol")], [k_("nu%d" % t)], lambda: V.tensor_tensor(src, T.m1[:, rs], ol, A.max), [b2], name=k_("nu"))
+        else:
+            v(C, [k_("m1"), k_("ol")], [k_("nf")], lambda: V.tensor_tensor(T.nf[:, rs], T.m1[:, rs], ol, A.max), [b2])
+            v(C, [k_("nf")], [k_("nu%d" % t)], lambda: V.tensor_copy(src, T.nf[:, rs]), name=k_("nu"))
         hop = 1 if not last else -t
-        dst, src = cores[(rank + hop) % N], cores[(rank - hop) % N]
+        to, frm = cores[(rank + hop) % N], cores[(rank - hop) % N]
         sem = "ar%d%s" % (t + 1, c)
-        k = len(common(core))
 
         def send():
-            assert topo.may_write(core, dst)
-            rid, pid, _ = topo.addr(dst)
+            assert topo.may_write(core, to)
+            rid, pid, _ = topo.addr(to)
             en = common(core)
-            ea, eb = en[:k // 2], en[k // 2:]
-            d = [DstId(rid=rid, pnc=pid)]
-            x = n0 + R
-            if last:
-                tr = [RemoteDMATransfer(dst_ids=d, dma_engine_mask=bits(en), remote_sem=T.sem[sem], src=NF, dst=T.lf[:, x:x + C])]
-            else:
-                tr = [RemoteDMATransfer(dst_ids=d, dma_engine_mask=bits(ea), remote_sem=T.sem[sem], src=NU, dst=T.lu[:, x:x + C]),
-                      RemoteDMATransfer(dst_ids=d, dma_engine_mask=bits(eb), remote_sem=T.sem[sem], src=NF, dst=T.lf[:, x:x + C])]
-            g.remote_dma_fused(tr, local_sem=T.sem.sent)
-            sent[0] += k
-        op("g", 300.0, [k_("nf%d" % t)] + ([] if last else [k_("nu%d" % t)]), ["lf%d%s" % (t + 1, c), "lu%d%s" % (t + 1, c)], send,
-           sig=(sem, len(common(src))), fin=EST["hop"], name=k_("send"))
+            g.remote_dma(dst, src, T.sem[sem], T.sem.sent, pid, rid, bits(en))
+            sent[0] += len(en)
+        op("g", 300.0, [k_("nu%d" % t)], ["lu%d%s" % (t + 1, c)], send, sig=(sem, len(common(frm))), fin=EST["hop"], name=k_("send"))
 
-        v(t0, [k_("us"), k_("oa")], [k_("ob")], lambda: V.tensor_tensor(B("ob")[:], B("oa")[:], B("us")[:, 0::17], A.subtract))
-        v(ga_(C), [k_("ob"), k_("o6"), "bl"], [k_("ee")],
-          lambda: V.tensor_tensor(B("ee")[:], B("ob")[:, 0:8].indirect(T.bl[:]), B("o6")[:], A.is_equal))
-        op("t", pe_(*([256] + [8] * 15)), [k_("ee"), k_("ob"), "eye4"] + ["wt%d" % nl for nl in range(1, 16)], [k_("lo")],
-           lambda: [Pe.matmul(lo, T.eye4[:], B("ob")[:], True, False)] +
-                   [Pe.matmul(lo, T.wt[:, nl * 128:(nl + 1) * 128], B("ee")[:, nl::16], False, nl == 15) for nl in range(1, 16)], [b1])
-        v(t0, [k_("lo"), "c8"], [k_("su")], lambda: V.tensor_scalar(B("su")[:, 0::2], lo, 2048.0, col(8), A.add, A.min), [b1])
+    def writers(cs):
+        r0, n = (C if cs == "a" else 0), C * len(cs)
+        rs, ns = slice(r0, r0 + n), slice(r0 // 16, (r0 + n) // 16)
+        k_ = lambda x: [x + c for c in cs]
+        p7 = T.ps7
+        x2, obp, lo = p7[:, 0:n], p7[:, 256:256 + n // 16], p7[:, 272:272 + n // 16]
+        mm(k_("of") + k_("ov") + ["eye", "wo"], ["obp"], 7,
+           [[(obp, T.eye[:], T.of[:, ns], 8)] + [(obp, sel("wo", nl), T.ov[:, r0 + nl:r0 + n:16], 8) for nl in range(16)]], name="obp" + cs)
+        lin("s", 8, ["obp"], k_("ob"), T.ob[:, ns], obp, 16 * WO, [7])
+        mm(k_("ob") + k_("po") + ["eye", "nblk", "tri"], ["x2"], 7,
+           [[(x2, T.nblk[:], T.po[:, rs], n), (x2, T.eye[:], T.tri[:, 0:n], n)] + [(p7[:, nl:n:16], T.eye[:], T.ob[:, ns], 8) for nl in range(1, 16)]], name="x2" + cs)
+        v(n, ["x2"], k_("ee"), ts(T.ee[:, rs], x2, 0.0, B, A.is_equal, A.mult), [7])
+        mm(k_("ee") + k_("ob") + ["eye", "w1"], ["lo"], 7,
+           [[(lo, T.eye[:], T.ob[:, ns], 8)] + [(lo, sel("w1", nl), T.ee[:, r0 + nl:r0 + n:16], 8) for nl in range(1, 16)]], name="lo" + cs)
+        v(8, ["lo", "c8"], k_("su"), ts(T.su[:, r0 // 8:(r0 + n) // 8:2], lo, 2048.0, col(8), A.add, A.min), [7])
 
-    v(t0, [], ["wt0"], lambda: V.memset(T.wt[:, 0:128], 0.0))
     for t in range(RO):
-        ph[0] = 20.0 * t
-        half(t, 0)
-        half(t, 1)
+        ph[0] = t
         for c in "ab":
-            for nh in range(7, -1, -1):
-                x = slice(nh * 16, nh * 16 + 16)
-                v(55.0 + 16 * EST["sc"] * EST["cy"], ["su" + c, "ji" + c, "fr" + c], TT,
-                  lambda c=c, nh=nh, x=x: V.tensor_tensor(T.tt[:, 0:W + 16].indirect(T["su" + c][:, 2 * nh:2 * nh + 1]),
-                                                          T["ji" + c][:, x], T["fr" + c][:, x], A.add), name="sc" + c)
+            half(t, c)
+            if not CFG["whole"]:
+                writers(c)
+        if CFG["whole"]:
+            writers("ba")
+        for nh in range(15, -1, -1):
+            c = "ba"[nh // 8]
+            op("v", 55.0 + 16 * EST["sc"] * EST["cy"], ["su" + c, "ju" + c], ["K", "Kx"],
+               lambda nh=nh: V.tensor_copy(T.ck[:, K0:K0 + W + 16].indirect(T.su[:, 2 * nh:2 * nh + 1]), T.ju[:, nh * 16:nh * 16 + 16]),
+               name="sc" + c, free=[] if CFG["waw"] or nh == 15 else ["K", "Kx"])
 
-    ph[0] = 20.0 * RO
-    for b in range(6):
-        v(vt_(512), TT, ["rk%d" % b], lambda b=b: V.tensor_scalar(T.rk[:, b * 512:(b + 1) * 512], T.tt[:, b * 512:(b + 1) * 512], M, -M, A.add, A.add))
-    for b in range(2):
-        x, y = slice(b * 512, (b + 1) * 512), slice((b + 2) * 512, (b + 3) * 512)
-        op("s", vt_(512) + 30, TT, ["js%da" % b], lambda b=b, x=x: Sc.activation(T.jsa[:, x], T.tt[:, (b + 6) * 512:(b + 7) * 512], F.Identity, bias=M), name="ra")
-        op("s", vt_(512) + 30, ["js%da" % b], ["js%da" % (b + 2)], lambda x=x, y=y: Sc.activation(T.jsa[:, y], T.jsa[:, x], F.Identity, bias=-M), name="rb")
-    steps = [(0, T.eye, T.rk[:, 0:512]), (1, T.eye, T.rk[:, 512:1024]), (6, T.eye4, T.jsa[:, 1024:1536]), (2, T.eye, T.rk[:, 1024:1536]),
-             (3, T.eye, T.rk[:, 1536:2048]), (7, T.eye4, T.jsa[:, 1536:2048]), (4, T.eye, T.rk[:, 2048:2560]), (5, T.eye, T.rk[:, 2560:3072])]
-    for i, (b, e, x) in enumerate(steps):
-        op("t", pe_(512 if b < 6 else 2048), ["rk%d" % b if b < 6 else "js%da" % (b - 4), "eye", "eye4"], ["pd0"],
-           lambda i=i, e=e, x=x: Pe.matmul(T.ps0[:], e[:], x, i == 0, i == 7), [0], name="fold")
-        ops[-1]["acc"] = i > 0
-    op("s", vt_(512), ["pd0"], ["ok"], lambda: Sc.activation(T.ok[:], T.ps0[:], F.Identity, bias=8 * 2048.0 - 4.0), [0])
-    dma("s", T.yk[:], T.ok[:], ["ok"], ["yk"], "st0", 2500.0)
-    for h in range(2):
-        c = "ba"[h]
-        x = RO * R + h * C
-        v(t1, ["lf6" + c], ["op" + c], lambda h=h, x=x: V.tensor_scalar(T.op[:, h * C:(h + 1) * C], T.lf[:, x:x + C], 2048.0, None, A.add))
-        dma("y", T.yp[:, h * C:(h + 1) * C], T.op[:, h * C:(h + 1) * C], ["op" + c], ["yp" + c], "st%d" % (1 + h), 2500.0)
+    ph[0] = RO
+    for b in range(8):
+        x = slice(b * E, (b + 1) * E)
+        lin("vs"[b % 2], E, ["K"], ["rk%d" % b], T.rk[:, x], T.ck[:, K0 + b * E:K0 + (b + 1) * E], -2048.0, name="rk")
+        mm(["rk%d" % b, "eye"], ["pd1"], 1, [[(T.ps1[:], T.eye[:], T.rk[:, x], E)]], name="fold", free=["pd1"] if b else [], opens=b == 0, closes=b == 7)
+    lin("v", E, ["pd1"], ["ok"], T.ok[:], T.ps1[:], 8 * 2048.0, [1])
+    dma(T.yk[:], T.ok[:], ["ok"], ["yk"], "st0", 2500.0)
+    for h, c in enumerate("ba"):
+        dma(T.yp[:, h * C:(h + 1) * C], T.op[:, h * C:(h + 1) * C], ["lu6" + c], ["yp" + c], "st%d" % (1 + h), 2500.0)
     return ops, sent
 
 
@@ -414,29 +401,27 @@ def order(ops):
             lw[k] = i
             rs[k] = []
         o["dep"] = d
+        o["lat"] = {j: 0.0 if ops[j]["q"] == o["q"] and k <= o["free"] else LAT for j, k in d.items()}
     succ = [[] for _ in range(n)]
     for i, o in enumerate(ops):
         for j in o["dep"]:
             succ[j].append(i)
     pr = [0.0] * n
-    key = [o["ph"] for o in ops]
+    key = [0.0] * n
     for i in range(n - 1, -1, -1):
         o = ops[i]
-        pr[i] = max(o["dur"], o["fin"]) + max([pr[s] + LAT for s in succ[i]] + [0.0])
-        if succ[i]:
-            key[i] = CFG["pri"].get(o["name"], 0.0) - pr[i] / 1000
-        if o.get("late"):
-            key[i] = 500.0 + i
+        pr[i] = max(o["dur"], o["fin"]) + max([pr[s] + ops[s]["lat"][i] for s in succ[i]] + [0.0])
+        key[i] = CFG["pri"].get(o["name"], 0.0) * 1000 + pr[i]
+        if o.get("first"):
+            key[i] = 1e9 - i
     left = [len(o["dep"]) for o in ops]
     ready = [i for i in range(n) if left[i] == 0]
-    qf, end, bank, out = {}, [0.0] * n, {}, []
+    qf, end, bank, out, dr = {}, [0.0] * n, {}, [], [0.0] * n
     while ready:
         est = {}
         for i in ready:
             o = ops[i]
-            s = qf.get(o["q"], 0.0)
-            for j in o["dep"]:
-                s = max(s, end[j] + LAT)
+            s = max(qf.get(o["q"], 0.0), dr[i])
             for b in o["banks"]:
                 for q, j in bank.get(b, {}).items():
                     if q != o["q"]:
@@ -444,7 +429,7 @@ def order(ops):
             est[i] = s
         i0 = min(ready, key=lambda i: est[i])
         cand = [i for i in ready if ops[i]["q"] == ops[i0]["q"] and est[i] <= est[i0] + CFG["win"]]
-        i = max(cand, key=lambda i: (-key[i], pr[i], -i))
+        i = max(cand, key=lambda i: (key[i], -i))
         o = ops[i]
         for b in o["banks"]:
             for q, j in bank.setdefault(b, {}).items():
@@ -458,6 +443,7 @@ def order(ops):
         ready.remove(i)
         for s in succ[i]:
             left[s] -= 1
+            dr[s] = max(dr[s], end[i] + ops[s]["lat"][i])
             if left[s] == 0:
                 ready.append(s)
     return out, max(end)
@@ -478,7 +464,7 @@ def rank_program(g, core, T, topo):
         q = o["q"]
         need = {}
         for j, toks in o["dep"].items():
-            if q == "t" and ops[j]["q"] == "t" and (o.get("acc") or o["name"][:2] == "uu") and toks <= {"pd0", "uua", "uub"}:
+            if ops[j]["q"] == q and toks and toks <= o["free"]:
                 continue
             sg = done[j]
             for s, val in ([sg[k] for k in toks if k in sg] if isinstance(sg, dict) else [sg]):

@@ -3,57 +3,64 @@ from concourse.mybir import AluOpType as A, ActivationFunctionType as F
 
 N, W, R, RO, E = 4, 4096, 256, 6, 512
 C = 128
+PARTS = "abcd"[:R // C]
 K0 = 2 * R
 B = 8192.0
 M16 = 201326592.0
-WO = 2064.0
+WO = 4160.0
+G = 64
 CFG = {
-    "vp": {"a": "3333", "b": "1111"},
-    "vp0": {"a": "1133", "b": "1133"},
-    "kg": {"a": "ss", "b": "ss"},
-    "kg0": {"a": "sv", "b": "sv"},
-    "cp": {"a": "2222", "b": "2112"},
-    "eng": {"ou": "s", "off": "s", "pf": "s", "ko": "s"},
-    "whole": False,
-    "tt16": True, "waw": True, "win": 60.0, "pri": {},
+    "vp": {"a": "2233", "b": "2322"},
+    "vp0": {"a": "2233", "b": "2322"},
+    "kg": {"a": "ssvv", "b": "ssss"},
+    "kg0": {"a": "ssvv", "b": "ssss"},
+    "cp": {"a": "1122", "b": "2111"},
+    "eng": {"ou": "v", "off": "s", "pf": "v", "ko": "s", "ov": "v", "ex": "s"},
+    "opt": {"dk": 0, "or": 0, "ofr": 0, "m1": 1, "fine": 0, "jf": 0},
+    "hop": 1800.0,
+    "order": "pena poa kg1a kg3a ola ora x2a eqa kg0a oua kg2a ppa koa js1a ofa vg1b vg0b df2a kpa cb2a cb1a ab0b vg3b df3a kg1b pd1b cb0a cb3a pfb vg2b uu0a ab1b uu1a uu2a uu3a ab3b js0a dk0b js2a ab2b ova js3a js1b zza kg2b aca dk1b vaa pxa yba ksb ofra wra ktb obpa exa js2b offa kub jua wwa kg0b xfa ppb pob nua eea kg3b orb senda olb oub eqb loa kob js3b x2b js0b kpb lsa df0b cb1b cb0b cb2b ofb +vg3a cb3b uu0b uu1b uu2b +vg1a penb uu3b +vg2a +pd3a ovb sua acb zzb +ab3a obpb vab +vg0a pxb +ab1a ybb ofrb wrb eeb +pd2a exb jub offb +ab0a wwb xfb +ab2a +pfa lob nub +dk0a sc0a sendb lsb +dk1a sc1a sub +ksa sc0b +kta +kua sc1b",
+    "first": "sj ncn pi4 c3 c4 yx0_15 c0 yx0_13 yx0_0 yx0_2 yx0_8 pi2 sd yx0_11 eye c1 yx0_3 blk yx0_9 yx0_7 w1 yx0_6 lu0a w16 yx0_1 c5 ex0 wo w2 kc yx0_5 neye c9 t1 t2 tm yx1_0 yx1_1 yx1_2 yx1_3 yx1_4 yx1_5 yx1_6 yx1_7 yx1_8 yx1_9 yx1_10 yx1_11 yx1_12 yx1_13 yx1_14 yx1_15 yx0_14 yx0_4 e1 pfb c2 yx0_10 pfa pe yx0_12 n15 c10 c8 bca vg2a vg3a pd2a vg1a vg1b ppb pd3a vg0a ab2a tri vg2b ab1a pd1b ab3a vg3b ab0a dk1a spr1 vg0b ab1b dk0a ab2b ksa ab3b kta k3 ab0b kua dk1b poa c6 wob kg1a kg3a ora dk0b k2 kg0a oua kg2a ola koa ksb js3a kg1b js2a kpa df2a Kx cb0a x2a ofa ncr cb2a ktb cb1a uu0a kg2b kub df3a nsh k4 eqa uu1a pob c7 uu2a cb3a bcb js2b kg0b ish uu3a js1a orb ova czr ppa js0a olb kg3b nis obpa oub aca zza dh eqb kob eea pena ofb kpb df0b jua vaa penb cb2b x2b eye4 cb0b pxa cb1b yba ofra spr0 exa cb3b uu0b uu1b offa wra uu2b k1 js0b uu3b js1b wwa xfa ovb loa sk nua zzb js3b obpb senda vab jub acb lsa ofrb eeb pxb offb exb lob xfb ybb sua lsb sc0a wrb sub wwb sc1a sc0b nub sc1b sendb",
+    "last": "ypb ypa pena poa kg2a kg0a ora ppa vg1b oua vg0b koa kg3a kg1a pd1b kpa x2a vg2b ofa ab1b df2a ab0b ola vg3b cb2a dk0b cb0a ab2b df3a js1a ab3b cb1a uu0a cb3a js2a dk1b eqa kg1b js0a uu1a uu2a ksb uu3a pfb kg0b ktb ova kub js3a zza pob obpa kg2b vaa ppb orb eea olb kg3b ofra oub aca eqb js1b kob yba js2b jua pxa js0b kpb df0b wra cb1b x2b cb0b loa cb2b ofb exa cb3b penb uu0b offa uu1b uu2b js3b lsa uu3b jub acb ovb pxb zzb exb obpb vab sua xfa ofrb eeb offb xfb lob ybb sc0a wwa lsb wrb sc1a wwb sub nua sc0b senda sc1b nub rk sendb fold ok yk",
 }
+CFG.update({'vp': {'a': '1233', 'b': '2322'}, 'vp0': {'a': '2233', 'b': '2232'}, 'kg': {'a': 'ssvs', 'b': 'ssvs'}, 'kg0': {'a': 'ssvv', 'b': 'svss'}, 'cp': {'a': '1212', 'b': '2111'}, 'eng': {'ou': 's', 'off': 'v', 'pf': 'v', 'ko': 's', 'ov': 'v', 'ex': 's'},
+"order": "dk0a kg1a kg2a kg3a ksa pfa kta js2a kg0a kua poa vg0b vg1b ora x2a vg3b oua ola ofa pena koa vg2b ab0b kpa df1a ab3b pd1b cb0a cb1a cb2a ab1b uu0a df3a eqa pfb ab2b js0a uu1a kg2b uu2a dk0b cb3a dk1b kg3b js1a uu3a js3a ppa ppb ksb ova kg0b ktb js2b zza kub obpa aca vaa kg1b pob pxa yba eea orb jua wra olb ofra exa oub eqb ofb js0b wwa kob offa js3b xfa kpb df0b cb1b x2b cb0b loa nua cb2b penb senda uu0b cb3b uu1b uu2b js1b uu3b jub ovb acb lsa zzb obpb vab sua pxb ofrb eeb exb ybb offb wrb lob xfb +vg3a wwb sc0a lsb +vg2a nub sc1a +pd3a sendb +vg0a +pd2a +ab3a sub +vg1a +ab2a sc0b +ab1a +ab0a +dk1a sc1b",
+"first": "sj qg iq qm ncn pi0 kc yx0_1 ys1 ys2 sd yx0_13 yx0_15 yx0_8 yx0_12 pi2 yx0_14 yx0_6 yx0_9 yx0_11 yx0_2 lu0a yx0_4 yx0_7 c0 yx0_5 bca pi4 c1 yx0_3 eye yx0_10 tri c2 c3 n15 yx0_0 neye c5 c4 w1 c9 blk wo vg2a vg0a vg0b vg3a pd2a vg1a w16 ab0a t1 t2 tm yx1_0 yx1_11 pd3a yx1_6 vg1b ab2a yx1_7 ab3a vg3b ab1a yx1_15 dk1a vg2b yx1_1 e1 c10 dk0a yx1_5 ab0b pd2b yx1_13 ab3b ksa pfa ab2b ex0 yx1_14 pe kta ab1b k3 pfb dk1b nsh kua bcb kg0a yx1_9 dk0b poa kg3a ppa yx1_12 w2 ora c7 c8 kg1a yx1_8 ola x2a kg2a ppb yx1_2 ofa oua spr1 js3a kg3b yx1_10 ksb js2a k2 yx1_3 ktb js0a koa js1a c6 kg2b yx1_4 kg1b df1a kpa cb1a eqa kub cb0a kg0b df3a Kx pob k1 cb2a cb3a orb js2b olb uu0a aca uu1a oub czr js1b uu2a uu3a dh kob js0b wob ish eye4 kpb spr0 df0b pena ova sk ofb cb2b zza obpa cb0b k4 nis ncr vaa penb cb1b uu0b jua pxa ofra cb3b yba uu1b offa uu2b eqb wra eea exa uu3b wwa xfa ovb loa nua zzb js3b x2b lsa senda vab obpb jub acb sua pxb ofrb eeb exb offb xfb lob ybb sc0a lsb wrb sc1a wwb sub sc0b nub sc1b sendb",
+"last": "ypa ypb dk0a kg3a kg2a pfa kg1a ksa kta kg0a kua vg3b vg1b poa vg0b ora ab3b ola ppa pd1b vg2b oua ab0b x2a koa eqa js1a ab1b pfb js3a kpa df1a js2a ab2b cb0a dk0b cb1a ppb dk1b js0a ofa cb2a kg0b df3a ksb uu0a uu1a cb3a ktb uu2a kub kg1b uu3a pob aca ova orb kg3b kg2b zza olb obpa oub vaa pena js1b kob eqb eea penb pxa kpb df0b cb1b ofra cb0b x2b cb2b ofb loa exa cb3b jua uu0b uu1b js3b uu2b offa uu3b lsa js2b ovb js0b sua zzb obpb acb vab pxb ofrb eeb exb jub ybb offb xfa xfb lob wrb yba sc0a wwb lsb wra sc1a wwa sub nub sc0b sendb nua sc1b senda rk fold ok yk"})
+CFG.update({'vp': {'a': '2233', 'b': '2322'}, 'vp0': {'a': '2232', 'b': '2332'}, 'kg': {'a': 'ssvs', 'b': 'ssvs'}, 'kg0': {'a': 'ssvv', 'b': 'svss'}, 'cp': {'a': '1212', 'b': '2111'}, 'eng': {'ou': 's', 'off': 's', 'pf': 'v', 'ko': 's', 'ov': 'v', 'ex': 's'}, 'opt': {'dk': 0, 'or': 0, 'ofr': 0, 'm1': 0, 'fine': 0, 'jf': 0}, 'order': 'dk1a pfa vg1b kg2a dk0a kg1a ksa pd1b pfb kta js2a kg0a ppa kua poa vg3b kg3a ora x2a vg0b oua ofa koa ab3b js0a df1a vg2b ab1b kpa cb1a cb0a ab0b cb2a df3a ab2b uu0a kg2b dk0b cb3a ola dk1b pena eqa uu1a js3a kg3b uu2a ksb uu3a js1a ppb ktb ova kg1b kub js2b zza pob obpa aca kg0b vaa orb eea pxa olb ofra oub exa eqb ofb js0b kob js3b offa jua kpb df0b xfa cb2b yba x2b cb0b cb1b loa penb b0a cb3b uu0b uu1b uu2b m1a uu3b nua ovb senda js1b lsa zzb obpb acb vab pxb ofrb eeb exb b0b offb ybb lob xfb +vg3a sua m1b sc0a jub nub +vg2a lsb +pd2b +pd3a sc1a sendb +vg1a +ab3a +pd2a sub +vg0a +ab1a +ab2a sc0b +ab0a sc1b', 'first': 'pi0 iq c0 sj ncn yx0_7 yx0_14 yx0_3 bca qm yx0_1 yx0_4 yx0_6 qg pi2 eye kc yx0_5 ys1 ys2 yx0_10 yx0_11 yx0_0 lu0a pi4 c3 yx0_13 yx0_9 c4 yx0_12 n15 c1 sd yx0_15 c5 tri yx0_8 neye pfa c7 c2 yx0_2 blk w1 vg3a vg1b vg1a w16 t1 t2 tm yx1_0 yx1_1 yx1_2 yx1_3 yx1_4 yx1_5 yx1_6 yx1_7 yx1_8 yx1_9 yx1_10 yx1_11 yx1_12 yx1_13 yx1_14 yx1_15 pd1b ab3a vg0a vg2a vg0b ab1a pd2a ab0a vg3b ab2a c10 ab1b c9 dk1a c8 vg2b dk0a ppa w2 ab3b ksa pd2b k3 e1 pfb k2 ab0b kta nsh ex0 ab2b kua dk0b kg3a kg1a dk1b poa ppb kg0a k4 ksb kg2a ola ora x2a wo oua kg1b kg3b eqa koa js3a kg2b ktb ish df1a js2a kpa kub bcb spr1 cb1a pob cb0a kg0b df3a Kx cb2a orb ofa cb3a js1a uu0a uu1a js0a oub pe olb wob uu2a dh kob uu3a js0b czr js2b c6 kpb k1 df0b ova ncr aca jua eqb penb zza cb1b obpa ofb cb0b vaa cb2b pena ofra cb3b pxa uu0b offa uu1b exa eea uu2b spr0 uu3b yba xfa b0a ovb x2b js1b m1a zzb js3b obpb nua vab loa jub sk senda acb eeb ofrb ybb pxb lsa offb exb sua lob xfb b0b lsb sc0a sub m1b sc1a nub sc0b sendb sc1b', 'last': 'ypa ypb dk1a vg3b vg1b dk0a kg3a ksa pfa pd1b kta kg2a kg1a ppa kua kg0a poa vg0b ola ora ab3b x2a js2a oua ab1b eqa vg2b koa ab0b pfb js1a df1a ab2b js3a kpa dk0b cb0a cb1a dk1b ofa cb2a kg0b ppb df3a ksb uu0a js0a uu1a cb3a ktb uu2a kub kg1b pob uu3a olb ova orb kg3b kg2b zza obpa oub vaa pena eqb aca kob ofra eea kpb pxa df0b cb1b exa loa ofb cb0b cb2b penb cb3b offa uu0b uu1b uu2b js1b js0b uu3b x2b js3b ovb js2b xfa zzb obpb jub acb jua vab lsa pxb ofrb eeb exb yba ybb sua offb b0a xfb lob m1a b0b sc0a lsb sc1a sub nua sc0b senda m1b sc1b nub rk sendb fold ok yk'})
+CFG.update({'vp': {'a': '2233', 'b': '2322'}, 'vp0': {'a': '2232', 'b': '2332'}, 'kg': {'a': 'ssvs', 'b': 'ssvs'}, 'kg0': {'a': 'ssvs', 'b': 'sssv'}, 'cp': {'a': '1212', 'b': '2111'}, 'eng': {'ou': 's', 'off': 's', 'pf': 'v', 'ko': 's', 'ov': 'v', 'ex': 's'}, 'opt': {'dk': 0, 'or': 0, 'ofr': 0, 'm1': 0, 'fine': 0, 'jf': 0, 'py': 1, 'obs': 1}, 'order': 'vg1b pfa pfb dk0a kg2a kg0a pd1b ksa kta js2a kg1a kua poa kg3a js0a vg3b ora ppb x2a oua ola vg2b koa ab3b df1a vg0b ab1b kpa cb1a cb0a ab0b cb2a df3a ab2b eqa dk0b js1a cb3a kg2b dk1b pena uu0a kg0b uu1a ksb uu2a js3a ppa uu3a ktb kg3b kub ova pob zza js2b obpa kg1b aca orb vaa js0b pxa olb obsa ofra js3b oub exa eqb kob eea offa jua kpb b0a xfa df0b cb1b x2b cb0b yba cb2b penb cb3b uu0b uu1b m1a uu2b js1b uu3b nua loa ovb senda acb lsa zzb pxb obpb vab exb sua jub obsb ofrb eeb b0b ybb offb xfb +vg3a lob m1b sc0a +vg2a nub +vg1a +pd3a sendb +ab3a lsb +pd2a sc1a sub +ab1a +vg0a +ab2a sc0b +ab0a +dk1a sc1b', 'first': 'pi0 sj iq ncn yx0_2 ys1 ys2 yx0_7 yx0_10 yx0_8 pi4 c3 yx0_5 pi2 bca c4 c0 yx0_3 yx0_1 yx0_13 qg c1 yx0_11 yx0_0 qm c8 yx0_12 eye tri yx0_9 lu0a kc w1 c7 n15 pfa yx0_15 w16 yx0_6 c5 ppa yx0_14 neye yx0_4 blk t1 t2 tm yx1_0 yx1_1 yx1_2 yx1_3 yx1_4 yx1_5 yx1_6 yx1_7 yx1_8 yx1_9 yx1_10 yx1_11 yx1_12 yx1_13 yx1_14 yx1_15 sd vg1a vg1b vg3b vg2a pd1b vg0a vg2b pd2a vg3a ab1a ab0a ex0 ab2a vg0b dk0a ab3a ab1b c9 msk dk1a c10 ab3b pd2b ab0b w2 msk7 msk0 dk0b ab2b c2 ksa k2 e1 nsh msk1 kg1a kta kg2a dk1b kg0a kua ish poa bcb kg3a ora pfb ksb ola ktb msk5 js2a oua kub wo koa pob msk4 msk6 kg3b msk3 kg2b kpa df1a orb k4 cb1a ppb cb0a oub eqa msk2 kg0b cb2a uu0a df3a js3a olb x2a kob js0a uu1a cb3a js0b uu2a eqb js2b kg1b js1a kpb uu3a Kx k1 aca ova czr sk spr1 pe df0b cb1b c6 dh wob zza pena js1b cb0b obpa vaa cb2b b0a pxa ncr jua uu0b exa obsa penb cb3b uu1b ofra spr0 eea uu2b uu3b offa yba js3b ovb x2b xfa jub acb zzb obpb m1a loa vab obsb nua ofrb eeb senda pxb offb lsa exb lob sua xfb ybb b0b lsb sc0a m1b sub sc1a nub sc0b sendb sc1b', 'last': 'ypa ypb vg1b vg3b dk0a kg3a ksa pfa kta kg0a kua poa vg0b kg1a ora pd1b kg2a oua ppa x2a ab3b ola koa pfb vg2b ab1b kpa df1a ab0b js2a js1a ab2b cb0a dk0b cb1a cb2a dk1b kg0b df3a ksb js0a ppb uu0a js3a uu1a cb3a uu2a ktb eqa kg3b kub uu3a pob aca ova kg1b olb kg2b orb obpa zza oub obsa eqb vaa kob eea pena kpb df0b cb1b loa cb0b x2b cb2b penb cb3b jua uu0b pxa uu1b uu2b js3b exa js1b uu3b ofra js0b ovb js2b offa zzb obpb jub acb vab obsb pxb xfa ofrb lsa exb eeb b0a yba offb ybb sua xfb lob m1a b0b sc0a lsb sc1a sub nua sc0b m1b sc1b nub rk sendb senda fold ok yk'})
 
-CFG.update({'vp': {'a': '3322', 'b': '2323'}, 'vp0': {'a': '2233', 'b': '2223'}, 'kg': {'a': 'sv', 'b': 'ss'}, 'kg0': {'a': 'sv', 'b': 'ss'}, 'cp': {'a': '1111', 'b': '1121'}, 'eng': {'ou': 's', 'off': 's', 'pf': 'v', 'ko': 's'}, 'whole': False, 'tt16': True, 'waw': True, 'win': 60.0, 'pri': {'vga': 2.0, 'oba': 8.0, 'penb': -1.5, 'offa': 21.0, 'scb': 4.0, 'cbb': 9.5, 'eea': 16.5, 'vab': -19.5, 'ktb': -8.0, 'obb': 14.5, 'eqa': 10.5, 'vaa': -9.5, 'nua': -20.0, 'kob': 1.0, 'aca': -4.5, 'exa': 15.0, 'ova': -19.5, 'sendb': -10.5, 'ybb': -5.5, 'xfa': 28.5, 'ola': -1.0, 'eeb': 6.5, 'x2a': 14.5, 'ofra': -3.0, 'kpb': 19.5, 'jsa': -13.0, 'cba': -1.0, 'eqb': 6.0, 'sub': 17.5, 'acb': 40.0, 'ofrb': 6.0, 'orb': 10.0, 'zza': -2.0, 'ppb': -9.0, 'pdb': -11.5, 'poa': -4.0, 'exb': -11.5, 'ksb': 23.5, 'koa': 21.0, 'pfa': -2.0, 'oub': 9.5, 'jub': -2.5, 'm1b': 6.0, 'sua': 5.0, 'm1a': -1.0, 'ovb': -31.5, 'kta': 6.0, 'pxa': 1.5, 'xfb': 27.0, 'kub': 13.0, 'uua': 3.5, 'jsb': -19.5, 'ppa': -11.5, 'senda': 16.5, 'lob': -29.0, 'kpa': 12.0, 'pfb': -6.0, 'kgb': -1.0, 'kua': -0.5, 'ksa': 4.0, 'x2b': -5.0, 'jua': -7.0, 'pob': -2.5, 'ofb': -22.5, 'pxb': 5.5, 'offb': -1.5, 'dka': 11.5, 'pena': -2.0, 'olb': 11.5, 'nub': 4.5, 'dfb': 7.5, 'zzb': 13.0, 'aba': 2.5, 'ora': 6.0, 'uub': -2.5, 'abb': 3.0, 'yba': 3.0, 'b0b': 10.0, 'dkb': 2.5, 'vgb': 2.0, 'b0a': -1.0, 'loa': -1.5, 'obpb': 1.0, 'kga': 2.0, 'oua': 1.0, 'obpa': -2.5}})
 S, P = "sbuf", "psum"
 SCRATCH = {
-    "vt": (S, [128, W], "bfloat16"), "ck": (S, [128, K0 + W + 16], "int32"),
+    "vt": (S, [128, W], "bfloat16"), "ck": (S, [128, K0 + W + G], "int32"),
     "nm": (S, [128, R], "int32"), "ys": (S, [128, 4 * R], "bfloat16"), "yx": (S, [128, 4 * W], "bfloat16"),
     "lu": (S, [128, RO * R], "uint16"), "nu": (S, [128, RO * R], "uint16"), "nf": (S, [128, R], "float32"), "op": (S, [128, R], "float32"),
-    "iq": (S, [128, R], "float32"), "qm": (S, [128, R], "float32"), "qg": (S, [128, 128], "float32"),
+    "iq": (S, [128, R], "float32"), "qm": (S, [128, 128], "float32"), "qg": (S, [128, 128], "float32"),
     "pi": (S, [128, 8], "int32"), "col": (S, [128, 16], "float32"),
-    "kc": (S, [128, 64], "bfloat16"), "sd": (S, [128, 128], "float32"), "sj": (S, [128, 1024], "bfloat16"),
+    "kc": (S, [128, 128], "bfloat16"), "sd": (S, [128, 128], "float32"), "sj": (S, [128, 2048], "bfloat16"),
     "e1": (S, [128, 32], "bfloat16"), "pe": (S, [128, 32], "bfloat16"), "ncn": (S, [128, R], "float16"), "ncr": (S, [128, 16], "float16"),
-    "tri": (S, [128, R], "bfloat16"),
-    "pf": (S, [128, R], "float16"), "ks": (S, [128, R], "float32"), "kt": (S, [128, 16], "float32"), "kw": (S, [128, 16], "float32"),
-    "ku": (S, [128, 16], "uint16"), "ou": (S, [128, 16], "uint16"), "of": (S, [128, 16], "float16"), "ob": (S, [128, 16], "float16"),
-    "off": (S, [128, 16], "uint16"), "su": (S, [128, 32], "uint16"),
+    "msk": (S, [128, 320], "bfloat16"), "obs": (S, [128, R], "float32"), "tri": (S, [128, 16], "bfloat16"), "eye4": (S, [128, 128], "float32"), "spr": (S, [128, 8], "float32"),
+    "sk": (S, [128, 128], "bfloat16"), "ls": (S, [128, R], "float32"), "k3": (S, [128, 8], "bfloat16"),
+    "pf": (S, [128, R], "float16"), "ks": (S, [128, R], "float32"), "kt": (S, [128, 16], "float32"),
+    "osn": (S, [128, R], "float16"), "fs": (S, [128, R], "float16"), "wr": (S, [128, R], "float32"),
+    "ku": (S, [128, 16], "uint16"), "ou": (S, [128, 16], "uint16"), "off": (S, [128, 16], "uint16"), "su": (S, [128, 16], "uint16"),
     "po": (S, [128, R], "float16"), "pen": (S, [128, R], "bfloat16"), "ko": (S, [128, R], "float16"), "eq": (S, [128, R], "bfloat16"),
     "ov": (S, [128, R], "bfloat16"), "va": (S, [128, R], "float16"), "xf": (S, [128, R], "float32"), "m1": (S, [128, R], "float32"),
-    "ac": (S, [128, R], "float16"), "ju": (S, [128, R], "float32"), "ee": (S, [128, R], "bfloat16"),
+    "ac": (S, [128, R], "float16"), "ju": (S, [128, R], "float32"), "ee": (S, [128, 640], "bfloat16"),
+    "vq": (S, [128, W], "bfloat16"), "vx": (S, [128, 16, 256], "bfloat16"), "ab": (S, [128, 16, 16, 16], "bfloat16"),
+    "kg": (S, [128, W], "float16"), "js": (S, [128, W], "float16"), "cb": (S, [128, W], "bfloat16"), "bc": (S, [128, 4], "float32"),
     "rk": (S, [128, W], "float16"), "ok": (S, [128, E], "float32"),
 }
-for _n in ("eye", "neye", "n15", "blk", "nblk", "ish", "nsh", "t1", "t2", "tm", "czr", "k1", "k2"):
+for _n in ("eye", "neye", "n15", "blk", "ish", "nsh", "t1", "t2", "tm", "czr", "k1", "k2", "dg", "nis", "wob", "dh", "k4"):
     SCRATCH[_n] = (S, [128, 128], "bfloat16")
 for _n in ("w1", "w2", "w16", "wo"):
     SCRATCH[_n] = (S, [128, 144], "bfloat16")
-for _c in "ab":
-    SCRATCH.update({
-        "vx" + _c: (S, [128, 8, 16, 16], "bfloat16"), "vq" + _c: (S, [128, 2048], "bfloat16"), "ab" + _c: (S, [128, 8, 16, 16], "bfloat16"),
-        "kg" + _c: (S, [128, 2048], "float16"), "js" + _c: (S, [128, 2048], "float16"), "cb" + _c: (S, [128, 2048], "bfloat16"),
-        "bc" + _c: (S, [128, 1], "float32"),
-    })
 for _b in range(8):
     SCRATCH["ps%d" % _b] = (P, [128, 512], "float32")
 
-SEMAPHORES = (["cv", "cs", "ct", "cg", "sent", "l_nm", "l_ys", "l_v", "l_k", "st0", "st1", "st2", "y1", "y2", "y3"]
-              + ["ar%d%s" % (t, c) for t in range(1, 7) for c in "ab"])
+SEMAPHORES = (["cv", "cs", "ct", "cg", "sent", "l_nm", "l_ys", "l_v", "l_k", "st", "y1", "y2", "y3"]
+              + ["st" + c for c in PARTS] + ["ar%d%s" % (t, c) for t in range(1, 7) for c in PARTS])
 
-EST = {"cy": 0.83, "g": 1.56, "sc": 3.8, "lat": 100.0, "v": 30.0, "s": 60.0, "pe": 0.42, "hop": 2800.0, "lv": 5500.0, "lk": 11500.0}
+EST = {"cy": 0.83, "g": 1.56, "sc": 3.8, "lat": 240.0, "v": 15.0, "s": 20.0, "pe": 0.33, "pf": 0.0, "lv": 5500.0, "lk": 11500.0}
 
 
 def vt_(n):
@@ -69,7 +76,7 @@ def ga_(n, q):
 
 
 def pe_(*ns):
-    return sum(10.0 + max(64, n) * EST["pe"] for n in ns)
+    return sum(EST["pf"] + max(64, n) * EST["pe"] for n in ns)
 
 
 def bits(engines):
@@ -85,6 +92,8 @@ def build(g, core, T, topo):
     ops = []
     ph = [-1]
     V, Sc, Pe = g.vector, g.scalar, g.tensor
+    O, eng = CFG["opt"], CFG["eng"]
+    first = {c: R - C * (i + 1) for i, c in enumerate(PARTS)}
 
     def op(q, dur, rd, wr, fn, banks=(), sig=None, fin=0.0, name=None, free=()):
         ops.append({"q": q, "dur": dur, "rd": list(rd), "wr": list(wr), "fn": fn, "banks": tuple(banks), "sig": sig, "fin": fin,
@@ -100,6 +109,7 @@ def build(g, core, T, topo):
         def fn():
             return [Pe.matmul(o, l, r, opens and i == 0, closes and i == len(grp) - 1) for grp in groups for i, (o, l, r, _) in enumerate(grp)]
         op("t", pe_(*[x[3] for grp in groups for x in grp]), rd, wr, fn, [bank], name=name, free=free)
+        ops[-1]["n"] = sum(len(grp) for grp in groups)
 
     def lin(q, n, rd, wr, out, in_, add, banks=(), name=None, half=False):
         if q == "v":
@@ -118,12 +128,11 @@ def build(g, core, T, topo):
 
     sent = [0]
 
-    dma(T.ys[:, 0:R], T.seen[:], [], ["ys0", "q"], "l_ys", 2000.0)
-    dma(T.nm[:], T.nam[:], [], ["nm", "q"], "l_nm", 2200.0)
-    dma(T.vt[:], T.val[:], [], ["vt", "q"], "l_v", EST["lv"])
-    dma(T.ck[:, K0:K0 + W], T.clk[:], [], ["K", "q"], "l_k", EST["lk"])
+    dma(T.ys[:, 0:R], T.seen[:], [], ["ys0"], "l_ys", 2000.0)
+    dma(T.nm[:], T.nam[:], [], ["nm"], "l_nm", 2200.0)
+    dma(T.vt[:], T.val[:], [], ["vt"], "l_v", EST["lv"])
+    dma(T.ck[:, K0:K0 + W], T.clk[:], [], ["K"], "l_k", EST["lk"])
     for o in ops:
-        o["wr"].remove("q")
         o["first"] = True
 
     def common(src):
@@ -134,34 +143,36 @@ def build(g, core, T, topo):
                 en = e if en is None else [x for x in en if x in e]
         return en
 
-    def send_y():
-        en = common(core)
-        k = len(en) // 4
+    def send_y(js):
+        en = common(core) if len(js) > 1 else topo.engines(core, cores[(rank + js[0]) % N])
+        k = len(en) // len(js)
         tr = []
-        for j in range(1, N):
+        for i, j in enumerate(js):
             d = cores[(rank + j) % N]
             assert topo.may_write(core, d)
             rid, pid, _ = topo.addr(d)
-            tr.append(RemoteDMATransfer(dst_ids=[DstId(rid=rid, pnc=pid)], dma_engine_mask=bits(en[(j - 1) * k:j * k]),
+            tr.append(RemoteDMATransfer(dst_ids=[DstId(rid=rid, pnc=pid)], dma_engine_mask=bits(en[i * k:(i + 1) * k]),
                                         remote_sem=T.sem["y%d" % j], src=T.ys[:, 0:R], dst=T.ys[:, j * R:(j + 1) * R]))
         g.remote_dma_fused(tr, local_sem=T.sem.sent)
-        sent[0] += k * (N - 1)
-    op("g", 1500.0, ["ys0"], ["ys1", "ys2", "ys3"], send_y,
-       sig={"ys%d" % j: ("y%d" % j, len(common(cores[(rank - j) % N])) // 4) for j in range(1, N)}, fin=5000.0)
+        sent[0] += k * len(js)
+    for js in ([1], [2, 3]):
+        op("g", 1500.0 / js[0] ** 2, ["ys0"], ["ys%d" % j for j in js], lambda js=js: send_y(js),
+           sig={"ys%d" % j: ("y%d" % j, len(common(cores[(rank - j) % N])) // 2 if j > 1 else len(topo.engines(cores[rank - 1], core))) for j in js}, fin=5000.0)
 
     flag = {"allow_small_or_imprecise_dtypes": True}
     op("g", 140.0, [], ["pi0"], lambda: g.iota(T.pi[:, 0:2], [[1, 2]], 0, 1))
     op("g", 560.0, [], ["iq"], lambda: g.iota(T.iq[:], [[1, R]], 0, 0, **flag))
-    op("g", 560.0, [], ["qm"], lambda: g.iota(T.qm[:], [[0, 16], [1, 16]], 0, 0, **flag))
+    op("g", 350.0, [], ["qm"], lambda: g.iota(T.qm[:], [[0, 8], [1, 16]], 0, 0, **flag))
     op("g", 350.0, [], ["qg"], lambda: g.iota(T.qg[:], [[16, 8], [0, 16]], 0, 0, **flag))
     col = lambda i: T.col[:, i:i + 1]
+    sg, hb = (1.0, 0.5) if eng["ov"] == "s" else (0.0, 1.0)
     v(1, ["pi0"], ["pi2"], lambda: V.tensor_scalar(T.pi[:, 2:4], T.pi[:, 0:2], 15, None, A.bitwise_and))
     v(1, ["pi0"], ["pi4"], lambda: V.tensor_scalar(T.pi[:, 4:5], T.pi[:, 0:1], 112, None, A.bitwise_and))
     v(1, ["pi0"], ["c0"], lambda: V.tensor_copy(col(0), T.pi[:, 0:1]))
     v(1, ["pi2"], ["c1"], lambda: V.tensor_copy(col(1), T.pi[:, 2:3]))
     v(1, ["pi2", "pi4"], ["c2"], lambda: V.tensor_tensor(col(2), T.pi[:, 3:4], T.pi[:, 4:5], A.add))
     v(1, ["pi4"], ["c3"], lambda: V.tensor_copy(col(3), T.pi[:, 4:5]))
-    for i, (a, b, src) in enumerate([(1.0, 15.0, 3), (1.0, 8.0, 1), (2.0, -2048.0 - K0, 1), (-B / 2, -B / 2, 1), (1.0, float(W), 1)]):
+    for i, (a, b, src) in enumerate([(1.0, 15.0, 3), (1.0, 8.0, 1), (2.0, -2048.0 - K0, 1), (-B / 2 * sg, -B * hb, 1), (1.0, float(W), 1)]):
         s(1, ["c%d" % src], ["c%d" % (4 + i)], lambda i=i, a=a, b=b, src=src: Sc.activation(col(4 + i), col(src), F.Identity, bias=b, scale=a))
     q128 = T.iq[:, 0:128]
     ts = lambda out, in_, a, b, o0, o1: (lambda: V.tensor_scalar(out, in_, a, b, o0, o1))
@@ -170,162 +181,229 @@ def build(g, core, T, topo):
     s(128, ["eye"], ["neye"], sc(T.neye[:], T.eye[:], -1.0))
     s(128, ["eye"], ["n15"], sc(T.n15[:], T.eye[:], -15.0))
     v(128, ["qg", "c3"], ["blk"], ts(T.blk[:], T.qg[:], col(3), 1.0, A.is_equal, A.mult))
-    s(128, ["blk"], ["nblk"], sc(T.nblk[:], T.blk[:], -1.0))
     v(128, ["iq", "c2"], ["nsh"], ts(T.nsh[:], q128, col(2), -1.0, A.is_equal, A.mult))
     v(256, ["eye", "nsh"], ["ish"], lambda: V.tensor_tensor(T.ish[:], T.eye[:], T.nsh[:], A.subtract))
-    s(128, ["blk"], ["t1"], sc(T.t1[:], T.blk[:], -B / 2))
+    s(128, ["blk"], ["t1"], sc(T.t1[:], T.blk[:], -B * hb))
     op("g", 390.0, ["t1"], ["t2"], lambda: g.affine_select(T.t2[:], T.t1[:], [[1, 128]], A.is_gt, 0.0, 0, -1))
-    op("g", 390.0, ["t2"], ["tm"], lambda: g.affine_select(T.tm[:], T.t2[:], [[1, 128]], A.not_equal, B / 2, 0, -1))
-    s(128, ["iq", "c7"], ["czr"], lambda: Sc.activation(T.czr[:], q128, F.Identity, bias=col(7), scale=0.0))
+    op("g", 390.0, ["t2"], ["tm"], lambda: g.affine_select(T.tm[:], T.t2[:], [[1, 128]], A.not_equal, B * hb, 0, -1))
+    s(C, ["iq", "c7"], ["czr"], lambda: Sc.activation(T.czr[:, 0:C], T.iq[:, 0:C], F.Identity, bias=col(7), scale=0.0))
     v(64, [], ["k1"], lambda: V.memset(T.k1[:], 2048.0 - 2 * B))
-    v(64, [], ["k2"], lambda: V.memset(T.k2[:], 2048.0))
     v(144, ["iq", "c4"], ["w1"], ts(T.w1[:], T.iq[:, 0:144], col(4), 1.0, A.is_equal, A.mult))
     for nme, x in (("w16", 16.0), ("w2", 2.0), ("wo", WO)):
         s(144, ["w1"], [nme], sc(T[nme][:], T.w1[:], x))
     sel = lambda w, nl: T[w][:, 15 - nl:143 - nl]
-    s(64, ["qm"], ["kc"], sc(T.kc[:], T.qm[:, 0:64], 1.0, -7.75))
-    v(128, ["qm"], ["sd"], ts(T.sd[:], T.qm[:, 0:128], 0.0, 1e9, A.is_equal, A.mult))
-    v(512, [], ["sj"], lambda: V.memset(T.sj[:], 0.0))
-    v(64, [], ["sj"], lambda: V.memset(T.sj[:, 0::16], -16384.0))
+    s(C, ["qm"], ["kc"], sc(T.kc[:, 0:C], T.qm[:, 0:C], 1.0, -7.75))
+    v(C, ["qm"], ["sd"], ts(T.sd[:, 0:C], T.qm[:, 0:C], 0.0, 1e9, A.is_equal, A.mult))
+    jn = JN = 256 if O["jf"] else 512
+    v(jn / 2, [], ["sj"], lambda: V.memset(T.sj[:, 0:jn], 0.0))
+    v(64, [], ["sj"], lambda: V.memset(T.sj[:, 0:jn:16], -16384.0))
     v(32, ["iq", "c5"], ["e1"], ts(T.e1[:], T.iq[:, 0:32], col(5), 1.0, A.is_equal, A.mult))
     s(32, ["e1"], ["pe"], sc(T.pe[:], T.e1[:], -B, B))
     s(R, ["iq"], ["ncn"], sc(T.ncn[:], T.iq[:], 2.0, -2048.0 - K0))
-    s(16, ["iq", "c6"], ["ncr"], lambda: Sc.activation(T.ncr[:], T.iq[:, 0:16], F.Identity, bias=col(6), scale=32.0))
-    v(R, ["qm", "c1"], ["tri"], ts(T.tri[:], T.qm[:], col(1), 0.5, A.is_le, A.mult))
-    v(K0, [], ["exa", "exb"], lambda: V.memset(T.ck[:, 0:K0], 0), name="ex0")
-    v(16, [], ["Kx"], lambda: V.memset(T.ck[:, K0 + W:], 0))
-    v(32, [], ["sua", "sub"], lambda: V.memset(T.su[:], 0), name="su0")
-    for c in "ab":
-        v(1, [], ["bc" + c], lambda c=c: V.memset(T["bc" + c][:], -7.0))
-        for q in range(4):
-            if CFG["cp"][c][q] == "1":
-                v(1, ["c1"], ["c9"], ts(col(9), col(1), 4.0 * q - 0.5, -16.0, A.is_gt, A.mult))
-                v(1, ["c1"], ["c10"], ts(col(10), col(1), 4.0 * q + 3.5, 16.0, A.is_gt, A.mult))
-                v(1, ["c9", "c10"], ["bc" + c], lambda c=c: V.tensor_scalar(T["bc" + c][:], T["bc" + c][:], col(9), col(10), A.add, A.add))
-                ops[-1]["rd"].append("bc" + c)
-    v(R, ["nm"], ["lu0a", "lu0b"], lambda: V.tensor_copy(T.lu[:, 0:R], T.nm[:]))
-    for k in range(16):
-        v(R / 2, ["ys0"], ["yx0_%d" % k], lambda k=k: V.tensor_copy(T.yx[:, k:W:16], T.ys[:, 0:R]))
-    for j in range(1, N):
+    v(16, ["iq", "c1"], ["tri"], ts(T.tri[:], T.iq[:, 0:16], col(1), 0.5, A.is_le, A.mult))
+    s(128, ["blk"], ["wob"], sc(T.wob[:], T.blk[:], WO))
+    v(C, ["qm", "c1"], ["k4"], ts(T.k4[:, 0:C], T.qm[:, 0:C], col(1), 1.0, A.is_equal, A.mult))
+    s(C, ["k4"], ["dh"], sc(T.dh[:, 0:C], T.k4[:, 0:C], 2.0 ** 20 + 16 * WO * sg + 2048.0, -2.0 ** 20))
+    v(160, [], ["msk"], lambda: V.memset(T.msk[:], 2048.0))
+    z = 0
+    for x in range(C // 16):
+        s(16, ["msk", "tri"], ["msk%d" % x], sc(T.msk[:, z:z + 16], T.tri[:], -16384.0, 2048.0))
+        z += (x // 4 + 1) * G - 16 * x
+    v(C, ["qm"], ["sk"], ts(T.sk[:, 0:C], T.qm[:, 0:C], 0.0, -2.0 ** 21, A.is_equal, A.mult))
+    if not O["obs"]:
+        v(8, [], ["k3"], lambda: V.memset(T.k3[:], 16 * WO * sg + 2048.0))
+    for x in range(C // G):
+        s(4, ["iq", "c8"], ["spr%d" % x], lambda x=x: Sc.activation(T.spr[:, 4 * x:4 * x + 4], T.iq[:, 0:4], F.Identity, bias=col(8), scale=16.0))
+    if O["or"] or O["ofr"]:
+        v(C, ["qm", "c1"], ["dg"], ts(T.dg[:, 0:C], T.qm[:, 0:C], col(1), -B, A.not_equal, A.mult))
+    if not O["ofr"]:
+        s(16, ["iq", "c6"], ["ncr"], lambda: Sc.activation(T.ncr[:], T.iq[:, 0:16], F.Identity, bias=col(6), scale=32.0))
+    if O["m1"]:
+        s(128, ["eye"], ["eye4"], sc(T.eye4[:], T.eye[:], 1.0))
+        v(256, ["nsh", "ish"], ["nis"], lambda: V.tensor_tensor(T.nis[:], T.nsh[:], T.ish[:], A.subtract))
+    v(64, [], ["k2"], lambda: V.memset(T.k2[:], 2048.0))
+    v(K0, [], ["ex" + c for c in PARTS], lambda: V.memset(T.ck[:, 0:K0], 0), name="ex0")
+    v(G, [], ["Kx"], lambda: V.memset(T.ck[:, K0 + W:], 0))
+    for i, c in enumerate(PARTS):
+        bc, cp = T.bc[:, i:i + 1], CFG["cp"][c]
+        v(1, [], ["bc" + c], lambda bc=bc: V.memset(bc, -23.0))
+        for q in range(len(cp)):
+            if cp[q] == "2":
+                v(1, ["c1"], ["c9"], ts(col(9), col(1), 16.0 * q / len(cp) - 0.5, 16.0, A.is_gt, A.mult))
+                v(1, ["c1"], ["c10"], ts(col(10), col(1), 16.0 * (q + 1) / len(cp) - 0.5, -16.0, A.is_gt, A.mult))
+                v(1, ["c9", "c10", "bc" + c], ["bc" + c], ts(bc, bc, col(9), col(10), A.add, A.add))
+    v(R, ["nm"], ["lu0" + c for c in PARTS], lambda: V.tensor_copy(T.lu[:, 0:R], T.nm[:]))
+    used = lambda names: [first[c] // 32 + x for c in PARTS for x in range(C // 32) if O["py"] or any(CFG[n][c][x] != "3" for n in names)]
+    for j in range(N):
+        xs = used(["vp", "vp0"] if j == 0 else ["vp"]) or [0]
+        a, b = 32 * min(xs), 32 * max(xs) + 32
         for k in range(16):
-            op("g", 600.0, ["ys%d" % j], ["yx%d_%d" % (j, k)],
-               lambda j=j, k=k: g.affine_select(T.yx[:, j * W + k:(j + 1) * W:16], T.ys[:, j * R:(j + 1) * R], [[0, R]], A.is_gt, 0.0, 1, 0))
+            out, in_ = T.yx[:, j * W + 16 * a + k:j * W + 16 * b:16], T.ys[:, j * R + a:j * R + b]
+            if j == 0:
+                v((b - a) / 2, ["ys0"], ["yx0_%d" % k], lambda out=out, in_=in_: V.tensor_copy(out, in_))
+            else:
+                op("g", 170.0 + 1.66 * (b - a), ["ys%d" % j], ["yx%d_%d" % (j, k)],
+                   lambda out=out, in_=in_, n=b - a: g.affine_select(out, in_, [[0, n]], A.is_gt, 0.0, 1, 0))
+                ops[-1]["after"] = j - 2
     cbank = [0]
     KW = T.ck[:, K0:K0 + W]
+    NB = C // 16
 
-    def half(t, c):
-        r0 = C if c == "a" else 0
-        rs, ns = slice(r0, r0 + C), slice(r0 // 16, r0 // 16 + 8)
-        H = lambda n: T[n + c]
+    def part(t, c):
+        r0, ix = first[c], PARTS.index(c)
+        rs, ns, ends = slice(r0, r0 + C), slice(r0 // 16, r0 // 16 + NB), slice(r0 + 15, r0 + C, 16)
         k_ = lambda n: n + c
-        eng = CFG["eng"]
-        n0 = t * R + r0
+        n0, e0 = t * R + r0, 16 * r0
         pu = "lu%d%s" % (t, c)
         PF = T.pf[:, rs]
-        b1, b2 = (3, 5) if c == "a" else (4, 6)
+        b1, b2, z2 = (3 + ix, 5 + ix, 0) if C > 64 else (3 + ix, 3 + ix, 256)
         p1, p2 = T["ps%d" % b1], T["ps%d" % b2]
-        uu, zz, orr, ofr = p1[:, 128:256], p1[:, 256:384], p1[:, 384:392], p1[:, 392:400]
-        ol, pp, b0, kp = p2[:, 0:128], p2[:, 128:256], p2[:, 256:384], p2[:, 384:512]
+        uu, zz, orr, ofr = p1[:, C:2 * C], p1[:, 2 * C:3 * C], p1[:, 3 * C:3 * C + NB], p1[:, 3 * C + 8:3 * C + 8 + NB]
+        ol, pp, b0, kp = [p2[:, z2 + i * C:z2 + (i + 1) * C] for i in range(4)]
         j = t % N
         yxs = ["yx%d_%d" % (j, k) for k in range(16)]
         vp, kq, cp = CFG["vp0" if t == 0 else "vp"][c], CFG["kg0" if t == 0 else "kg"][c], CFG["cp"][c]
         lin(eng["pf"], C, [pu], [k_("pf")], PF, T.lu[:, n0:n0 + C], -2048.0, half=True)
-        for x in range(4):
-            cs = slice(x * 512, (x + 1) * 512)
+        for x in range(C // 32):
             win = lambda x=x: T.vt[:, 0:W].indirect(T.lu[:, n0 + x * 32:n0 + (x + 1) * 32])
-            y0 = j * W + r0 * 16 + x * 512
-            yy, ab, vx, vq = T.yx[:, y0:y0 + 512], H("ab")[:, 2 * x:2 * x + 2], H("vx")[:, 2 * x:2 * x + 2], H("vq")[:, cs]
+            y0 = e0 + x * 512
+            yy, ab, vq = T.yx[:, j * W + y0:j * W + y0 + 512], T.ab[:, y0 // 256:y0 // 256 + 2], T.vq[:, y0:y0 + 512]
             if vp[x] == "1":
-                op("v", ga_(512, "v"), [pu, "vt"] + yxs, [k_("vx%d" % x)], lambda vx=vx, win=win, yy=yy: V.tensor_tensor(vx, win(), yy, A.subtract), name=k_("vg"))
-                v(256, [k_("vx%d" % x)], [k_("ab%d" % x)], ts(ab, vx, 0.0, -2.0, A.min, A.mult), name=k_("ab"))
+                for y in range(2):
+                    a = y0 + y * 256
+                    op("v", ga_(256, "v"), [pu, "vt"] + yxs, [k_("vq%d%d" % (x, y))],
+                       lambda a=a: V.tensor_tensor(T.vx[:, a // 256, :], T.vt[:, 0:W].indirect(T.lu[:, t * R + a // 16:t * R + a // 16 + 16]),
+                                                   T.yx[:, j * W + a:j * W + a + 256], A.subtract), name=k_("vg%d" % x))
+                v(256, [k_("vq%d%d" % (x, y)) for y in range(2)], [k_("ab%d" % x)],
+                  ts(ab, T.vx[:, y0 // 256:y0 // 256 + 2, :], 0.0, -2.0, A.min, A.mult))
             elif vp[x] == "2":
-                op("v", ga_(512, "v"), [pu, "vt"] + yxs, [k_("vq%d" % x)], lambda vq=vq, win=win, yy=yy: V.tensor_tensor(vq, win(), yy, A.subtract), name=k_("vg"))
-                s(512, [k_("vq%d" % x)], [k_("ab%d" % x)], lambda ab=ab, vq=vq: Sc.activation(ab, vq, F.Abs), name=k_("ab"))
+                nv = 2 if O["fine"] else 1
+                for y in range(nv):
+                    a, n = y0 + y * 512 // nv, 512 // nv
+                    op("v", ga_(n, "v"), [pu, "vt"] + yxs, [k_("vq%d%d" % (x, y))],
+                       lambda a=a, n=n: V.tensor_tensor(T.vq[:, a:a + n], T.vt[:, 0:W].indirect(T.lu[:, t * R + a // 16:t * R + (a + n) // 16]),
+                                                        T.yx[:, j * W + a:j * W + a + n], A.subtract), name=k_("vg%d" % x))
+                s(512, [k_("vq%d%d" % (x, y)) for y in range(2)], [k_("ab%d" % x)], lambda ab=ab, vq=vq: Sc.activation(ab, vq, F.Abs))
             else:
-                gat("s", 512, [pu, "vt"], [k_("vq%d" % x)], vq, win, 0.0, name=k_("vg"))
-                mm([k_("vq%d" % x), "eye", "neye"] + yxs, ["pd0"], 0, [[(T.ps0[:], T.eye[:], vq, 512), (T.ps0[:], T.neye[:], yy, 512)]], name=k_("pd"))
-                s(512, ["pd0"], [k_("ab%d" % x)], lambda ab=ab: Sc.activation(ab, T.ps0[:], F.Abs), [0], name=k_("ab"))
-        kn = 2048 // len(kq)
+                gat("s", 512, [pu, "vt"], [k_("vq%d%d" % (x, y)) for y in range(2)], vq, win, 0.0, name=k_("vg%d" % x))
+                bk = cbank[0] % 2
+                cbank[0] += 1
+                pd = T["ps%d" % bk]
+                y1 = T.ys[:, j * R + r0 + 32 * x:j * R + r0 + 32 * x + 32]
+                mm([k_("vq%d0" % x), k_("vq%d1" % x), "eye", "neye", "ys%d" % j] + (yxs if O["py"] else []), ["pd%d" % bk], bk,
+                   [[(pd[:], T.eye[:], vq, 512)] + ([(pd[:], T.neye[:], yy, 512)] if O["py"] else [(pd[:, k::16], T.neye[:], y1, 32) for k in range(16)])],
+                   name=k_("pd%d" % x))
+                s(512, ["pd%d" % bk], [k_("ab%d" % x)], lambda ab=ab, pd=pd: Sc.activation(ab, pd[:], F.Abs), [bk])
+        kn = 16 * C // len(kq)
         for x in range(len(kq)):
-            cs = slice(x * kn, (x + 1) * kn)
-            gat(kq[x], kn, [pu, "K"], [k_("kg%d" % x)], H("kg")[:, cs],
-                lambda x=x: KW.indirect(T.lu[:, n0 + x * kn // 16:n0 + (x + 1) * kn // 16]), -2048.0, name=k_("kg"))
-            v(kn / 2, [k_("kg%d" % x), "sj"], [k_("js%d" % x)],
-              lambda cs=cs: V.tensor_tensor_scan(H("js")[:, cs], T.sj[:, 0:kn], H("kg")[:, cs], 0.0, A.add, A.max), name=k_("js"))
-        kgs, jss = [k_("kg%d" % x) for x in range(len(kq))], [k_("js%d" % x) for x in range(len(kq))]
-        for x in range(2):
-            d = p1[:, 64 * x:64 * x + 64]
-            grp = [(d, T.eye[:], T.kc[:], 64)] + [(d, sel("w16", nl), H("ab")[:, 4 * x:4 * x + 4, nl, :], 64) for nl in range(16)]
-            ones = [y for y in (2 * x, 2 * x + 1) if vp[y] == "1"]
-            if ones:
-                a, b = ones[0], ones[-1] + 1
-                grp += [(p1[:, 32 * a:32 * b], sel("w16", nl), H("vx")[:, 2 * a:2 * b, nl, :], 64) for nl in range(16)]
-            mm([k_("ab%d" % y) for y in (2 * x, 2 * x + 1)] + [k_("vx%d" % y) for y in ones] + ["w16", "eye", "kc"], [k_("dk%d" % x)], b1, [grp], name=k_("dk"))
-        v(C, [k_("dk0"), k_("dk1"), "sd"], [k_("ks")], lambda: V.tensor_tensor_scan(T.ks[:, rs], T.sd[:], p1[:, 0:128], 0.0, A.add, A.min), [b1])
-        kl = T.ks[:, r0 + 15:r0 + C:16]
-        v(8, [k_("ks")], [k_("kt")], ts(T.kt[:, ns], kl, M16, -M16 - 16.0, A.add, A.add))
-        if CFG["tt16"]:
-            v(16, [k_("ks"), k_("kt")], [k_("ku")], lambda: V.tensor_tensor(T.ku[:, ns], kl, T.kt[:, ns], A.subtract))
-        else:
-            v(16, [k_("ks"), k_("kt")], [k_("kw")], lambda: V.tensor_tensor(T.kw[:, ns], kl, T.kt[:, ns], A.subtract))
-            v(8, [k_("kw")], [k_("ku")], lambda: V.tensor_copy(T.ku[:, ns], T.kw[:, ns]))
+            cs = slice(e0 + x * kn, e0 + (x + 1) * kn)
+            gat(kq[x], kn, [pu, "K"], [k_("kg%d" % x)], T.kg[:, cs],
+                lambda x=x: KW.indirect(T.lu[:, n0 + x * kn // 16:n0 + (x + 1) * kn // 16]), -2048.0)
+        for x in range(16 * C // JN):
+            cs = slice(e0 + x * JN, e0 + (x + 1) * JN)
+            v(JN / 2, [k_("kg%d" % (x * JN // kn)), "sj"], [k_("js%d" % x)],
+              lambda cs=cs: V.tensor_tensor_scan(T.js[:, cs], T.sj[:, 0:JN], T.kg[:, cs], 0.0, A.add, A.max))
+        kgs, jss = [k_("kg%d" % x) for x in range(len(kq))], [k_("js%d" % x) for x in range(16 * C // JN)]
+        entry = lambda buf, k: buf[:, e0 + k:e0 + 16 * C:16]
+        nd = 1 if O["dk"] or C == 64 else 2
+        dw, nx = C // nd, C // 32 // nd
+        for x in range(nd):
+            d, h0 = p1[:, dw * x:dw * (x + 1)], r0 // 16 + 2 * nx * x
+            grp = [(d, T.eye[:], T.kc[:, 0:dw], dw)] + [(d, sel("w16", nl), T.ab[:, h0:h0 + 2 * nx, nl, :], dw) for nl in range(16)]
+            ones = [y for y in range(nx * x, nx * (x + 1)) if vp[y] == "1"]
+            for a, b in ([(ones[0], ones[-1] + 1)] if ones and ones[-1] - ones[0] == len(ones) - 1 else [(y, y + 1) for y in ones]):
+                grp += [(p1[:, 32 * a:32 * b], sel("w16", nl), T.vx[:, r0 // 16 + 2 * a:r0 // 16 + 2 * b, 16 * nl:16 * nl + 16], 32 * (b - a)) for nl in range(16)]
+            mm([k_("ab%d" % y) for y in range(nx * x, nx * (x + 1))] + [k_("vq%d%d" % (y, z)) for y in ones for z in range(2)] + ["w16", "eye", "kc"],
+               [k_("dk%d" % x)], b1, [grp])
+        v(C, [k_("dk%d" % x) for x in range(nd)] + ["sd"], [k_("ks")], lambda: V.tensor_tensor_scan(T.ks[:, rs], T.sd[:, 0:C], p1[:, 0:C], 0.0, A.add, A.min), [b1])
+        v(8, [k_("ks")], [k_("kt")], ts(T.kt[:, ns], T.ks[:, ends], M16, -M16 - 16.0, A.add, A.add))
+        v(16, [k_("ks"), k_("kt")], [k_("ku")], lambda: V.tensor_tensor(T.ku[:, ns], T.ks[:, ends], T.kt[:, ns], A.subtract))
         po, pen = T.po[:, rs], T.pen[:, rs]
         op("v", ga_(C, "v"), [k_("ku"), k_("pf"), "e1"], [k_("po")], lambda: V.tensor_tensor(po, T.e1[:, 0:32].indirect(T.ku[:, ns]), PF, A.mult))
         gat("s", C, [k_("ku"), "pe"], [k_("pen")], pen, lambda: T.pe[:, 0:32].indirect(T.ku[:, ns]), 0.0)
-        mm([k_("po"), "w1"], [k_("or")], b1, [[(orr, sel("w1", nl), T.po[:, r0 + nl:r0 + C:16], 8) for nl in range(16)]])
-        lin(eng["ou"], 8, [k_("or")], [k_("ou")], T.ou[:, ns], orr, 2048.0, [b1])
-        lin("s", 8, [k_("or")], [k_("of")], T.of[:, ns], orr, 0.0, [b1])
+        rows = lambda out, w, buf: [(out, sel(w, nl), buf[:, r0 + nl:r0 + C:16], NB) for nl in range(16)]
+        if not O["or"]:
+            mm([k_("po"), "w1"], [k_("or")], b1, [rows(orr, "w1", T.po)])
+            lin(eng["ou"], 8, [k_("or")], [k_("ou")], T.ou[:, ns], orr, 2048.0, [b1])
+            if not O["obs"]:
+                lin("s", 8, [k_("or")], [k_("of")], T.osn[:, ends], orr, 0.0, [b1])
+        else:
+            mm([k_("po"), "blk", "eye", "dg"], [k_("zz")], b1, [[(zz, T.eye[:], T.dg[:, 0:C], C), (zz, T.blk[:], po, C)]], name=k_("or"))
+            v(C, [k_("zz"), "sj"], [k_("of")], lambda: V.tensor_tensor_scan(T.osn[:, rs], T.sj[:, 0:C], zz, 0.0, A.add, A.max), [b1], name=k_("os"))
+            lin(eng["ou"], 8, [k_("of")], [k_("ou")], T.ou[:, ns], T.osn[:, ends], 2048.0)
         gat(eng["ko"], C, [k_("ou"), "K"], [k_("ko")], T.ko[:, rs], lambda: KW.indirect(T.ou[:, ns]), -2048.0)
         mm([k_("po"), "blk"], [k_("ol")], b2, [[(ol, T.blk[:], po, C)]])
         v(C, [k_("ol"), k_("pf")], [k_("eq")], lambda: V.tensor_tensor(T.eq[:, rs], PF, ol, A.is_equal), [b2])
         if "1" in cp:
             mm([k_("ko"), "eye"], [k_("kp")], b2, [[(kp, T.eye[:], T.ko[:, rs], C)]])
-        for q in range(4):
-            ks_ = range(4 * q, 4 * q + 4)
+        nq, grp, rd = len(cp), [], []
+        for q in range(nq):
+            ks_ = range(16 * q // nq, 16 * (q + 1) // nq)
+            cb = lambda k, n=1: T.cb[:, e0 + k * C:e0 + (k + n) * C]
             if cp[q] == "1":
                 for k in ks_:
-                    v(C, kgs + [k_("kp")], [k_("cb%d" % k)],
-                      lambda k=k: V.tensor_tensor(H("cb")[:, k * C:(k + 1) * C], H("kg")[:, k::16], kp, A.is_ge), [b2], name=k_("cb"))
+                    v(C, kgs + [k_("kp")], [k_("cb%d" % k)], lambda k=k, cb=cb: V.tensor_tensor(cb(k), entry(T.kg, k), kp, A.is_ge), [b2], name=k_("cb%d" % q))
             else:
-                bk = 1 + cbank[0] % 2
-                cbank[0] += 1
-                pd = T["ps%d" % bk]
-                mm(kgs + [k_("ko"), "eye", "neye"], ["pd%d" % bk], bk,
-                   [[(pd[:, i * C:(i + 1) * C], T.eye[:], H("kg")[:, k::16], C), (pd[:, i * C:(i + 1) * C], T.neye[:], T.ko[:, rs], C)] for i, k in enumerate(ks_)], name=k_("df"))
-                s(512, ["pd%d" % bk], [k_("cb%d" % k) for k in ks_],
-                  lambda q=q, pd=pd: Sc.activation(H("cb")[:, q * 512:(q + 1) * 512], pd[:], F.Sign, bias=0.5), [bk], name=k_("cb"))
-            grp = [(uu, sel("w2" if cp[q] == "1" else "w1", k), H("cb")[:, k * C:(k + 1) * C], C) for k in ks_]
-            if q == 3:
-                grp.append((uu, T.n15[:], T.eq[:, rs], C))
-            mm([k_("cb%d" % k) for k in ks_] + ["w1", "w2", "n15"] + ([k_("eq")] if q == 3 else [k_("ou"), k_("of")] if q == 0 else []), [k_("uu")], b1, [grp],
-               free=[k_("uu")] if q else [], opens=q == 0, closes=q == 3)
-        s(C, [k_("uu"), k_("bc")], [k_("ov")], lambda: Sc.activation(T.ov[:, rs], uu, F.Sign, bias=H("bc")[:]), [b1])
-        mm([k_("ov"), k_("pf"), "tm", "czr", "eye"], [k_("zz")], b1, [[(zz, T.eye[:], PF, C), (zz, T.eye[:], T.czr[:], C), (zz, T.tm[:], T.ov[:, rs], C)]])
+                pd = T.ps2
+                mm(kgs + [k_("ko"), "eye", "neye"], ["pd2"], 2,
+                   [[(pd[:, i * C:(i + 1) * C], T.eye[:], entry(T.kg, k), C), (pd[:, i * C:(i + 1) * C], T.neye[:], T.ko[:, rs], C)] for i, k in enumerate(ks_)], name=k_("df%d" % q))
+                s(len(ks_) * C, ["pd2"], [k_("cb%d" % k) for k in ks_],
+                  lambda ks_=ks_, cb=cb, pd=pd: Sc.activation(cb(ks_[0], len(ks_)), pd[:, 0:len(ks_) * C], F.Sign, bias=0.5), [2], name=k_("cb%d" % q))
+            grp += [(uu, sel("w2" if cp[q] == "1" else "w1", k), cb(k), C) for k in ks_]
+            rd += [k_("cb%d" % k) for k in ks_]
+            if q == nq - 1:
+                grp.insert(0, (uu, T.n15[:], T.eq[:, rs], C))
+                rd.append(k_("eq"))
+            if q == nq - 1 or b1 != b2:
+                whole = b1 == b2
+                mm(rd + ["w1", "w2", "n15"] + ([k_("ou"), k_("of")] if q == 0 else []), [k_("uu")], b1, [grp],
+                   name=k_("uu%d" % q), free=[k_("uu")] if q and not whole else [], opens=q == 0 or whole, closes=q == nq - 1)
+                grp, rd = [], []
+        if eng["ov"] == "s":
+            s(C, [k_("uu"), k_("bc")], [k_("ov")], lambda: Sc.activation(T.ov[:, rs], uu, F.Sign, bias=T.bc[:, ix:ix + 1]), [b1])
+        else:
+            v(C, [k_("uu"), k_("bc")], [k_("ov")], ts(T.ov[:, rs], uu, T.bc[:, ix:ix + 1], 0.0, A.add, A.is_gt), [b1])
+        mm([k_("ov"), k_("pf"), "tm", "czr", "eye"], [k_("zz")], b1, [[(zz, T.eye[:], PF, C), (zz, T.eye[:], T.czr[:, 0:C], C), (zz, T.tm[:], T.ov[:, rs], C)]])
         v(C, [k_("zz"), "ncn"], [k_("va")], lambda: V.tensor_tensor(T.va[:, rs], T.ncn[:, rs], zz, A.max), [b1])
-        mm([k_("va"), "w1", "n15", "ncr"], [k_("ofr")], b1,
-           [[(ofr, T.n15[:], T.ncr[:, ns], 8)] + [(ofr, sel("w1", nl), T.va[:, r0 + nl:r0 + C:16], 8) for nl in range(16)]])
-        lin(eng["off"], 8, [k_("ofr")], [k_("off")], T.off[:, ns], ofr, 2048.0 + K0 - 2 * r0, [b1])
+        if not O["ofr"]:
+            mm([k_("va"), "w1", "n15", "ncr"], [k_("ofr")], b1, [[(ofr, T.n15[:], T.ncr[:, ns], 8)] + rows(ofr, "w1", T.va)])
+            lin(eng["off"], 8, [k_("ofr")], [k_("off")], T.off[:, ns], ofr, 2048.0 + K0 - 2 * r0, [b1])
+        else:
+            mm([k_("va"), "blk", "eye", "dg", "n15", "ncn"], [k_("zz")], b1,
+               [[(zz, T.eye[:], T.dg[:, 0:C], C), (zz, T.n15[:], T.ncn[:, rs], C), (zz, T.blk[:], T.va[:, rs], C)]], name=k_("ofr"))
+            v(C, [k_("zz"), "sj"], [k_("fs")], lambda: V.tensor_tensor_scan(T.fs[:, rs], T.sj[:, 0:C], zz, 0.0, A.add, A.max), [b1])
+            lin(eng["off"], 8, [k_("fs")], [k_("off")], T.off[:, ns], T.fs[:, ends], 2048.0 + K0 - 2 * r0)
         mm([k_("pf"), "eye"], [k_("pp")], b2, [[(pp, T.eye[:], PF, C)]])
-        v(C, jss + [k_("pp")], [k_("ac")], lambda: V.tensor_tensor(T.ac[:, rs], H("js")[:, 15::16], pp, A.max), [b2])
-        mm([k_("ac"), k_("pen"), "eye"], [k_("pp")], b2, [[(pp, T.eye[:], T.ac[:, rs], C), (pp, T.eye[:], pen, C)]], name=k_("px"))
-        lin("s", C, [k_("pp")], [k_("ex")], T.ck[:, 2 * r0:2 * r0 + 2 * C:2], pp, 2048.0, [b2])
-        lin("s", C, jss, [k_("ju")], T.ju[:, rs], H("js")[:, 15::16], 2048.0)
-        mm([k_("pf"), k_("pen"), "eye", "ish", "k1"], [k_("b0")], b2, [[(b0, T.eye[:], PF, C), (b0, T.eye[:], T.k1[:], C), (b0, T.ish[:], pen, C)]])
-        mm([k_("va"), k_("pen"), "eye", "nsh", "k2", "n15", "ncn", "blk"], [k_("ol")], b2,
-           [[(ol, T.eye[:], T.k2[:], C), (ol, T.n15[:], T.ncn[:, rs], C), (ol, T.nsh[:], pen, C), (ol, T.blk[:], T.va[:, rs], C)]], name=k_("yb"))
-        op("v", ga_(C, "v"), [k_("off"), k_("pen"), "K", "exa"] + (["exb"] if c == "b" else []), [k_("xf")],
+        v(C, jss + [k_("pp")], [k_("ac")], lambda: V.tensor_tensor(T.ac[:, rs], entry(T.js, 15), pp, A.max), [b2])
+        if eng["ex"] == "s" or not O["m1"]:
+            mm([k_("ac"), k_("pen"), "eye"], [k_("pp")], b2, [[(pp, T.eye[:], T.ac[:, rs], C), (pp, T.eye[:], pen, C)]], name=k_("px"))
+            lin("s", C, [k_("pp")], [k_("ex")], T.ck[:, 2 * r0:2 * r0 + 2 * C:2], pp, 2048.0, [b2])
+        else:
+            mm([k_("pen"), "eye", "k2"], [k_("b0")], b2, [[(b0, T.eye[:], T.k2[:, 0:C], C), (b0, T.eye[:], pen, C)]], name=k_("px"))
+            v(C, [k_("ac"), k_("b0")], [k_("ex")], lambda: V.tensor_tensor(T.ck[:, 2 * r0:2 * r0 + 2 * C:2], T.ac[:, rs], b0, A.add), [b2])
+        lin("s", C, jss, [k_("ju")], T.ju[:, rs], entry(T.js, 15), 2048.0)
+        g0 = [(b0, T.eye[:], PF, C), (b0, T.eye[:], T.k1[:, 0:C], C), (b0, T.ish[:], pen, C)]
+        if not O["m1"]:
+            mm([k_("pf"), k_("pen"), "eye", "ish", "k1"], [k_("b0")], b2, [g0])
+            mm([k_("va"), k_("pen"), "eye", "nsh", "k2", "n15", "ncn", "blk"], [k_("ol")], b2,
+               [[(ol, T.eye[:], T.k2[:, 0:C], C), (ol, T.n15[:], T.ncn[:, rs], C), (ol, T.nsh[:], pen, C), (ol, T.blk[:], T.va[:, rs], C)]], name=k_("yb"))
+        else:
+            mm([k_("va"), k_("pen"), k_("pf"), "neye", "nis", "n15", "ncn", "blk"], [k_("ol")], b2,
+               [[(ol, T.neye[:], PF, C), (ol, T.n15[:], T.ncn[:, rs], C), (ol, T.nis[:], pen, C), (ol, T.blk[:], T.va[:, rs], C)]], name=k_("yb"))
+            s(C, [k_("ol")], [k_("wr")], lambda: Sc.activation(T.wr[:, rs], ol, F.Relu, bias=2 * B), [b2])
+            mm([k_("pf"), k_("pen"), k_("wr"), "eye", "eye4", "ish", "k1"], [k_("b0")], b2, [g0 + [(b0, T.eye4[:], T.wr[:, rs], 4 * C)]], name=k_("ww"))
+        op("v", ga_(C, "v"), [k_("off"), k_("pen"), "K"] + ["ex" + x for x in PARTS[:ix + 1]], [k_("xf")],
            lambda: V.tensor_tensor(T.xf[:, rs], T.ck[:, 2 * r0:K0 + W].indirect(T.off[:, ns]), pen, A.subtract))
-        v(C, [k_("xf"), k_("b0")], [k_("m1")], lambda: V.tensor_tensor(T.m1[:, rs], T.xf[:, rs], b0, A.max), [b2])
         last = t == RO - 1
         if last:
             src, dst = T.nf[:, rs], T.op[:, rs]
         else:
             src, dst = T.nu[:, n0:n0 + C], T.lu[:, n0 + R:n0 + R + C]
-        if last or CFG["tt16"]:
+        if not O["m1"]:
+            v(C, [k_("xf"), k_("b0")], [k_("m1")], lambda: V.tensor_tensor(T.m1[:, rs], T.xf[:, rs], b0, A.max), [b2])
             v(C, [k_("m1"), k_("ol")], [k_("nu%d" % t)], lambda: V.tensor_tensor(src, T.m1[:, rs], ol, A.max), [b2], name=k_("nu"))
         else:
-            v(C, [k_("m1"), k_("ol")], [k_("nf")], lambda: V.tensor_tensor(T.nf[:, rs], T.m1[:, rs], ol, A.max), [b2])
-            v(C, [k_("nf")], [k_("nu%d" % t)], lambda: V.tensor_copy(src, T.nf[:, rs]), name=k_("nu"))
+            v(C, [k_("xf"), k_("b0")], [k_("nu%d" % t)], lambda: V.tensor_tensor(src, T.xf[:, rs], b0, A.max), [b2], name=k_("nu"))
         hop = 1 if not last else -t
         to, frm = cores[(rank + hop) % N], cores[(rank - hop) % N]
         sem = "ar%d%s" % (t + 1, c)
@@ -333,40 +411,50 @@ def build(g, core, T, topo):
         def send():
             assert topo.may_write(core, to)
             rid, pid, _ = topo.addr(to)
-            en = common(core)
+            en = topo.engines(core, to)
             g.remote_dma(dst, src, T.sem[sem], T.sem.sent, pid, rid, bits(en))
             sent[0] += len(en)
-        op("g", 300.0, [k_("nu%d" % t)], ["lu%d%s" % (t + 1, c)], send, sig=(sem, len(common(frm))), fin=EST["hop"], name=k_("send"))
+        op("g", 300.0, [k_("nu%d" % t)], ["lu%d%s" % (t + 1, c)], send, sig=(sem, len(topo.engines(frm, core))), fin=CFG["hop"], name=k_("send"))
 
-    def writers(cs):
-        r0, n = (C if cs == "a" else 0), C * len(cs)
-        rs, ns = slice(r0, r0 + n), slice(r0 // 16, (r0 + n) // 16)
-        k_ = lambda x: [x + c for c in cs]
-        p7 = T.ps7
-        x2, obp, lo = p7[:, 0:n], p7[:, 256:256 + n // 16], p7[:, 272:272 + n // 16]
-        mm(k_("of") + k_("ov") + ["eye", "wo"], ["obp"], 7,
-           [[(obp, T.eye[:], T.of[:, ns], 8)] + [(obp, sel("wo", nl), T.ov[:, r0 + nl:r0 + n:16], 8) for nl in range(16)]], name="obp" + cs)
-        lin("s", 8, ["obp"], k_("ob"), T.ob[:, ns], obp, 16 * WO, [7])
-        mm(k_("ob") + k_("po") + ["eye", "nblk", "tri"], ["x2"], 7,
-           [[(x2, T.nblk[:], T.po[:, rs], n), (x2, T.eye[:], T.tri[:, 0:n], n)] + [(p7[:, nl:n:16], T.eye[:], T.ob[:, ns], 8) for nl in range(1, 16)]], name="x2" + cs)
-        v(n, ["x2"], k_("ee"), ts(T.ee[:, rs], x2, 0.0, B, A.is_equal, A.mult), [7])
-        mm(k_("ee") + k_("ob") + ["eye", "w1"], ["lo"], 7,
-           [[(lo, T.eye[:], T.ob[:, ns], 8)] + [(lo, sel("w1", nl), T.ee[:, r0 + nl:r0 + n:16], 8) for nl in range(1, 16)]], name="lo" + cs)
-        v(8, ["lo", "c8"], k_("su"), ts(T.su[:, r0 // 8:(r0 + n) // 8:2], lo, 2048.0, col(8), A.add, A.min), [7])
+        p7, y7, d7 = T.ps7, 0, ""
+        if C == 64:
+            y7, d7 = 256 * (ix % 2), "01"[ix % 2]
+        obp = p7[:, y7 + 5 * C // 2:y7 + 5 * C // 2 + NB]
+        seg, z = [], 0
+        for x in range(NB):
+            seg.append((16 * x, (x // 4 + 1) * G, z))
+            z += (x // 4 + 1) * G - 16 * x
+        ee = lambda z, n: T.ee[:, 5 * r0 // 2 + z:5 * r0 // 2 + z + n]
+        mm([k_("po"), "eye", "blk"] + ["msk%d" % x for x in range(NB)], ["x2" + d7], 7,
+           [[(p7[:, y7:y7 + z], T.eye[:], T.msk[:, 0:z], z)] + [(p7[:, y7 + z:y7 + z + b - a], T.blk[:], T.po[:, r0 + a:r0 + b], G) for a, b, z in seg]], name=k_("x2"))
+        own = [(T.eye[:], T.dh[:, 0:C]), (T.blk[:], po), (T.wob[:], T.ov[:, rs])]
+        if O["obs"]:
+            ob7 = p7[:, 384:384 + C]
+            mm([k_("po"), k_("ov"), "eye", "blk", "wob", "dh"], ["obp" + d7], 7, [[(ob7, l, r, C) for l, r in own]], name=k_("obp"))
+            v(C, ["obp" + d7, "sk"], [k_("obs")], lambda: V.tensor_tensor_scan(T.obs[:, rs], T.sk[:, 0:C], ob7, 0.0, A.add, A.max), [7])
+        else:
+            mm([k_("of"), k_("ov"), "eye", "wo", "k3"], ["obp" + d7], 7,
+               [[(obp, T.eye[:], T.osn[:, ends], 8), (obp, T.eye[:], T.k3[:, 0:NB], 8)] + rows(obp, "wo", T.ov)], name=k_("obp"))
+        for x, (a, b, z) in enumerate(seg):
+            y = y7 + 5 * C // 2 + x
+            if O["obs"]:
+                y = r0 + 16 * x + 15
+                v(G, ["x2" + d7, k_("obs")], [k_("ee%d" % x)], ts(ee(z, b - a), p7[:, y7 + z:y7 + z + b - a], T.obs[:, y:y + 1], 1.0, A.is_equal, A.mult), [7], name=k_("ee"))
+            else:
+                v(G, ["x2" + d7, "obp" + d7], [k_("ee%d" % x)], ts(ee(z, b - a), p7[:, y7 + z:y7 + z + b - a], p7[:, y:y + 1], 1.0, A.is_equal, A.mult), [7], name=k_("ee"))
+        mm([k_("ee%d" % x) for x in range(NB)] + [k_("po"), k_("ov"), "eye", "blk", "wob", "dh"], [k_("uu")], b1,
+           [[(uu, l, r, C) for l, r in own] + [(p1[:, C + a:C + b], T.wob[:], ee(z, b - a), G) for a, b, z in seg]], name=k_("lo"))
+        v(C, [k_("uu"), "sk"], [k_("ls")], lambda: V.tensor_tensor_scan(T.ls[:, rs], T.sk[:, 0:C], uu, 0.0, A.add, A.max), [b1])
+        v(16, [k_("ls"), "spr0", "spr1"], [k_("su")], lambda: V.tensor_tensor(T.su[:, ns], T.ls[:, ends], T.spr[:, 0:NB], A.min))
 
     for t in range(RO):
         ph[0] = t
-        for c in "ab":
-            half(t, c)
-            if not CFG["whole"]:
-                writers(c)
-        if CFG["whole"]:
-            writers("ba")
-        for nh in range(15, -1, -1):
-            c = "ba"[nh // 8]
-            op("v", 55.0 + 16 * EST["sc"] * EST["cy"], ["su" + c, "ju" + c], ["K", "Kx"],
-               lambda nh=nh: V.tensor_copy(T.ck[:, K0:K0 + W + 16].indirect(T.su[:, 2 * nh:2 * nh + 1]), T.ju[:, nh * 16:nh * 16 + 16]),
-               name="sc" + c, free=[] if CFG["waw"] or nh == 15 else ["K", "Kx"])
+        for c in PARTS:
+            part(t, c)
+        for x in range(R // G - 1, -1, -1):
+            c = PARTS[(R - 1 - x * G) // C]
+            op("v", 55.0 + G * EST["sc"] * EST["cy"], ["su" + c, "ju" + c], ["K", "Kx"],
+               lambda x=x: V.tensor_copy(T.ck[:, K0:K0 + W + G].indirect(T.su[:, 4 * x:4 * x + 4]), T.ju[:, x * G:(x + 1) * G]), name="sc%d%s" % ((R - 1 - x * G) % C // G, c))
 
     ph[0] = RO
     for b in range(8):
@@ -374,13 +462,14 @@ def build(g, core, T, topo):
         lin("vs"[b % 2], E, ["K"], ["rk%d" % b], T.rk[:, x], T.ck[:, K0 + b * E:K0 + (b + 1) * E], -2048.0, name="rk")
         mm(["rk%d" % b, "eye"], ["pd1"], 1, [[(T.ps1[:], T.eye[:], T.rk[:, x], E)]], name="fold", free=["pd1"] if b else [], opens=b == 0, closes=b == 7)
     lin("v", E, ["pd1"], ["ok"], T.ok[:], T.ps1[:], 8 * 2048.0, [1])
-    dma(T.yk[:], T.ok[:], ["ok"], ["yk"], "st0", 2500.0)
-    for h, c in enumerate("ba"):
-        dma(T.yp[:, h * C:(h + 1) * C], T.op[:, h * C:(h + 1) * C], ["lu6" + c], ["yp" + c], "st%d" % (1 + h), 2500.0)
+    dma(T.yk[:], T.ok[:], ["ok"], ["yk"], "st", 2500.0)
+    for c in PARTS:
+        x = slice(first[c], first[c] + C)
+        dma(T.yp[:, x], T.op[:, x], ["lu6" + c], ["yp" + c], "st" + c, 2500.0)
     return ops, sent
 
 
-def order(ops):
+def depend(ops):
     n = len(ops)
     LAT = EST["lat"]
     lw, rs = {}, {}
@@ -402,51 +491,65 @@ def order(ops):
             rs[k] = []
         o["dep"] = d
         o["lat"] = {j: 0.0 if ops[j]["q"] == o["q"] and k <= o["free"] else LAT for j, k in d.items()}
-    succ = [[] for _ in range(n)]
+    last = {o["ph"]: j for j, o in enumerate(ops) if o["name"] == "send" + PARTS[-1]}
+    for o in ops:
+        if o.get("after", -1) >= 0:
+            j = last[o["after"]]
+            o["dep"][j], o["lat"][j] = {"q"}, -ops[j]["fin"]
+            o["free"].add("q")
+    for o in ops:
+        o["succ"], o["pr"] = [], 0.0
     for i, o in enumerate(ops):
         for j in o["dep"]:
-            succ[j].append(i)
-    pr = [0.0] * n
-    key = [0.0] * n
+            ops[j]["succ"].append(i)
     for i in range(n - 1, -1, -1):
         o = ops[i]
-        pr[i] = max(o["dur"], o["fin"]) + max([pr[s] + ops[s]["lat"][i] for s in succ[i]] + [0.0])
-        key[i] = CFG["pri"].get(o["name"], 0.0) * 1000 + pr[i]
-        if o.get("first"):
-            key[i] = 1e9 - i
+        o["pr"] = max(o["dur"], o["fin"]) + max([ops[s]["pr"] + ops[s]["lat"][i] for s in o["succ"]] + [0.0])
+
+
+def place(ops):
+    n = len(ops)
+    pos = [{x.lstrip("+"): i - 1000 * (x[0] == "+") for i, x in enumerate(l.split())} for l in (CFG["first"], CFG["order"], CFG["last"])]
+    key = []
+    for i, o in enumerate(ops):
+        if o["name"] in pos[2] and o["ph"] >= RO - 1:
+            key.append(1000 * (RO - 1) + pos[2][o["name"]])
+        elif o["name"] in pos[0] and o["ph"] <= 0:
+            key.append(pos[0][o["name"]] - 500)
+        elif 0 <= o["ph"] < RO:
+            key.append(1000 * o["ph"] + pos[1][o["name"]])
+        elif o.get("after", -1) >= 0:
+            key.append(1000 * o["after"] + 999)
+        else:
+            key.append(i - 9e6 if o.get("first") else -2e6 - o["pr"] if o["ph"] < 0 else 9e6 - o["pr"])
     left = [len(o["dep"]) for o in ops]
-    ready = [i for i in range(n) if left[i] == 0]
-    qf, end, bank, out, dr = {}, [0.0] * n, {}, [], [0.0] * n
-    while ready:
-        est = {}
-        for i in ready:
+    due, out, bank = [False] * n, [], {}
+    for i0 in sorted(range(n), key=lambda i: key[i]):
+        due[i0] = True
+        todo = [] if left[i0] else [i0]
+        while todo:
+            i = todo.pop(0)
             o = ops[i]
-            s = max(qf.get(o["q"], 0.0), dr[i])
+            o["turn"] = []
             for b in o["banks"]:
-                for q, j in bank.get(b, {}).items():
-                    if q != o["q"]:
-                        s = max(s, end[j] + LAT)
-            est[i] = s
-        i0 = min(ready, key=lambda i: est[i])
-        cand = [i for i in ready if ops[i]["q"] == ops[i0]["q"] and est[i] <= est[i0] + CFG["win"]]
-        i = max(cand, key=lambda i: (key[i], -i))
-        o = ops[i]
-        for b in o["banks"]:
-            for q, j in bank.setdefault(b, {}).items():
-                if q != o["q"]:
-                    o["dep"].setdefault(j, set())
-            bank[b][o["q"]] = i
-        o["start"] = est[i]
-        qf[o["q"]] = est[i] + o["dur"]
-        end[i] = est[i] + max(o["dur"], o["fin"])
-        out.append(i)
-        ready.remove(i)
-        for s in succ[i]:
-            left[s] -= 1
-            dr[s] = max(dr[s], end[i] + ops[s]["lat"][i])
-            if left[s] == 0:
-                ready.append(s)
-    return out, max(end)
+                o["turn"] += [j for q, j in bank.setdefault(b, {}).items() if q != o["q"]]
+                bank[b][o["q"]] = i
+            out.append(i)
+            for j in o["succ"]:
+                left[j] -= 1
+                if not left[j] and due[j]:
+                    todo.append(j)
+            todo.sort(key=lambda i: key[i])
+    return out, 0.0
+
+
+def order(ops):
+    depend(ops)
+    out, end = place(ops)
+    for o in ops:
+        for j in o["turn"]:
+            o["dep"].setdefault(j, set())
+    return out, end
 
 
 def rank_program(g, core, T, topo):

from concourse.bass import DstId, RemoteDMATransfer
from concourse.mybir import AluOpType as A, ActivationFunctionType as F

N, W, R, RO, E = 4, 4096, 256, 6, 512
C = 128
PARTS = "abcd"[:R // C]
K0 = 2 * R
B = 8192.0
M16 = 201326592.0
WO = 4160.0
G = 64
CFG = {
    "vp": {"a": "2233", "b": "2322"},
    "vp0": {"a": "2233", "b": "2322"},
    "kg": {"a": "ssvv", "b": "ssss"},
    "kg0": {"a": "ssvv", "b": "ssss"},
    "cp": {"a": "1122", "b": "2111"},
    "eng": {"ou": "v", "off": "s", "pf": "v", "ko": "s", "ov": "v", "ex": "s"},
    "opt": {"dk": 0, "or": 0, "ofr": 0, "m1": 1, "fine": 0, "jf": 0},
    "hop": 1800.0,
    "order": "pena poa kg1a kg3a ola ora x2a eqa kg0a oua kg2a ppa koa js1a ofa vg1b vg0b df2a kpa cb2a cb1a ab0b vg3b df3a kg1b pd1b cb0a cb3a pfb vg2b uu0a ab1b uu1a uu2a uu3a ab3b js0a dk0b js2a ab2b ova js3a js1b zza kg2b aca dk1b vaa pxa yba ksb ofra wra ktb obpa exa js2b offa kub jua wwa kg0b xfa ppb pob nua eea kg3b orb senda olb oub eqb loa kob js3b x2b js0b kpb lsa df0b cb1b cb0b cb2b ofb +vg3a cb3b uu0b uu1b uu2b +vg1a penb uu3b +vg2a +pd3a ovb sua acb zzb +ab3a obpb vab +vg0a pxb +ab1a ybb ofrb wrb eeb +pd2a exb jub offb +ab0a wwb xfb +ab2a +pfa lob nub +dk0a sc0a sendb lsb +dk1a sc1a sub +ksa sc0b +kta +kua sc1b",
    "first": "sj ncn pi4 c3 c4 yx0_15 c0 yx0_13 yx0_0 yx0_2 yx0_8 pi2 sd yx0_11 eye c1 yx0_3 blk yx0_9 yx0_7 w1 yx0_6 lu0a w16 yx0_1 c5 ex0 wo w2 kc yx0_5 neye c9 t1 t2 tm yx1_0 yx1_1 yx1_2 yx1_3 yx1_4 yx1_5 yx1_6 yx1_7 yx1_8 yx1_9 yx1_10 yx1_11 yx1_12 yx1_13 yx1_14 yx1_15 yx0_14 yx0_4 e1 pfb c2 yx0_10 pfa pe yx0_12 n15 c10 c8 bca vg2a vg3a pd2a vg1a vg1b ppb pd3a vg0a ab2a tri vg2b ab1a pd1b ab3a vg3b ab0a dk1a spr1 vg0b ab1b dk0a ab2b ksa ab3b kta k3 ab0b kua dk1b poa c6 wob kg1a kg3a ora dk0b k2 kg0a oua kg2a ola koa ksb js3a kg1b js2a kpa df2a Kx cb0a x2a ofa ncr cb2a ktb cb1a uu0a kg2b kub df3a nsh k4 eqa uu1a pob c7 uu2a cb3a bcb js2b kg0b ish uu3a js1a orb ova czr ppa js0a olb kg3b nis obpa oub aca zza dh eqb kob eea pena ofb kpb df0b jua vaa penb cb2b x2b eye4 cb0b pxa cb1b yba ofra spr0 exa cb3b uu0b uu1b offa wra uu2b k1 js0b uu3b js1b wwa xfa ovb loa sk nua zzb js3b obpb senda vab jub acb lsa ofrb eeb pxb offb exb lob xfb ybb sua lsb sc0a wrb sub wwb sc1a sc0b nub sc1b sendb",
    "last": "ypb ypa pena poa kg2a kg0a ora ppa vg1b oua vg0b koa kg3a kg1a pd1b kpa x2a vg2b ofa ab1b df2a ab0b ola vg3b cb2a dk0b cb0a ab2b df3a js1a ab3b cb1a uu0a cb3a js2a dk1b eqa kg1b js0a uu1a uu2a ksb uu3a pfb kg0b ktb ova kub js3a zza pob obpa kg2b vaa ppb orb eea olb kg3b ofra oub aca eqb js1b kob yba js2b jua pxa js0b kpb df0b wra cb1b x2b cb0b loa cb2b ofb exa cb3b penb uu0b offa uu1b uu2b js3b lsa uu3b jub acb ovb pxb zzb exb obpb vab sua xfa ofrb eeb offb xfb lob ybb sc0a wwa lsb wrb sc1a wwb sub nua sc0b senda sc1b nub rk sendb fold ok yk",
}
CFG.update({'vp': {'a': '1233', 'b': '2322'}, 'vp0': {'a': '2233', 'b': '2232'}, 'kg': {'a': 'ssvs', 'b': 'ssvs'}, 'kg0': {'a': 'ssvv', 'b': 'svss'}, 'cp': {'a': '1212', 'b': '2111'}, 'eng': {'ou': 's', 'off': 'v', 'pf': 'v', 'ko': 's', 'ov': 'v', 'ex': 's'},
"order": "dk0a kg1a kg2a kg3a ksa pfa kta js2a kg0a kua poa vg0b vg1b ora x2a vg3b oua ola ofa pena koa vg2b ab0b kpa df1a ab3b pd1b cb0a cb1a cb2a ab1b uu0a df3a eqa pfb ab2b js0a uu1a kg2b uu2a dk0b cb3a dk1b kg3b js1a uu3a js3a ppa ppb ksb ova kg0b ktb js2b zza kub obpa aca vaa kg1b pob pxa yba eea orb jua wra olb ofra exa oub eqb ofb js0b wwa kob offa js3b xfa kpb df0b cb1b x2b cb0b loa nua cb2b penb senda uu0b cb3b uu1b uu2b js1b uu3b jub ovb acb lsa zzb obpb vab sua pxb ofrb eeb exb ybb offb wrb lob xfb +vg3a wwb sc0a lsb +vg2a nub sc1a +pd3a sendb +vg0a +pd2a +ab3a sub +vg1a +ab2a sc0b +ab1a +ab0a +dk1a sc1b",
"first": "sj qg iq qm ncn pi0 kc yx0_1 ys1 ys2 sd yx0_13 yx0_15 yx0_8 yx0_12 pi2 yx0_14 yx0_6 yx0_9 yx0_11 yx0_2 lu0a yx0_4 yx0_7 c0 yx0_5 bca pi4 c1 yx0_3 eye yx0_10 tri c2 c3 n15 yx0_0 neye c5 c4 w1 c9 blk wo vg2a vg0a vg0b vg3a pd2a vg1a w16 ab0a t1 t2 tm yx1_0 yx1_11 pd3a yx1_6 vg1b ab2a yx1_7 ab3a vg3b ab1a yx1_15 dk1a vg2b yx1_1 e1 c10 dk0a yx1_5 ab0b pd2b yx1_13 ab3b ksa pfa ab2b ex0 yx1_14 pe kta ab1b k3 pfb dk1b nsh kua bcb kg0a yx1_9 dk0b poa kg3a ppa yx1_12 w2 ora c7 c8 kg1a yx1_8 ola x2a kg2a ppb yx1_2 ofa oua spr1 js3a kg3b yx1_10 ksb js2a k2 yx1_3 ktb js0a koa js1a c6 kg2b yx1_4 kg1b df1a kpa cb1a eqa kub cb0a kg0b df3a Kx pob k1 cb2a cb3a orb js2b olb uu0a aca uu1a oub czr js1b uu2a uu3a dh kob js0b wob ish eye4 kpb spr0 df0b pena ova sk ofb cb2b zza obpa cb0b k4 nis ncr vaa penb cb1b uu0b jua pxa ofra cb3b yba uu1b offa uu2b eqb wra eea exa uu3b wwa xfa ovb loa nua zzb js3b x2b lsa senda vab obpb jub acb sua pxb ofrb eeb exb offb xfb lob ybb sc0a lsb wrb sc1a wwb sub sc0b nub sc1b sendb",
"last": "ypa ypb dk0a kg3a kg2a pfa kg1a ksa kta kg0a kua vg3b vg1b poa vg0b ora ab3b ola ppa pd1b vg2b oua ab0b x2a koa eqa js1a ab1b pfb js3a kpa df1a js2a ab2b cb0a dk0b cb1a ppb dk1b js0a ofa cb2a kg0b df3a ksb uu0a uu1a cb3a ktb uu2a kub kg1b uu3a pob aca ova orb kg3b kg2b zza olb obpa oub vaa pena js1b kob eqb eea penb pxa kpb df0b cb1b ofra cb0b x2b cb2b ofb loa exa cb3b jua uu0b uu1b js3b uu2b offa uu3b lsa js2b ovb js0b sua zzb obpb acb vab pxb ofrb eeb exb jub ybb offb xfa xfb lob wrb yba sc0a wwb lsb wra sc1a wwa sub nub sc0b sendb nua sc1b senda rk fold ok yk"})
CFG.update({'vp': {'a': '2233', 'b': '2322'}, 'vp0': {'a': '2232', 'b': '2332'}, 'kg': {'a': 'ssvs', 'b': 'ssvs'}, 'kg0': {'a': 'ssvv', 'b': 'svss'}, 'cp': {'a': '1212', 'b': '2111'}, 'eng': {'ou': 's', 'off': 's', 'pf': 'v', 'ko': 's', 'ov': 'v', 'ex': 's'}, 'opt': {'dk': 0, 'or': 0, 'ofr': 0, 'm1': 0, 'fine': 0, 'jf': 0}, 'order': 'dk1a pfa vg1b kg2a dk0a kg1a ksa pd1b pfb kta js2a kg0a ppa kua poa vg3b kg3a ora x2a vg0b oua ofa koa ab3b js0a df1a vg2b ab1b kpa cb1a cb0a ab0b cb2a df3a ab2b uu0a kg2b dk0b cb3a ola dk1b pena eqa uu1a js3a kg3b uu2a ksb uu3a js1a ppb ktb ova kg1b kub js2b zza pob obpa aca kg0b vaa orb eea pxa olb ofra oub exa eqb ofb js0b kob js3b offa jua kpb df0b xfa cb2b yba x2b cb0b cb1b loa penb b0a cb3b uu0b uu1b uu2b m1a uu3b nua ovb senda js1b lsa zzb obpb acb vab pxb ofrb eeb exb b0b offb ybb lob xfb +vg3a sua m1b sc0a jub nub +vg2a lsb +pd2b +pd3a sc1a sendb +vg1a +ab3a +pd2a sub +vg0a +ab1a +ab2a sc0b +ab0a sc1b', 'first': 'pi0 iq c0 sj ncn yx0_7 yx0_14 yx0_3 bca qm yx0_1 yx0_4 yx0_6 qg pi2 eye kc yx0_5 ys1 ys2 yx0_10 yx0_11 yx0_0 lu0a pi4 c3 yx0_13 yx0_9 c4 yx0_12 n15 c1 sd yx0_15 c5 tri yx0_8 neye pfa c7 c2 yx0_2 blk w1 vg3a vg1b vg1a w16 t1 t2 tm yx1_0 yx1_1 yx1_2 yx1_3 yx1_4 yx1_5 yx1_6 yx1_7 yx1_8 yx1_9 yx1_10 yx1_11 yx1_12 yx1_13 yx1_14 yx1_15 pd1b ab3a vg0a vg2a vg0b ab1a pd2a ab0a vg3b ab2a c10 ab1b c9 dk1a c8 vg2b dk0a ppa w2 ab3b ksa pd2b k3 e1 pfb k2 ab0b kta nsh ex0 ab2b kua dk0b kg3a kg1a dk1b poa ppb kg0a k4 ksb kg2a ola ora x2a wo oua kg1b kg3b eqa koa js3a kg2b ktb ish df1a js2a kpa kub bcb spr1 cb1a pob cb0a kg0b df3a Kx cb2a orb ofa cb3a js1a uu0a uu1a js0a oub pe olb wob uu2a dh kob uu3a js0b czr js2b c6 kpb k1 df0b ova ncr aca jua eqb penb zza cb1b obpa ofb cb0b vaa cb2b pena ofra cb3b pxa uu0b offa uu1b exa eea uu2b spr0 uu3b yba xfa b0a ovb x2b js1b m1a zzb js3b obpb nua vab loa jub sk senda acb eeb ofrb ybb pxb lsa offb exb sua lob xfb b0b lsb sc0a sub m1b sc1a nub sc0b sendb sc1b', 'last': 'ypa ypb dk1a vg3b vg1b dk0a kg3a ksa pfa pd1b kta kg2a kg1a ppa kua kg0a poa vg0b ola ora ab3b x2a js2a oua ab1b eqa vg2b koa ab0b pfb js1a df1a ab2b js3a kpa dk0b cb0a cb1a dk1b ofa cb2a kg0b ppb df3a ksb uu0a js0a uu1a cb3a ktb uu2a kub kg1b pob uu3a olb ova orb kg3b kg2b zza obpa oub vaa pena eqb aca kob ofra eea kpb pxa df0b cb1b exa loa ofb cb0b cb2b penb cb3b offa uu0b uu1b uu2b js1b js0b uu3b x2b js3b ovb js2b xfa zzb obpb jub acb jua vab lsa pxb ofrb eeb exb yba ybb sua offb b0a xfb lob m1a b0b sc0a lsb sc1a sub nua sc0b senda m1b sc1b nub rk sendb fold ok yk'})
CFG.update({'vp': {'a': '2233', 'b': '2322'}, 'vp0': {'a': '2232', 'b': '2332'}, 'kg': {'a': 'ssvs', 'b': 'ssvs'}, 'kg0': {'a': 'ssvs', 'b': 'sssv'}, 'cp': {'a': '1212', 'b': '2111'}, 'eng': {'ou': 's', 'off': 's', 'pf': 'v', 'ko': 's', 'ov': 'v', 'ex': 's'}, 'opt': {'dk': 0, 'or': 0, 'ofr': 0, 'm1': 0, 'fine': 0, 'jf': 0, 'py': 1, 'obs': 1}, 'order': 'vg1b pfa pfb dk0a kg2a kg0a pd1b ksa kta js2a kg1a kua poa kg3a js0a vg3b ora ppb x2a oua ola vg2b koa ab3b df1a vg0b ab1b kpa cb1a cb0a ab0b cb2a df3a ab2b eqa dk0b js1a cb3a kg2b dk1b pena uu0a kg0b uu1a ksb uu2a js3a ppa uu3a ktb kg3b kub ova pob zza js2b obpa kg1b aca orb vaa js0b pxa olb obsa ofra js3b oub exa eqb kob eea offa jua kpb b0a xfa df0b cb1b x2b cb0b yba cb2b penb cb3b uu0b uu1b m1a uu2b js1b uu3b nua loa ovb senda acb lsa zzb pxb obpb vab exb sua jub obsb ofrb eeb b0b ybb offb xfb +vg3a lob m1b sc0a +vg2a nub +vg1a +pd3a sendb +ab3a lsb +pd2a sc1a sub +ab1a +vg0a +ab2a sc0b +ab0a +dk1a sc1b', 'first': 'pi0 sj iq ncn yx0_2 ys1 ys2 yx0_7 yx0_10 yx0_8 pi4 c3 yx0_5 pi2 bca c4 c0 yx0_3 yx0_1 yx0_13 qg c1 yx0_11 yx0_0 qm c8 yx0_12 eye tri yx0_9 lu0a kc w1 c7 n15 pfa yx0_15 w16 yx0_6 c5 ppa yx0_14 neye yx0_4 blk t1 t2 tm yx1_0 yx1_1 yx1_2 yx1_3 yx1_4 yx1_5 yx1_6 yx1_7 yx1_8 yx1_9 yx1_10 yx1_11 yx1_12 yx1_13 yx1_14 yx1_15 sd vg1a vg1b vg3b vg2a pd1b vg0a vg2b pd2a vg3a ab1a ab0a ex0 ab2a vg0b dk0a ab3a ab1b c9 msk dk1a c10 ab3b pd2b ab0b w2 msk7 msk0 dk0b ab2b c2 ksa k2 e1 nsh msk1 kg1a kta kg2a dk1b kg0a kua ish poa bcb kg3a ora pfb ksb ola ktb msk5 js2a oua kub wo koa pob msk4 msk6 kg3b msk3 kg2b kpa df1a orb k4 cb1a ppb cb0a oub eqa msk2 kg0b cb2a uu0a df3a js3a olb x2a kob js0a uu1a cb3a js0b uu2a eqb js2b kg1b js1a kpb uu3a Kx k1 aca ova czr sk spr1 pe df0b cb1b c6 dh wob zza pena js1b cb0b obpa vaa cb2b b0a pxa ncr jua uu0b exa obsa penb cb3b uu1b ofra spr0 eea uu2b uu3b offa yba js3b ovb x2b xfa jub acb zzb obpb m1a loa vab obsb nua ofrb eeb senda pxb offb lsa exb lob sua xfb ybb b0b lsb sc0a m1b sub sc1a nub sc0b sendb sc1b', 'last': 'ypa ypb vg1b vg3b dk0a kg3a ksa pfa kta kg0a kua poa vg0b kg1a ora pd1b kg2a oua ppa x2a ab3b ola koa pfb vg2b ab1b kpa df1a ab0b js2a js1a ab2b cb0a dk0b cb1a cb2a dk1b kg0b df3a ksb js0a ppb uu0a js3a uu1a cb3a uu2a ktb eqa kg3b kub uu3a pob aca ova kg1b olb kg2b orb obpa zza oub obsa eqb vaa kob eea pena kpb df0b cb1b loa cb0b x2b cb2b penb cb3b jua uu0b pxa uu1b uu2b js3b exa js1b uu3b ofra js0b ovb js2b offa zzb obpb jub acb vab obsb pxb xfa ofrb lsa exb eeb b0a yba offb ybb sua xfb lob m1a b0b sc0a lsb sc1a sub nua sc0b m1b sc1b nub rk sendb senda fold ok yk'})

S, P = "sbuf", "psum"
SCRATCH = {
    "vt": (S, [128, W], "bfloat16"), "ck": (S, [128, K0 + W + G], "int32"),
    "nm": (S, [128, R], "int32"), "ys": (S, [128, 4 * R], "bfloat16"), "yx": (S, [128, 4 * W], "bfloat16"),
    "lu": (S, [128, RO * R], "uint16"), "nu": (S, [128, RO * R], "uint16"), "nf": (S, [128, R], "float32"), "op": (S, [128, R], "float32"),
    "iq": (S, [128, R], "float32"), "qm": (S, [128, 128], "float32"), "qg": (S, [128, 128], "float32"),
    "pi": (S, [128, 8], "int32"), "col": (S, [128, 16], "float32"),
    "kc": (S, [128, 128], "bfloat16"), "sd": (S, [128, 128], "float32"), "sj": (S, [128, 2048], "bfloat16"),
    "e1": (S, [128, 32], "bfloat16"), "pe": (S, [128, 32], "bfloat16"), "ncn": (S, [128, R], "float16"), "ncr": (S, [128, 16], "float16"),
    "msk": (S, [128, 320], "bfloat16"), "obs": (S, [128, R], "float32"), "tri": (S, [128, 16], "bfloat16"), "eye4": (S, [128, 128], "float32"), "spr": (S, [128, 8], "float32"),
    "sk": (S, [128, 128], "bfloat16"), "ls": (S, [128, R], "float32"), "k3": (S, [128, 8], "bfloat16"),
    "pf": (S, [128, R], "float16"), "ks": (S, [128, R], "float32"), "kt": (S, [128, 16], "float32"),
    "osn": (S, [128, R], "float16"), "fs": (S, [128, R], "float16"), "wr": (S, [128, R], "float32"),
    "ku": (S, [128, 16], "uint16"), "ou": (S, [128, 16], "uint16"), "off": (S, [128, 16], "uint16"), "su": (S, [128, 16], "uint16"),
    "po": (S, [128, R], "float16"), "pen": (S, [128, R], "bfloat16"), "ko": (S, [128, R], "float16"), "eq": (S, [128, R], "bfloat16"),
    "ov": (S, [128, R], "bfloat16"), "va": (S, [128, R], "float16"), "xf": (S, [128, R], "float32"), "m1": (S, [128, R], "float32"),
    "ac": (S, [128, R], "float16"), "ju": (S, [128, R], "float32"), "ee": (S, [128, 640], "bfloat16"),
    "vq": (S, [128, W], "bfloat16"), "vx": (S, [128, 16, 256], "bfloat16"), "ab": (S, [128, 16, 16, 16], "bfloat16"),
    "kg": (S, [128, W], "float16"), "js": (S, [128, W], "float16"), "cb": (S, [128, W], "bfloat16"), "bc": (S, [128, 4], "float32"),
    "rk": (S, [128, W], "float16"), "ok": (S, [128, E], "float32"),
}
for _n in ("eye", "neye", "n15", "blk", "ish", "nsh", "t1", "t2", "tm", "czr", "k1", "k2", "dg", "nis", "wob", "dh", "k4"):
    SCRATCH[_n] = (S, [128, 128], "bfloat16")
for _n in ("w1", "w2", "w16", "wo"):
    SCRATCH[_n] = (S, [128, 144], "bfloat16")
for _b in range(8):
    SCRATCH["ps%d" % _b] = (P, [128, 512], "float32")

SEMAPHORES = (["cv", "cs", "ct", "cg", "sent", "l_nm", "l_ys", "l_v", "l_k", "st", "y1", "y2", "y3"]
              + ["st" + c for c in PARTS] + ["ar%d%s" % (t, c) for t in range(1, 7) for c in PARTS])

EST = {"cy": 0.83, "g": 1.56, "sc": 3.8, "lat": 240.0, "v": 15.0, "s": 20.0, "pe": 0.33, "pf": 0.0, "lv": 5500.0, "lk": 11500.0}


def vt_(n):
    return EST["v"] + max(64.0, n) * EST["cy"]


def st_(n):
    return EST["s"] + max(64.0, n) * EST["cy"]


def ga_(n, q):
    return (55.0 if q == "v" else 70.0) + n * EST["g"] * EST["cy"]


def pe_(*ns):
    return sum(EST["pf"] + max(64, n) * EST["pe"] for n in ns)


def bits(engines):
    m = 0
    for e in engines:
        m |= 1 << e
    return m


def build(g, core, T, topo):
    rank = T.rank_of(core)
    cores = T.cores
    ops = []
    ph = [-1]
    V, Sc, Pe = g.vector, g.scalar, g.tensor
    O, eng = CFG["opt"], CFG["eng"]
    first = {c: R - C * (i + 1) for i, c in enumerate(PARTS)}

    def op(q, dur, rd, wr, fn, banks=(), sig=None, fin=0.0, name=None, free=()):
        ops.append({"q": q, "dur": dur, "rd": list(rd), "wr": list(wr), "fn": fn, "banks": tuple(banks), "sig": sig, "fin": fin,
                    "name": name or wr[0], "ph": ph[0], "free": set(free)})

    def v(n, rd, wr, fn, banks=(), name=None):
        op("v", vt_(n), rd, wr, fn, banks, name=name)

    def s(n, rd, wr, fn, banks=(), name=None):
        op("s", st_(n), rd, wr, fn, banks, name=name)

    def mm(rd, wr, bank, groups, name=None, free=(), opens=True, closes=True):
        def fn():
            return [Pe.matmul(o, l, r, opens and i == 0, closes and i == len(grp) - 1) for grp in groups for i, (o, l, r, _) in enumerate(grp)]
        op("t", pe_(*[x[3] for grp in groups for x in grp]), rd, wr, fn, [bank], name=name, free=free)
        ops[-1]["n"] = sum(len(grp) for grp in groups)

    def lin(q, n, rd, wr, out, in_, add, banks=(), name=None, half=False):
        if q == "v":
            v(n / 2 if half else n, rd, wr, lambda: V.tensor_scalar(out, in_, add, None, A.add), banks, name)
        else:
            s(n, rd, wr, lambda: Sc.activation(out, in_, F.Identity, bias=add), banks, name)

    def gat(q, n, rd, wr, out, win, add, name=None):
        if q == "v":
            op(q, ga_(n, q), rd, wr, lambda: V.tensor_scalar(out, win(), add, None, A.add), name=name)
        else:
            op(q, ga_(n, q), rd, wr, lambda: Sc.activation(out, win(), F.Identity, bias=add), name=name)

    def dma(out, in_, rd, wr, sem, fin):
        op("y", 60.0, rd, wr, lambda: g.sync.dma_start(out, in_).then_inc(T.sem[sem], 16), sig=(sem, 16), fin=fin)

    sent = [0]

    dma(T.ys[:, 0:R], T.seen[:], [], ["ys0"], "l_ys", 2000.0)
    dma(T.nm[:], T.nam[:], [], ["nm"], "l_nm", 2200.0)
    dma(T.vt[:], T.val[:], [], ["vt"], "l_v", EST["lv"])
    dma(T.ck[:, K0:K0 + W], T.clk[:], [], ["K"], "l_k", EST["lk"])
    for o in ops:
        o["first"] = True

    def common(src):
        en = None
        for d in cores:
            if d != src:
                e = topo.engines(src, d)
                en = e if en is None else [x for x in en if x in e]
        return en

    def send_y(js):
        en = common(core) if len(js) > 1 else topo.engines(core, cores[(rank + js[0]) % N])
        k = len(en) // len(js)
        tr = []
        for i, j in enumerate(js):
            d = cores[(rank + j) % N]
            assert topo.may_write(core, d)
            rid, pid, _ = topo.addr(d)
            tr.append(RemoteDMATransfer(dst_ids=[DstId(rid=rid, pnc=pid)], dma_engine_mask=bits(en[i * k:(i + 1) * k]),
                                        remote_sem=T.sem["y%d" % j], src=T.ys[:, 0:R], dst=T.ys[:, j * R:(j + 1) * R]))
        g.remote_dma_fused(tr, local_sem=T.sem.sent)
        sent[0] += k * len(js)
    for js in ([1], [2, 3]):
        op("g", 1500.0 / js[0] ** 2, ["ys0"], ["ys%d" % j for j in js], lambda js=js: send_y(js),
           sig={"ys%d" % j: ("y%d" % j, len(common(cores[(rank - j) % N])) // 2 if j > 1 else len(topo.engines(cores[rank - 1], core))) for j in js}, fin=5000.0)

    flag = {"allow_small_or_imprecise_dtypes": True}
    op("g", 140.0, [], ["pi0"], lambda: g.iota(T.pi[:, 0:2], [[1, 2]], 0, 1))
    op("g", 560.0, [], ["iq"], lambda: g.iota(T.iq[:], [[1, R]], 0, 0, **flag))
    op("g", 350.0, [], ["qm"], lambda: g.iota(T.qm[:], [[0, 8], [1, 16]], 0, 0, **flag))
    op("g", 350.0, [], ["qg"], lambda: g.iota(T.qg[:], [[16, 8], [0, 16]], 0, 0, **flag))
    col = lambda i: T.col[:, i:i + 1]
    sg, hb = (1.0, 0.5) if eng["ov"] == "s" else (0.0, 1.0)
    v(1, ["pi0"], ["pi2"], lambda: V.tensor_scalar(T.pi[:, 2:4], T.pi[:, 0:2], 15, None, A.bitwise_and))
    v(1, ["pi0"], ["pi4"], lambda: V.tensor_scalar(T.pi[:, 4:5], T.pi[:, 0:1], 112, None, A.bitwise_and))
    v(1, ["pi0"], ["c0"], lambda: V.tensor_copy(col(0), T.pi[:, 0:1]))
    v(1, ["pi2"], ["c1"], lambda: V.tensor_copy(col(1), T.pi[:, 2:3]))
    v(1, ["pi2", "pi4"], ["c2"], lambda: V.tensor_tensor(col(2), T.pi[:, 3:4], T.pi[:, 4:5], A.add))
    v(1, ["pi4"], ["c3"], lambda: V.tensor_copy(col(3), T.pi[:, 4:5]))
    for i, (a, b, src) in enumerate([(1.0, 15.0, 3), (1.0, 8.0, 1), (2.0, -2048.0 - K0, 1), (-B / 2 * sg, -B * hb, 1), (1.0, float(W), 1)]):
        s(1, ["c%d" % src], ["c%d" % (4 + i)], lambda i=i, a=a, b=b, src=src: Sc.activation(col(4 + i), col(src), F.Identity, bias=b, scale=a))
    q128 = T.iq[:, 0:128]
    ts = lambda out, in_, a, b, o0, o1: (lambda: V.tensor_scalar(out, in_, a, b, o0, o1))
    sc = lambda out, in_, a, b=0.0: (lambda: Sc.activation(out, in_, F.Identity, bias=b, scale=a))
    v(128, ["iq", "c0"], ["eye"], ts(T.eye[:], q128, col(0), 1.0, A.is_equal, A.mult))
    s(128, ["eye"], ["neye"], sc(T.neye[:], T.eye[:], -1.0))
    s(128, ["eye"], ["n15"], sc(T.n15[:], T.eye[:], -15.0))
    v(128, ["qg", "c3"], ["blk"], ts(T.blk[:], T.qg[:], col(3), 1.0, A.is_equal, A.mult))
    v(128, ["iq", "c2"], ["nsh"], ts(T.nsh[:], q128, col(2), -1.0, A.is_equal, A.mult))
    v(256, ["eye", "nsh"], ["ish"], lambda: V.tensor_tensor(T.ish[:], T.eye[:], T.nsh[:], A.subtract))
    s(128, ["blk"], ["t1"], sc(T.t1[:], T.blk[:], -B * hb))
    op("g", 390.0, ["t1"], ["t2"], lambda: g.affine_select(T.t2[:], T.t1[:], [[1, 128]], A.is_gt, 0.0, 0, -1))
    op("g", 390.0, ["t2"], ["tm"], lambda: g.affine_select(T.tm[:], T.t2[:], [[1, 128]], A.not_equal, B * hb, 0, -1))
    s(C, ["iq", "c7"], ["czr"], lambda: Sc.activation(T.czr[:, 0:C], T.iq[:, 0:C], F.Identity, bias=col(7), scale=0.0))
    v(64, [], ["k1"], lambda: V.memset(T.k1[:], 2048.0 - 2 * B))
    v(144, ["iq", "c4"], ["w1"], ts(T.w1[:], T.iq[:, 0:144], col(4), 1.0, A.is_equal, A.mult))
    for nme, x in (("w16", 16.0), ("w2", 2.0), ("wo", WO)):
        s(144, ["w1"], [nme], sc(T[nme][:], T.w1[:], x))
    sel = lambda w, nl: T[w][:, 15 - nl:143 - nl]
    s(C, ["qm"], ["kc"], sc(T.kc[:, 0:C], T.qm[:, 0:C], 1.0, -7.75))
    v(C, ["qm"], ["sd"], ts(T.sd[:, 0:C], T.qm[:, 0:C], 0.0, 1e9, A.is_equal, A.mult))
    jn = JN = 256 if O["jf"] else 512
    v(jn / 2, [], ["sj"], lambda: V.memset(T.sj[:, 0:jn], 0.0))
    v(64, [], ["sj"], lambda: V.memset(T.sj[:, 0:jn:16], -16384.0))
    v(32, ["iq", "c5"], ["e1"], ts(T.e1[:], T.iq[:, 0:32], col(5), 1.0, A.is_equal, A.mult))
    s(32, ["e1"], ["pe"], sc(T.pe[:], T.e1[:], -B, B))
    s(R, ["iq"], ["ncn"], sc(T.ncn[:], T.iq[:], 2.0, -2048.0 - K0))
    v(16, ["iq", "c1"], ["tri"], ts(T.tri[:], T.iq[:, 0:16], col(1), 0.5, A.is_le, A.mult))
    s(128, ["blk"], ["wob"], sc(T.wob[:], T.blk[:], WO))
    v(C, ["qm", "c1"], ["k4"], ts(T.k4[:, 0:C], T.qm[:, 0:C], col(1), 1.0, A.is_equal, A.mult))
    s(C, ["k4"], ["dh"], sc(T.dh[:, 0:C], T.k4[:, 0:C], 2.0 ** 20 + 16 * WO * sg + 2048.0, -2.0 ** 20))
    v(160, [], ["msk"], lambda: V.memset(T.msk[:], 2048.0))
    z = 0
    for x in range(C // 16):
        s(16, ["msk", "tri"], ["msk%d" % x], sc(T.msk[:, z:z + 16], T.tri[:], -16384.0, 2048.0))
        z += (x // 4 + 1) * G - 16 * x
    v(C, ["qm"], ["sk"], ts(T.sk[:, 0:C], T.qm[:, 0:C], 0.0, -2.0 ** 21, A.is_equal, A.mult))
    if not O["obs"]:
        v(8, [], ["k3"], lambda: V.memset(T.k3[:], 16 * WO * sg + 2048.0))
    for x in range(C // G):
        s(4, ["iq", "c8"], ["spr%d" % x], lambda x=x: Sc.activation(T.spr[:, 4 * x:4 * x + 4], T.iq[:, 0:4], F.Identity, bias=col(8), scale=16.0))
    if O["or"] or O["ofr"]:
        v(C, ["qm", "c1"], ["dg"], ts(T.dg[:, 0:C], T.qm[:, 0:C], col(1), -B, A.not_equal, A.mult))
    if not O["ofr"]:
        s(16, ["iq", "c6"], ["ncr"], lambda: Sc.activation(T.ncr[:], T.iq[:, 0:16], F.Identity, bias=col(6), scale=32.0))
    if O["m1"]:
        s(128, ["eye"], ["eye4"], sc(T.eye4[:], T.eye[:], 1.0))
        v(256, ["nsh", "ish"], ["nis"], lambda: V.tensor_tensor(T.nis[:], T.nsh[:], T.ish[:], A.subtract))
    v(64, [], ["k2"], lambda: V.memset(T.k2[:], 2048.0))
    v(K0, [], ["ex" + c for c in PARTS], lambda: V.memset(T.ck[:, 0:K0], 0), name="ex0")
    v(G, [], ["Kx"], lambda: V.memset(T.ck[:, K0 + W:], 0))
    for i, c in enumerate(PARTS):
        bc, cp = T.bc[:, i:i + 1], CFG["cp"][c]
        v(1, [], ["bc" + c], lambda bc=bc: V.memset(bc, -23.0))
        for q in range(len(cp)):
            if cp[q] == "2":
                v(1, ["c1"], ["c9"], ts(col(9), col(1), 16.0 * q / len(cp) - 0.5, 16.0, A.is_gt, A.mult))
                v(1, ["c1"], ["c10"], ts(col(10), col(1), 16.0 * (q + 1) / len(cp) - 0.5, -16.0, A.is_gt, A.mult))
                v(1, ["c9", "c10", "bc" + c], ["bc" + c], ts(bc, bc, col(9), col(10), A.add, A.add))
    v(R, ["nm"], ["lu0" + c for c in PARTS], lambda: V.tensor_copy(T.lu[:, 0:R], T.nm[:]))
    used = lambda names: [first[c] // 32 + x for c in PARTS for x in range(C // 32) if O["py"] or any(CFG[n][c][x] != "3" for n in names)]
    for j in range(N):
        xs = used(["vp", "vp0"] if j == 0 else ["vp"]) or [0]
        a, b = 32 * min(xs), 32 * max(xs) + 32
        for k in range(16):
            out, in_ = T.yx[:, j * W + 16 * a + k:j * W + 16 * b:16], T.ys[:, j * R + a:j * R + b]
            if j == 0:
                v((b - a) / 2, ["ys0"], ["yx0_%d" % k], lambda out=out, in_=in_: V.tensor_copy(out, in_))
            else:
                op("g", 170.0 + 1.66 * (b - a), ["ys%d" % j], ["yx%d_%d" % (j, k)],
                   lambda out=out, in_=in_, n=b - a: g.affine_select(out, in_, [[0, n]], A.is_gt, 0.0, 1, 0))
                ops[-1]["after"] = j - 2
    cbank = [0]
    KW = T.ck[:, K0:K0 + W]
    NB = C // 16

    def part(t, c):
        r0, ix = first[c], PARTS.index(c)
        rs, ns, ends = slice(r0, r0 + C), slice(r0 // 16, r0 // 16 + NB), slice(r0 + 15, r0 + C, 16)
        k_ = lambda n: n + c
        n0, e0 = t * R + r0, 16 * r0
        pu = "lu%d%s" % (t, c)
        PF = T.pf[:, rs]
        b1, b2, z2 = (3 + ix, 5 + ix, 0) if C > 64 else (3 + ix, 3 + ix, 256)
        p1, p2 = T["ps%d" % b1], T["ps%d" % b2]
        uu, zz, orr, ofr = p1[:, C:2 * C], p1[:, 2 * C:3 * C], p1[:, 3 * C:3 * C + NB], p1[:, 3 * C + 8:3 * C + 8 + NB]
        ol, pp, b0, kp = [p2[:, z2 + i * C:z2 + (i + 1) * C] for i in range(4)]
        j = t % N
        yxs = ["yx%d_%d" % (j, k) for k in range(16)]
        vp, kq, cp = CFG["vp0" if t == 0 else "vp"][c], CFG["kg0" if t == 0 else "kg"][c], CFG["cp"][c]
        lin(eng["pf"], C, [pu], [k_("pf")], PF, T.lu[:, n0:n0 + C], -2048.0, half=True)
        for x in range(C // 32):
            win = lambda x=x: T.vt[:, 0:W].indirect(T.lu[:, n0 + x * 32:n0 + (x + 1) * 32])
            y0 = e0 + x * 512
            yy, ab, vq = T.yx[:, j * W + y0:j * W + y0 + 512], T.ab[:, y0 // 256:y0 // 256 + 2], T.vq[:, y0:y0 + 512]
            if vp[x] == "1":
                for y in range(2):
                    a = y0 + y * 256
                    op("v", ga_(256, "v"), [pu, "vt"] + yxs, [k_("vq%d%d" % (x, y))],
                       lambda a=a: V.tensor_tensor(T.vx[:, a // 256, :], T.vt[:, 0:W].indirect(T.lu[:, t * R + a // 16:t * R + a // 16 + 16]),
                                                   T.yx[:, j * W + a:j * W + a + 256], A.subtract), name=k_("vg%d" % x))
                v(256, [k_("vq%d%d" % (x, y)) for y in range(2)], [k_("ab%d" % x)],
                  ts(ab, T.vx[:, y0 // 256:y0 // 256 + 2, :], 0.0, -2.0, A.min, A.mult))
            elif vp[x] == "2":
                nv = 2 if O["fine"] else 1
                for y in range(nv):
                    a, n = y0 + y * 512 // nv, 512 // nv
                    op("v", ga_(n, "v"), [pu, "vt"] + yxs, [k_("vq%d%d" % (x, y))],
                       lambda a=a, n=n: V.tensor_tensor(T.vq[:, a:a + n], T.vt[:, 0:W].indirect(T.lu[:, t * R + a // 16:t * R + (a + n) // 16]),
                                                        T.yx[:, j * W + a:j * W + a + n], A.subtract), name=k_("vg%d" % x))
                s(512, [k_("vq%d%d" % (x, y)) for y in range(2)], [k_("ab%d" % x)], lambda ab=ab, vq=vq: Sc.activation(ab, vq, F.Abs))
            else:
                gat("s", 512, [pu, "vt"], [k_("vq%d%d" % (x, y)) for y in range(2)], vq, win, 0.0, name=k_("vg%d" % x))
                bk = cbank[0] % 2
                cbank[0] += 1
                pd = T["ps%d" % bk]
                y1 = T.ys[:, j * R + r0 + 32 * x:j * R + r0 + 32 * x + 32]
                mm([k_("vq%d0" % x), k_("vq%d1" % x), "eye", "neye", "ys%d" % j] + (yxs if O["py"] else []), ["pd%d" % bk], bk,
                   [[(pd[:], T.eye[:], vq, 512)] + ([(pd[:], T.neye[:], yy, 512)] if O["py"] else [(pd[:, k::16], T.neye[:], y1, 32) for k in range(16)])],
                   name=k_("pd%d" % x))
                s(512, ["pd%d" % bk], [k_("ab%d" % x)], lambda ab=ab, pd=pd: Sc.activation(ab, pd[:], F.Abs), [bk])
        kn = 16 * C // len(kq)
        for x in range(len(kq)):
            cs = slice(e0 + x * kn, e0 + (x + 1) * kn)
            gat(kq[x], kn, [pu, "K"], [k_("kg%d" % x)], T.kg[:, cs],
                lambda x=x: KW.indirect(T.lu[:, n0 + x * kn // 16:n0 + (x + 1) * kn // 16]), -2048.0)
        for x in range(16 * C // JN):
            cs = slice(e0 + x * JN, e0 + (x + 1) * JN)
            v(JN / 2, [k_("kg%d" % (x * JN // kn)), "sj"], [k_("js%d" % x)],
              lambda cs=cs: V.tensor_tensor_scan(T.js[:, cs], T.sj[:, 0:JN], T.kg[:, cs], 0.0, A.add, A.max))
        kgs, jss = [k_("kg%d" % x) for x in range(len(kq))], [k_("js%d" % x) for x in range(16 * C // JN)]
        entry = lambda buf, k: buf[:, e0 + k:e0 + 16 * C:16]
        nd = 1 if O["dk"] or C == 64 else 2
        dw, nx = C // nd, C // 32 // nd
        for x in range(nd):
            d, h0 = p1[:, dw * x:dw * (x + 1)], r0 // 16 + 2 * nx * x
            grp = [(d, T.eye[:], T.kc[:, 0:dw], dw)] + [(d, sel("w16", nl), T.ab[:, h0:h0 + 2 * nx, nl, :], dw) for nl in range(16)]
            ones = [y for y in range(nx * x, nx * (x + 1)) if vp[y] == "1"]
            for a, b in ([(ones[0], ones[-1] + 1)] if ones and ones[-1] - ones[0] == len(ones) - 1 else [(y, y + 1) for y in ones]):
                grp += [(p1[:, 32 * a:32 * b], sel("w16", nl), T.vx[:, r0 // 16 + 2 * a:r0 // 16 + 2 * b, 16 * nl:16 * nl + 16], 32 * (b - a)) for nl in range(16)]
            mm([k_("ab%d" % y) for y in range(nx * x, nx * (x + 1))] + [k_("vq%d%d" % (y, z)) for y in ones for z in range(2)] + ["w16", "eye", "kc"],
               [k_("dk%d" % x)], b1, [grp])
        v(C, [k_("dk%d" % x) for x in range(nd)] + ["sd"], [k_("ks")], lambda: V.tensor_tensor_scan(T.ks[:, rs], T.sd[:, 0:C], p1[:, 0:C], 0.0, A.add, A.min), [b1])
        v(8, [k_("ks")], [k_("kt")], ts(T.kt[:, ns], T.ks[:, ends], M16, -M16 - 16.0, A.add, A.add))
        v(16, [k_("ks"), k_("kt")], [k_("ku")], lambda: V.tensor_tensor(T.ku[:, ns], T.ks[:, ends], T.kt[:, ns], A.subtract))
        po, pen = T.po[:, rs], T.pen[:, rs]
        op("v", ga_(C, "v"), [k_("ku"), k_("pf"), "e1"], [k_("po")], lambda: V.tensor_tensor(po, T.e1[:, 0:32].indirect(T.ku[:, ns]), PF, A.mult))
        gat("s", C, [k_("ku"), "pe"], [k_("pen")], pen, lambda: T.pe[:, 0:32].indirect(T.ku[:, ns]), 0.0)
        rows = lambda out, w, buf: [(out, sel(w, nl), buf[:, r0 + nl:r0 + C:16], NB) for nl in range(16)]
        if not O["or"]:
            mm([k_("po"), "w1"], [k_("or")], b1, [rows(orr, "w1", T.po)])
            lin(eng["ou"], 8, [k_("or")], [k_("ou")], T.ou[:, ns], orr, 2048.0, [b1])
            if not O["obs"]:
                lin("s", 8, [k_("or")], [k_("of")], T.osn[:, ends], orr, 0.0, [b1])
        else:
            mm([k_("po"), "blk", "eye", "dg"], [k_("zz")], b1, [[(zz, T.eye[:], T.dg[:, 0:C], C), (zz, T.blk[:], po, C)]], name=k_("or"))
            v(C, [k_("zz"), "sj"], [k_("of")], lambda: V.tensor_tensor_scan(T.osn[:, rs], T.sj[:, 0:C], zz, 0.0, A.add, A.max), [b1], name=k_("os"))
            lin(eng["ou"], 8, [k_("of")], [k_("ou")], T.ou[:, ns], T.osn[:, ends], 2048.0)
        gat(eng["ko"], C, [k_("ou"), "K"], [k_("ko")], T.ko[:, rs], lambda: KW.indirect(T.ou[:, ns]), -2048.0)
        mm([k_("po"), "blk"], [k_("ol")], b2, [[(ol, T.blk[:], po, C)]])
        v(C, [k_("ol"), k_("pf")], [k_("eq")], lambda: V.tensor_tensor(T.eq[:, rs], PF, ol, A.is_equal), [b2])
        if "1" in cp:
            mm([k_("ko"), "eye"], [k_("kp")], b2, [[(kp, T.eye[:], T.ko[:, rs], C)]])
        nq, grp, rd = len(cp), [], []
        for q in range(nq):
            ks_ = range(16 * q // nq, 16 * (q + 1) // nq)
            cb = lambda k, n=1: T.cb[:, e0 + k * C:e0 + (k + n) * C]
            if cp[q] == "1":
                for k in ks_:
                    v(C, kgs + [k_("kp")], [k_("cb%d" % k)], lambda k=k, cb=cb: V.tensor_tensor(cb(k), entry(T.kg, k), kp, A.is_ge), [b2], name=k_("cb%d" % q))
            else:
                pd = T.ps2
                mm(kgs + [k_("ko"), "eye", "neye"], ["pd2"], 2,
                   [[(pd[:, i * C:(i + 1) * C], T.eye[:], entry(T.kg, k), C), (pd[:, i * C:(i + 1) * C], T.neye[:], T.ko[:, rs], C)] for i, k in enumerate(ks_)], name=k_("df%d" % q))
                s(len(ks_) * C, ["pd2"], [k_("cb%d" % k) for k in ks_],
                  lambda ks_=ks_, cb=cb, pd=pd: Sc.activation(cb(ks_[0], len(ks_)), pd[:, 0:len(ks_) * C], F.Sign, bias=0.5), [2], name=k_("cb%d" % q))
            grp += [(uu, sel("w2" if cp[q] == "1" else "w1", k), cb(k), C) for k in ks_]
            rd += [k_("cb%d" % k) for k in ks_]
            if q == nq - 1:
                grp.insert(0, (uu, T.n15[:], T.eq[:, rs], C))
                rd.append(k_("eq"))
            if q == nq - 1 or b1 != b2:
                whole = b1 == b2
                mm(rd + ["w1", "w2", "n15"] + ([k_("ou"), k_("of")] if q == 0 else []), [k_("uu")], b1, [grp],
                   name=k_("uu%d" % q), free=[k_("uu")] if q and not whole else [], opens=q == 0 or whole, closes=q == nq - 1)
                grp, rd = [], []
        if eng["ov"] == "s":
            s(C, [k_("uu"), k_("bc")], [k_("ov")], lambda: Sc.activation(T.ov[:, rs], uu, F.Sign, bias=T.bc[:, ix:ix + 1]), [b1])
        else:
            v(C, [k_("uu"), k_("bc")], [k_("ov")], ts(T.ov[:, rs], uu, T.bc[:, ix:ix + 1], 0.0, A.add, A.is_gt), [b1])
        mm([k_("ov"), k_("pf"), "tm", "czr", "eye"], [k_("zz")], b1, [[(zz, T.eye[:], PF, C), (zz, T.eye[:], T.czr[:, 0:C], C), (zz, T.tm[:], T.ov[:, rs], C)]])
        v(C, [k_("zz"), "ncn"], [k_("va")], lambda: V.tensor_tensor(T.va[:, rs], T.ncn[:, rs], zz, A.max), [b1])
        if not O["ofr"]:
            mm([k_("va"), "w1", "n15", "ncr"], [k_("ofr")], b1, [[(ofr, T.n15[:], T.ncr[:, ns], 8)] + rows(ofr, "w1", T.va)])
            lin(eng["off"], 8, [k_("ofr")], [k_("off")], T.off[:, ns], ofr, 2048.0 + K0 - 2 * r0, [b1])
        else:
            mm([k_("va"), "blk", "eye", "dg", "n15", "ncn"], [k_("zz")], b1,
               [[(zz, T.eye[:], T.dg[:, 0:C], C), (zz, T.n15[:], T.ncn[:, rs], C), (zz, T.blk[:], T.va[:, rs], C)]], name=k_("ofr"))
            v(C, [k_("zz"), "sj"], [k_("fs")], lambda: V.tensor_tensor_scan(T.fs[:, rs], T.sj[:, 0:C], zz, 0.0, A.add, A.max), [b1])
            lin(eng["off"], 8, [k_("fs")], [k_("off")], T.off[:, ns], T.fs[:, ends], 2048.0 + K0 - 2 * r0)
        mm([k_("pf"), "eye"], [k_("pp")], b2, [[(pp, T.eye[:], PF, C)]])
        v(C, jss + [k_("pp")], [k_("ac")], lambda: V.tensor_tensor(T.ac[:, rs], entry(T.js, 15), pp, A.max), [b2])
        if eng["ex"] == "s" or not O["m1"]:
            mm([k_("ac"), k_("pen"), "eye"], [k_("pp")], b2, [[(pp, T.eye[:], T.ac[:, rs], C), (pp, T.eye[:], pen, C)]], name=k_("px"))
            lin("s", C, [k_("pp")], [k_("ex")], T.ck[:, 2 * r0:2 * r0 + 2 * C:2], pp, 2048.0, [b2])
        else:
            mm([k_("pen"), "eye", "k2"], [k_("b0")], b2, [[(b0, T.eye[:], T.k2[:, 0:C], C), (b0, T.eye[:], pen, C)]], name=k_("px"))
            v(C, [k_("ac"), k_("b0")], [k_("ex")], lambda: V.tensor_tensor(T.ck[:, 2 * r0:2 * r0 + 2 * C:2], T.ac[:, rs], b0, A.add), [b2])
        lin("s", C, jss, [k_("ju")], T.ju[:, rs], entry(T.js, 15), 2048.0)
        g0 = [(b0, T.eye[:], PF, C), (b0, T.eye[:], T.k1[:, 0:C], C), (b0, T.ish[:], pen, C)]
        if not O["m1"]:
            mm([k_("pf"), k_("pen"), "eye", "ish", "k1"], [k_("b0")], b2, [g0])
            mm([k_("va"), k_("pen"), "eye", "nsh", "k2", "n15", "ncn", "blk"], [k_("ol")], b2,
               [[(ol, T.eye[:], T.k2[:, 0:C], C), (ol, T.n15[:], T.ncn[:, rs], C), (ol, T.nsh[:], pen, C), (ol, T.blk[:], T.va[:, rs], C)]], name=k_("yb"))
        else:
            mm([k_("va"), k_("pen"), k_("pf"), "neye", "nis", "n15", "ncn", "blk"], [k_("ol")], b2,
               [[(ol, T.neye[:], PF, C), (ol, T.n15[:], T.ncn[:, rs], C), (ol, T.nis[:], pen, C), (ol, T.blk[:], T.va[:, rs], C)]], name=k_("yb"))
            s(C, [k_("ol")], [k_("wr")], lambda: Sc.activation(T.wr[:, rs], ol, F.Relu, bias=2 * B), [b2])
            mm([k_("pf"), k_("pen"), k_("wr"), "eye", "eye4", "ish", "k1"], [k_("b0")], b2, [g0 + [(b0, T.eye4[:], T.wr[:, rs], 4 * C)]], name=k_("ww"))
        op("v", ga_(C, "v"), [k_("off"), k_("pen"), "K"] + ["ex" + x for x in PARTS[:ix + 1]], [k_("xf")],
           lambda: V.tensor_tensor(T.xf[:, rs], T.ck[:, 2 * r0:K0 + W].indirect(T.off[:, ns]), pen, A.subtract))
        last = t == RO - 1
        if last:
            src, dst = T.nf[:, rs], T.op[:, rs]
        else:
            src, dst = T.nu[:, n0:n0 + C], T.lu[:, n0 + R:n0 + R + C]
        if not O["m1"]:
            v(C, [k_("xf"), k_("b0")], [k_("m1")], lambda: V.tensor_tensor(T.m1[:, rs], T.xf[:, rs], b0, A.max), [b2])
            v(C, [k_("m1"), k_("ol")], [k_("nu%d" % t)], lambda: V.tensor_tensor(src, T.m1[:, rs], ol, A.max), [b2], name=k_("nu"))
        else:
            v(C, [k_("xf"), k_("b0")], [k_("nu%d" % t)], lambda: V.tensor_tensor(src, T.xf[:, rs], b0, A.max), [b2], name=k_("nu"))
        hop = 1 if not last else -t
        to, frm = cores[(rank + hop) % N], cores[(rank - hop) % N]
        sem = "ar%d%s" % (t + 1, c)

        def send():
            assert topo.may_write(core, to)
            rid, pid, _ = topo.addr(to)
            en = topo.engines(core, to)
            g.remote_dma(dst, src, T.sem[sem], T.sem.sent, pid, rid, bits(en))
            sent[0] += len(en)
        op("g", 300.0, [k_("nu%d" % t)], ["lu%d%s" % (t + 1, c)], send, sig=(sem, len(topo.engines(frm, core))), fin=CFG["hop"], name=k_("send"))

        p7, y7, d7 = T.ps7, 0, ""
        if C == 64:
            y7, d7 = 256 * (ix % 2), "01"[ix % 2]
        obp = p7[:, y7 + 5 * C // 2:y7 + 5 * C // 2 + NB]
        seg, z = [], 0
        for x in range(NB):
            seg.append((16 * x, (x // 4 + 1) * G, z))
            z += (x // 4 + 1) * G - 16 * x
        ee = lambda z, n: T.ee[:, 5 * r0 // 2 + z:5 * r0 // 2 + z + n]
        mm([k_("po"), "eye", "blk"] + ["msk%d" % x for x in range(NB)], ["x2" + d7], 7,
           [[(p7[:, y7:y7 + z], T.eye[:], T.msk[:, 0:z], z)] + [(p7[:, y7 + z:y7 + z + b - a], T.blk[:], T.po[:, r0 + a:r0 + b], G) for a, b, z in seg]], name=k_("x2"))
        own = [(T.eye[:], T.dh[:, 0:C]), (T.blk[:], po), (T.wob[:], T.ov[:, rs])]
        if O["obs"]:
            ob7 = p7[:, 384:384 + C]
            mm([k_("po"), k_("ov"), "eye", "blk", "wob", "dh"], ["obp" + d7], 7, [[(ob7, l, r, C) for l, r in own]], name=k_("obp"))
            v(C, ["obp" + d7, "sk"], [k_("obs")], lambda: V.tensor_tensor_scan(T.obs[:, rs], T.sk[:, 0:C], ob7, 0.0, A.add, A.max), [7])
        else:
            mm([k_("of"), k_("ov"), "eye", "wo", "k3"], ["obp" + d7], 7,
               [[(obp, T.eye[:], T.osn[:, ends], 8), (obp, T.eye[:], T.k3[:, 0:NB], 8)] + rows(obp, "wo", T.ov)], name=k_("obp"))
        for x, (a, b, z) in enumerate(seg):
            y = y7 + 5 * C // 2 + x
            if O["obs"]:
                y = r0 + 16 * x + 15
                v(G, ["x2" + d7, k_("obs")], [k_("ee%d" % x)], ts(ee(z, b - a), p7[:, y7 + z:y7 + z + b - a], T.obs[:, y:y + 1], 1.0, A.is_equal, A.mult), [7], name=k_("ee"))
            else:
                v(G, ["x2" + d7, "obp" + d7], [k_("ee%d" % x)], ts(ee(z, b - a), p7[:, y7 + z:y7 + z + b - a], p7[:, y:y + 1], 1.0, A.is_equal, A.mult), [7], name=k_("ee"))
        mm([k_("ee%d" % x) for x in range(NB)] + [k_("po"), k_("ov"), "eye", "blk", "wob", "dh"], [k_("uu")], b1,
           [[(uu, l, r, C) for l, r in own] + [(p1[:, C + a:C + b], T.wob[:], ee(z, b - a), G) for a, b, z in seg]], name=k_("lo"))
        v(C, [k_("uu"), "sk"], [k_("ls")], lambda: V.tensor_tensor_scan(T.ls[:, rs], T.sk[:, 0:C], uu, 0.0, A.add, A.max), [b1])
        v(16, [k_("ls"), "spr0", "spr1"], [k_("su")], lambda: V.tensor_tensor(T.su[:, ns], T.ls[:, ends], T.spr[:, 0:NB], A.min))

    for t in range(RO):
        ph[0] = t
        for c in PARTS:
            part(t, c)
        for x in range(R // G - 1, -1, -1):
            c = PARTS[(R - 1 - x * G) // C]
            op("v", 55.0 + G * EST["sc"] * EST["cy"], ["su" + c, "ju" + c], ["K", "Kx"],
               lambda x=x: V.tensor_copy(T.ck[:, K0:K0 + W + G].indirect(T.su[:, 4 * x:4 * x + 4]), T.ju[:, x * G:(x + 1) * G]), name="sc%d%s" % ((R - 1 - x * G) % C // G, c))

    ph[0] = RO
    for b in range(8):
        x = slice(b * E, (b + 1) * E)
        lin("vs"[b % 2], E, ["K"], ["rk%d" % b], T.rk[:, x], T.ck[:, K0 + b * E:K0 + (b + 1) * E], -2048.0, name="rk")
        mm(["rk%d" % b, "eye"], ["pd1"], 1, [[(T.ps1[:], T.eye[:], T.rk[:, x], E)]], name="fold", free=["pd1"] if b else [], opens=b == 0, closes=b == 7)
    lin("v", E, ["pd1"], ["ok"], T.ok[:], T.ps1[:], 8 * 2048.0, [1])
    dma(T.yk[:], T.ok[:], ["ok"], ["yk"], "st", 2500.0)
    for c in PARTS:
        x = slice(first[c], first[c] + C)
        dma(T.yp[:, x], T.op[:, x], ["lu6" + c], ["yp" + c], "st" + c, 2500.0)
    return ops, sent


def depend(ops):
    n = len(ops)
    LAT = EST["lat"]
    lw, rs = {}, {}
    for i, o in enumerate(ops):
        d = {}
        for k in o["rd"]:
            if k in lw:
                d.setdefault(lw[k], set()).add(k)
        for k in o["wr"]:
            if k in lw:
                d.setdefault(lw[k], set()).add(k)
            for r in rs.get(k, ()):
                if r != i:
                    d.setdefault(r, set()).add(k)
        for k in o["rd"]:
            rs.setdefault(k, []).append(i)
        for k in o["wr"]:
            lw[k] = i
            rs[k] = []
        o["dep"] = d
        o["lat"] = {j: 0.0 if ops[j]["q"] == o["q"] and k <= o["free"] else LAT for j, k in d.items()}
    last = {o["ph"]: j for j, o in enumerate(ops) if o["name"] == "send" + PARTS[-1]}
    for o in ops:
        if o.get("after", -1) >= 0:
            j = last[o["after"]]
            o["dep"][j], o["lat"][j] = {"q"}, -ops[j]["fin"]
            o["free"].add("q")
    for o in ops:
        o["succ"], o["pr"] = [], 0.0
    for i, o in enumerate(ops):
        for j in o["dep"]:
            ops[j]["succ"].append(i)
    for i in range(n - 1, -1, -1):
        o = ops[i]
        o["pr"] = max(o["dur"], o["fin"]) + max([ops[s]["pr"] + ops[s]["lat"][i] for s in o["succ"]] + [0.0])


def place(ops):
    n = len(ops)
    pos = [{x.lstrip("+"): i - 1000 * (x[0] == "+") for i, x in enumerate(l.split())} for l in (CFG["first"], CFG["order"], CFG["last"])]
    key = []
    for i, o in enumerate(ops):
        if o["name"] in pos[2] and o["ph"] >= RO - 1:
            key.append(1000 * (RO - 1) + pos[2][o["name"]])
        elif o["name"] in pos[0] and o["ph"] <= 0:
            key.append(pos[0][o["name"]] - 500)
        elif 0 <= o["ph"] < RO:
            key.append(1000 * o["ph"] + pos[1][o["name"]])
        elif o.get("after", -1) >= 0:
            key.append(1000 * o["after"] + 999)
        else:
            key.append(i - 9e6 if o.get("first") else -2e6 - o["pr"] if o["ph"] < 0 else 9e6 - o["pr"])
    left = [len(o["dep"]) for o in ops]
    due, out, bank = [False] * n, [], {}
    for i0 in sorted(range(n), key=lambda i: key[i]):
        due[i0] = True
        todo = [] if left[i0] else [i0]
        while todo:
            i = todo.pop(0)
            o = ops[i]
            o["turn"] = []
            for b in o["banks"]:
                o["turn"] += [j for q, j in bank.setdefault(b, {}).items() if q != o["q"]]
                bank[b][o["q"]] = i
            out.append(i)
            for j in o["succ"]:
                left[j] -= 1
                if not left[j] and due[j]:
                    todo.append(j)
            todo.sort(key=lambda i: key[i])
    return out, 0.0


def order(ops):
    depend(ops)
    out, end = place(ops)
    for o in ops:
        for j in o["turn"]:
            o["dep"].setdefault(j, set())
    return out, end


def rank_program(g, core, T, topo):
    if T.rank_of(core) is None:
        return
    ops, sent = build(g, core, T, topo)
    seq, _ = order(ops)
    Q = {"v": g.vector, "s": g.scalar, "t": g.tensor, "g": g, "y": g.sync}
    cnt = {"v": 0, "s": 0, "t": 0, "g": 0}
    seen = {q: {} for q in Q}
    done = {}
    final = {}
    for i in seq:
        o = ops[i]
        q = o["q"]
        need = {}
        for j, toks in o["dep"].items():
            if ops[j]["q"] == q and toks and toks <= o["free"]:
                continue
            sg = done[j]
            for s, val in ([sg[k] for k in toks if k in sg] if isinstance(sg, dict) else [sg]):
                need[s] = max(need.get(s, 0), val)
        for s, val in need.items():
            if seen[q].get(s, 0) < val:
                Q[q].wait_ge(T.sem[s], val)
                seen[q][s] = val
        r = o["fn"]()
        if o["sig"] is None:
            for ins in (r if isinstance(r, list) else [r]):
                ins.then_inc(T.sem["c" + q], 1)
                cnt[q] += 1
            done[i] = ("c" + q, cnt[q])
        else:
            done[i] = o["sig"]
        for s, val in (done[i].values() if isinstance(done[i], dict) else [done[i]]):
            final[s] = val
    final["sent"] = sent[0]
    for s, val in final.items():
        g.wait_ge(T.sem[s], val)
